import numpy as np
import ml_dtypes


def mxq(x, axis, fmt="e4m3"):
    dtype, down = {"e4m3": (ml_dtypes.float8_e4m3fn, 7), "e5m2": (ml_dtypes.float8_e5m2, 14)}[fmt]
    v = np.moveaxis(np.asarray(x, np.float32).astype(ml_dtypes.bfloat16).astype(np.float64), axis, -1)
    blocks = v.reshape(v.shape[:-1] + (-1, 32))
    amax = np.abs(blocks).max(-1, keepdims=True)
    byte = np.maximum(np.where(amax > 0, np.frexp(amax)[1] - 1 + 127, 0) - down, 1)
    scale = np.exp2(byte - 127.0)
    codes = (blocks / scale).astype(np.float32).astype(dtype).astype(np.float64)
    return np.moveaxis((codes * scale).reshape(v.shape), -1, axis)


WIDE = False


def mx_kscale(k):
    if not WIDE:
        return np.ones(k)
    levels = np.array([30, -30])
    if k % 512:
        return np.exp2(np.random.permutation(np.resize(levels, k // 32))).repeat(32)
    a = np.empty((k // 512, 16))
    for p in range(k // 512):
        a[p, :8] = np.random.permutation(np.resize(levels, 8))
        for g in range(8):
            far = levels[np.abs(levels - a[p, g]) >= 10]
            a[p, g + 8] = far[np.random.randint(len(far))]
    return np.exp2(a.ravel()).repeat(32)


def f64(x):
    return np.asarray(x).astype(np.float64)


def striped(idx):
    return np.tile(idx.reshape(-1, 16).T, (8, 1)).astype(np.uint16)


def unstriped(offs):
    return offs[:16].T.reshape(-1).astype(np.int64)


def d_relu(v):
    return (v > 0).astype(np.float64)


K, T, E, C, H, N = 768, 1024, 2, 512, 1024, 512


def by_expert(wq, xq):
    return np.concatenate([wq[e].T @ xq[:, e * C:(e + 1) * C] for e in range(E)], axis=1)


def setup_inputs():
    n = np.random.standard_normal
    s = mx_kscale(N)[:, None]
    u = mx_kscale(H)
    return {
        "dyT": (n((N, T)) * s).astype(np.float32),
        "a": n((H, E * C)).astype(np.float32),
        "w2": (n((E, N, H)) / np.sqrt(N) / s[None] * u[None, None, :]).astype(np.float32),
        "w1": (n((E, H, K)) / np.sqrt(H) / u[None, :, None]).astype(np.float32),
        "gate": np.tile(np.random.uniform(0.2, 1.0, E * C), (N, 1)).astype(np.float32),
        "offs": striped(np.random.permutation(T)[:E * C]),
    }


def reference(dyT, a, w2, w1, gate, offs):
    idx = unstriped(offs)
    gq = mxq(f64(gate) * f64(dyT)[:, idx], 0, "e5m2")
    dh = by_expert(mxq(f64(w2), 1, "e4m3"), gq)
    da = dh * d_relu(f64(a))
    dx = by_expert(mxq(f64(w1), 1, "e4m3"), mxq(da, 0, "e5m2"))
    out = np.zeros((K, T))
    out[:, idx] = dx
    return out

@@ -1,0 +1,212 @@
+from contextlib import ExitStack
+
+import concourse.mybir as mybir
+
+E, C, T = 2, 512, 1024
+K, H, N = 768, 1024, 512
+FLOPS = 2 * E * C * (N * H + H * K)
+BYTES = 4 * (N * T + H * E * C + E * N * H + E * H * K + E * C + K * T) + 2 * 128 * (E * C // 16)
+
+F32 = mybir.dt.float32
+BF16 = mybir.dt.bfloat16
+U32 = mybir.dt.uint32
+U16 = mybir.dt.uint16
+U8 = mybir.dt.uint8
+E4 = mybir.dt.float8_e4m3fn_x4
+E5 = mybir.dt.float8_e5m2_x4
+MULT = mybir.AluOpType.mult
+ADD = mybir.AluOpType.add
+IS_GT = mybir.AluOpType.is_gt
+ACT = mybir.ActivationFunctionType
+
+P = 128
+HB = H // 512
+KT = K // P
+
+
+def tile_moe_bdx_mlp_relu_kernel(tc, dyT, a, w2, w1, gate, offs, out):
+    nc = tc.nc
+    with ExitStack() as ctx:
+        keep = ctx.enter_context(tc.tile_pool(name="keep", bufs=1))
+        ring = ctx.enter_context(tc.tile_pool(name="ring", bufs=2))
+        psum = ctx.enter_context(tc.psum_pool(name="psum", bufs=4))
+
+        def copy_on(eng, out_ap, in_ap):
+            if eng == "v":
+                nc.vector.tensor_copy(out=out_ap, in_=in_ap)
+            elif eng == "s":
+                nc.scalar.copy(out=out_ap, in_=in_ap)
+            else:
+                nc.gpsimd.tensor_scalar(out=out_ap, in0=in_ap, scalar1=1.0, scalar2=0.0, op0=MULT, op1=ADD)
+
+        def interleave(eng, dst, src):
+            if eng == "g":
+                copy_on(eng, dst.rearrange("p c t -> p c t"), src.rearrange("p t c -> p c t"))
+            else:
+                copy_on(eng, dst.rearrange("p (c i) t -> p c t i", i=4), src.rearrange("p t (c i) -> p c t i", i=4))
+
+        def quantize(src, width, fmt, name):
+            codes = keep.tile([P, width], U32, name=name + "_codes", align_bytes=64)
+            scales = keep.tile([P, width], U8, name=name + "_scales", align_bytes=64)
+            nc.vector.quantize_mx(out=codes[:].bitcast(fmt), scales=scales[:], in_=src)
+            return codes, scales
+
+        offs_t = keep.tile([P, E * C // 16], U16, name="offs_t")
+        nc.sync.dma_start(offs_t[:], offs)
+        dy_view = dyT.rearrange("(p t) j -> p t j", t=4)
+        dy = []
+        gates = []
+
+        def load_dy(t):
+            plane = keep.tile([P, T], F32, name="dy%d" % t)
+            nc.sync.dma_start(out=plane[:], in_=dy_view[:, t, :])
+            dy.append(plane)
+
+        def load_gate(e):
+            g = keep.tile([P, C], F32, name="gate%d" % e)
+            nc.sync.dma_start(out=g[:], in_=gate[0:P, e * C:(e + 1) * C])
+            gates.append(g)
+
+        def load_w2(e):
+            raw = ring.tile([P, 4, H], F32, name="w2raw", bufs=1)
+            nc.sync.dma_start(out=raw[:], in_=w2[e].rearrange("(p j) c -> p j c", j=4))
+            return raw
+
+        def load_a(e, b):
+            raw = ring.tile([P, 4, C], F32, name="araw")
+            nc.sync.dma_start(out=raw[:], in_=a[b * 512:(b + 1) * 512, e * C:(e + 1) * C].rearrange("(p t) j -> p t j", t=4))
+            return raw
+
+        def load_w1(e, b):
+            raw = ring.tile([P, 4, K], F32, name="w1raw")
+            nc.sync.dma_start(out=raw[:], in_=w1[e, b * 512:(b + 1) * 512, :].rearrange("(p j) c -> p j c", j=4))
+            return raw
+
+        def gather(e):
+            g4 = ring.tile([P, 4, C], F32, name="g4")
+            for t in range(4):
+                nc.vector.tensor_tensor(g4[:, t, :], dy[t][:].indirect(offs_t[:, e * (C // 16):(e + 1) * (C // 16)]), gates[e][:], MULT)
+            return g4
+
+        def make_g(e, g4, engs):
+            grouped = ring.tile([P, C, 4], BF16, name="ggrp", align_bytes=64)
+            w = C // len(engs)
+            for s, eng in enumerate(engs):
+                interleave(eng, grouped[:, s * w:(s + 1) * w, :], g4[:, :, s * w:(s + 1) * w])
+            return quantize(grouped[:].rearrange("p c t -> p (c t)"), C, E5, "g%d" % e)
+
+        def make_w2(e, b, raw, eng):
+            grouped = ring.tile([P, 2048], BF16, name="w2grp", align_bytes=64)
+            src = raw[:, :, b * 512:(b + 1) * 512]
+            if eng == "g":
+                copy_on(eng, grouped[:].rearrange("p (t m j) -> p t m j", t=4, j=4), src.rearrange("p j (m t) -> p t m j", t=4))
+            else:
+                copy_on(eng, grouped[:].rearrange("p (t m j) -> p m j t", t=4, j=4), src.rearrange("p j (m t) -> p m j t", t=4))
+            codes, scales = quantize(grouped[:], 512, E4, "w2_%d%d" % (e, b))
+            return codes[:], scales[:]
+
+        def make_w1(e, raws, engs):
+            grouped = ring.tile([P, HB * K, 4], BF16, name="w1grp", align_bytes=64, bufs=1)
+            for b in range(HB):
+                w = K // len(engs[b])
+                for s, eng in enumerate(engs[b]):
+                    interleave(eng, grouped[:, b * K + s * w:b * K + s * w + w, :], raws[b][:, :, s * w:s * w + w])
+            codes = keep.tile([P, HB * K], U32, name="w1_%d_codes" % e, align_bytes=64)
+            scales = keep.tile([P, HB * K], U8, name="w1_%d_scales" % e, align_bytes=64)
+            flat = grouped[:].rearrange("p c t -> p (c t)")
+            for c0, c1 in ((0, 1024), (1024, 1536)):
+                nc.vector.quantize_mx(out=codes[:, c0:c1].bitcast(E4), scales=scales[:, c0:c1], in_=flat[:, 4 * c0:4 * c1])
+            return codes, scales
+
+        def dh_tile(w2q, gq, t):
+            bank = psum.tile([P, C], F32, name="dh")
+            cols = slice(t * P, (t + 1) * P)
+            nc.tensor.matmul_mx(out=bank[:], lhsT=w2q[0][:, cols].bitcast(E4), lhsT_scale=w2q[1][:, cols],
+                                rhs=gq[0][:].bitcast(E5), rhs_scale=gq[1][:], start=True, stop=True)
+            return bank
+
+        def da_vector(e, b, w2q, gq, raw, engs):
+            plain = ring.tile([P, 4, C], BF16, name="daplain", align_bytes=64)
+            for t in range(4):
+                bank = dh_tile(w2q, gq, t)
+                nc.vector.scalar_tensor_tensor(out=plain[:, t, :], in0=raw[:, t, :], scalar=0.0, in1=bank[:], op0=IS_GT, op1=MULT)
+            grouped = ring.tile([P, C, 4], BF16, name="dagrp", align_bytes=64)
+            w = C // len(engs)
+            for s, eng in enumerate(engs):
+                interleave(eng, grouped[:, s * w:(s + 1) * w, :], plain[:, :, s * w:(s + 1) * w])
+            codes, scales = quantize(grouped[:].rearrange("p c t -> p (c t)"), C, E5, "da_%d%d" % (e, b))
+            return codes[:], scales[:]
+
+        def make_mask(raw):
+            sign = ring.tile([P, C, 4], BF16, name="sign", align_bytes=64, bufs=1)
+            nc.scalar.activation(out=sign[:].rearrange("p (c i) t -> p c t i", i=4), in_=raw[:].rearrange("p t (c i) -> p c t i", i=4), func=ACT.Sign)
+            mask = ring.tile([P, C, 4], BF16, name="mask", align_bytes=64, bufs=1)
+            nc.scalar.activation(out=mask[:], in_=sign[:], func=ACT.Relu)
+            return mask
+
+        def da_split(e, b, w2q, gq, mask):
+            plain = ring.tile([P, 4, C], BF16, name="daplain", align_bytes=64)
+            for t in range(4):
+                bank = dh_tile(w2q, gq, t)
+                nc.scalar.copy(out=plain[:, t, :], in_=bank[:])
+            grouped = ring.tile([P, C, 4], BF16, name="dagrp", align_bytes=64)
+            for s in range(4):
+                h = slice(s * 128, (s + 1) * 128)
+                nc.gpsimd.tensor_tensor(grouped[:, h, :], plain[:, :, h].rearrange("p t c -> p c t"), mask[:, h, :], MULT)
+            codes, scales = quantize(grouped[:].rearrange("p c t -> p (c t)"), C, E5, "da_%d%d" % (e, b))
+            return codes[:], scales[:]
+
+        windows = []
+        for kt in range(KT):
+            window = keep.tile([P, T], F32, name="window%d" % kt)
+            windows.append(window)
+
+        def dx_tile(kt, w1q, daq):
+            codes, scales = w1q
+            bank = psum.tile([P, C], F32, name="dx")
+            for b in range(HB):
+                cols = slice(b * K + kt * P, b * K + kt * P + P)
+                nc.tensor.matmul_mx(out=bank[:], lhsT=codes[:, cols].bitcast(E4), lhsT_scale=scales[:, cols],
+                                    rhs=daq[b][0].bitcast(E5), rhs_scale=daq[b][1], start=(b == 0), stop=(b == HB - 1))
+            staged = ring.tile([P, C], F32, name="staged", bufs=6)
+            nc.scalar.copy(out=staged[:], in_=bank[:])
+            return staged
+
+        def scatter(e, kt, staged):
+            nc.vector.tensor_copy(out=windows[kt][:].indirect(offs_t[:, e * (C // 16):(e + 1) * (C // 16)]), in_=staged[:])
+
+        load_dy(0)
+        load_gate(0)
+        for t in range(1, 4):
+            load_dy(t)
+        load_gate(1)
+        w2raw = load_w2(0)
+        a00 = load_a(0, 0)
+        a01 = load_a(0, 1)
+        w1raw0 = load_w1(0, 0)
+        w1raw1 = load_w1(0, 1)
+
+        gq = make_g(0, gather(0), "s")
+        w2q0, w2q1 = make_w2(0, 0, w2raw, "v"), make_w2(0, 1, w2raw, "s")
+        w1q = make_w1(0, (w1raw0, w1raw1), ("s", "s"))
+        daq = (da_vector(0, 0, w2q0, gq, a00, "g"), da_vector(0, 1, w2q1, gq, a01, "v"))
+
+        w2raw = load_w2(1)
+        a10 = load_a(1, 0)
+        a11 = load_a(1, 1)
+        w1raw0 = load_w1(1, 0)
+        w1raw1 = load_w1(1, 1)
+
+        gq1 = make_g(1, gather(1), "gs")
+        scatter(0, 0, dx_tile(0, w1q, daq))
+        w2q0, w2q1 = make_w2(1, 0, w2raw, "s"), make_w2(1, 1, w2raw, "s")
+        for kt in (1, 2, 3):
+            scatter(0, kt, dx_tile(kt, w1q, daq))
+        da0 = da_split(1, 0, w2q0, gq1, make_mask(a10))
+        scatter(0, 4, dx_tile(4, w1q, daq))
+        w1q1 = make_w1(1, (w1raw0, w1raw1), ("s", "s"))
+        da1 = da_vector(1, 1, w2q1, gq1, a11, "s")
+        scatter(0, 5, dx_tile(5, w1q, daq))
+        for kt in range(KT):
+            scatter(1, kt, dx_tile(kt, w1q1, (da0, da1)))
+            nc.sync.dma_start(out=out[kt * P:(kt + 1) * P, :], in_=windows[kt][:])

@@ -22,14 +22,25 @@ ACT = mybir.ActivationFunctionType
 P = 128
 HB = H // 512
 KT = K // P
+KC = 256
+KB = 1024
 
 
 def tile_moe_bdx_mlp_relu_kernel(tc, dyT, a, w2, w1, gate, offs, out):
     nc = tc.nc
     with ExitStack() as ctx:
         keep = ctx.enter_context(tc.tile_pool(name="keep", bufs=1))
-        ring = ctx.enter_context(tc.tile_pool(name="ring", bufs=2))
+        placed = ctx.enter_context(tc.tile_pool(name="placed", bufs=1))
         psum = ctx.enter_context(tc.psum_pool(name="psum", bufs=4))
+
+        def at(kb, width, dtype, name):
+            return placed.tile([P, width], dtype, name=name, offset=kb * KB, align_bytes=64)
+
+        def rows4(ap):
+            return ap.rearrange("p (t c) -> p t c", t=4)
+
+        def words4(ap):
+            return ap.rearrange("p (c t) -> p c t", t=4)
 
         def copy_on(eng, out_ap, in_ap):
             if eng == "v":
@@ -41,82 +52,66 @@ def tile_moe_bdx_mlp_relu_kernel(tc, dyT, a, w2, w1, gate, offs, out):
 
         def interleave(eng, dst, src):
             if eng == "g":
-                copy_on(eng, dst.rearrange("p c t -> p c t"), src.rearrange("p t c -> p c t"))
+                copy_on(eng, dst, src.rearrange("p t c -> p c t"))
             else:
                 copy_on(eng, dst.rearrange("p (c i) t -> p c t i", i=4), src.rearrange("p t (c i) -> p c t i", i=4))
 
-        def quantize(src, width, fmt, name):
-            codes = keep.tile([P, width], U32, name=name + "_codes", align_bytes=64)
-            scales = keep.tile([P, width], U8, name=name + "_scales", align_bytes=64)
-            nc.vector.quantize_mx(out=codes[:].bitcast(fmt), scales=scales[:], in_=src)
+        def group_rows(dst, src, shares):
+            c0 = 0
+            for eng, width in shares:
+                interleave(eng, words4(dst)[:, c0:c0 + width, :], src[:, :, c0:c0 + width])
+                c0 = c0 + width
+
+        def group_w2(dst, raw, eng):
+            if eng == "g":
+                copy_on(eng, dst.rearrange("p (t m j) -> p t m j", t=4, j=4), raw[:].rearrange("p j (m t) -> p t m j", t=4))
+            else:
+                copy_on(eng, dst.rearrange("p (t m j) -> p m j t", t=4, j=4), raw[:].rearrange("p j (m t) -> p m j t", t=4))
+
+        def group_w1(dst, raws, engs):
+            for b in range(HB):
+                interleave(engs[b], words4(dst)[:, b * KC:(b + 1) * KC, :], raws[b][:])
+
+        def quantize(grouped, fmt, name, codes=None):
+            if codes is None:
+                codes = keep.tile([P, 512], U32, name=name + "_codes", align_bytes=64)
+            scales = keep.tile([P, 512], U8, name=name + "_scales", align_bytes=64)
+            nc.vector.quantize_mx(out=codes[:].bitcast(fmt), scales=scales[:], in_=grouped)
             return codes, scales
 
         offs_t = keep.tile([P, E * C // 16], U16, name="offs_t")
         nc.sync.dma_start(offs_t[:], offs)
         dy_view = dyT.rearrange("(p t) j -> p t j", t=4)
-        dy = []
-        gates = []
 
         def load_dy(t):
-            plane = keep.tile([P, T], F32, name="dy%d" % t)
+            plane = at(4 * t, T, F32, "dy%d" % t)
             nc.sync.dma_start(out=plane[:], in_=dy_view[:, t, :])
-            dy.append(plane)
+            return plane
 
         def load_gate(e):
             g = keep.tile([P, C], F32, name="gate%d" % e)
             nc.sync.dma_start(out=g[:], in_=gate[0:P, e * C:(e + 1) * C])
-            gates.append(g)
+            return g
 
-        def load_w2(e):
-            raw = ring.tile([P, 4, H], F32, name="w2raw", bufs=1)
-            nc.sync.dma_start(out=raw[:], in_=w2[e].rearrange("(p j) c -> p j c", j=4))
+        def load_rows(name, rows):
+            raw = keep.tile([P, 4, rows.shape[1]], F32, name=name)
+            nc.sync.dma_start(out=raw[:], in_=rows.rearrange("(p j) c -> p j c", j=4))
             return raw
+
+        def load_w2(e, b):
+            return load_rows("w2raw%d%d" % (e, b), w2[e, :, b * 512:(b + 1) * 512])
 
         def load_a(e, b):
-            raw = ring.tile([P, 4, C], F32, name="araw")
-            nc.sync.dma_start(out=raw[:], in_=a[b * 512:(b + 1) * 512, e * C:(e + 1) * C].rearrange("(p t) j -> p t j", t=4))
-            return raw
+            return load_rows("araw%d%d" % (e, b), a[b * 512:(b + 1) * 512, e * C:(e + 1) * C])
 
-        def load_w1(e, b):
-            raw = ring.tile([P, 4, K], F32, name="w1raw")
-            nc.sync.dma_start(out=raw[:], in_=w1[e, b * 512:(b + 1) * 512, :].rearrange("(p j) c -> p j c", j=4))
-            return raw
+        def load_w1(e, c0, c1):
+            return [load_rows("w1raw%d%d_%d" % (e, b, c0), w1[e, b * 512:(b + 1) * 512, c0:c1]) for b in range(HB)]
 
-        def gather(e):
-            g4 = ring.tile([P, 4, C], F32, name="g4")
-            for t in range(4):
-                nc.vector.tensor_tensor(g4[:, t, :], dy[t][:].indirect(offs_t[:, e * (C // 16):(e + 1) * (C // 16)]), gates[e][:], MULT)
-            return g4
+        def slots_of(e):
+            return offs_t[:, e * (C // 16):(e + 1) * (C // 16)]
 
-        def make_g(e, g4, engs):
-            grouped = ring.tile([P, C, 4], BF16, name="ggrp", align_bytes=64)
-            w = C // len(engs)
-            for s, eng in enumerate(engs):
-                interleave(eng, grouped[:, s * w:(s + 1) * w, :], g4[:, :, s * w:(s + 1) * w])
-            return quantize(grouped[:].rearrange("p c t -> p (c t)"), C, E5, "g%d" % e)
-
-        def make_w2(e, b, raw, eng):
-            grouped = ring.tile([P, 2048], BF16, name="w2grp", align_bytes=64)
-            src = raw[:, :, b * 512:(b + 1) * 512]
-            if eng == "g":
-                copy_on(eng, grouped[:].rearrange("p (t m j) -> p t m j", t=4, j=4), src.rearrange("p j (m t) -> p t m j", t=4))
-            else:
-                copy_on(eng, grouped[:].rearrange("p (t m j) -> p m j t", t=4, j=4), src.rearrange("p j (m t) -> p m j t", t=4))
-            codes, scales = quantize(grouped[:], 512, E4, "w2_%d%d" % (e, b))
-            return codes[:], scales[:]
-
-        def make_w1(e, raws, engs):
-            grouped = ring.tile([P, HB * K, 4], BF16, name="w1grp", align_bytes=64, bufs=1)
-            for b in range(HB):
-                w = K // len(engs[b])
-                for s, eng in enumerate(engs[b]):
-                    interleave(eng, grouped[:, b * K + s * w:b * K + s * w + w, :], raws[b][:, :, s * w:s * w + w])
-            codes = keep.tile([P, HB * K], U32, name="w1_%d_codes" % e, align_bytes=64)
-            scales = keep.tile([P, HB * K], U8, name="w1_%d_scales" % e, align_bytes=64)
-            flat = grouped[:].rearrange("p c t -> p (c t)")
-            for c0, c1 in ((0, 1024), (1024, 1536)):
-                nc.vector.quantize_mx(out=codes[:, c0:c1].bitcast(E4), scales=scales[:, c0:c1], in_=flat[:, 4 * c0:4 * c1])
-            return codes, scales
+        def gather(e, t, dst, dy, gate_t):
+            nc.vector.tensor_tensor(dst[:, t * C:(t + 1) * C], dy[t][:].indirect(slots_of(e)), gate_t[:], MULT)
 
         def dh_tile(w2q, gq, t):
             bank = psum.tile([P, C], F32, name="dh")
@@ -125,88 +120,140 @@ def tile_moe_bdx_mlp_relu_kernel(tc, dyT, a, w2, w1, gate, offs, out):
                                 rhs=gq[0][:].bitcast(E5), rhs_scale=gq[1][:], start=True, stop=True)
             return bank
 
-        def da_vector(e, b, w2q, gq, raw, engs):
-            plain = ring.tile([P, 4, C], BF16, name="daplain", align_bytes=64)
-            for t in range(4):
-                bank = dh_tile(w2q, gq, t)
-                nc.vector.scalar_tensor_tensor(out=plain[:, t, :], in0=raw[:, t, :], scalar=0.0, in1=bank[:], op0=IS_GT, op1=MULT)
-            grouped = ring.tile([P, C, 4], BF16, name="dagrp", align_bytes=64)
-            w = C // len(engs)
-            for s, eng in enumerate(engs):
-                interleave(eng, grouped[:, s * w:(s + 1) * w, :], plain[:, :, s * w:(s + 1) * w])
-            codes, scales = quantize(grouped[:].rearrange("p c t -> p (c t)"), C, E5, "da_%d%d" % (e, b))
-            return codes[:], scales[:]
+        def da_plane(plain, t, w2q, gq, raw):
+            bank = dh_tile(w2q, gq, t)
+            nc.vector.scalar_tensor_tensor(out=plain[:, t * C:(t + 1) * C], in0=raw[:, t, :], scalar=0.0, in1=bank[:], op0=IS_GT, op1=MULT)
 
-        def make_mask(raw):
-            sign = ring.tile([P, C, 4], BF16, name="sign", align_bytes=64, bufs=1)
-            nc.scalar.activation(out=sign[:].rearrange("p (c i) t -> p c t i", i=4), in_=raw[:].rearrange("p t (c i) -> p c t i", i=4), func=ACT.Sign)
-            mask = ring.tile([P, C, 4], BF16, name="mask", align_bytes=64, bufs=1)
-            nc.scalar.activation(out=mask[:], in_=sign[:], func=ACT.Relu)
-            return mask
-
-        def da_split(e, b, w2q, gq, mask):
-            plain = ring.tile([P, 4, C], BF16, name="daplain", align_bytes=64)
-            for t in range(4):
-                bank = dh_tile(w2q, gq, t)
-                nc.scalar.copy(out=plain[:, t, :], in_=bank[:])
-            grouped = ring.tile([P, C, 4], BF16, name="dagrp", align_bytes=64)
-            for s in range(4):
-                h = slice(s * 128, (s + 1) * 128)
-                nc.gpsimd.tensor_tensor(grouped[:, h, :], plain[:, :, h].rearrange("p t c -> p c t"), mask[:, h, :], MULT)
-            codes, scales = quantize(grouped[:].rearrange("p c t -> p (c t)"), C, E5, "da_%d%d" % (e, b))
-            return codes[:], scales[:]
-
-        windows = []
-        for kt in range(KT):
-            window = keep.tile([P, T], F32, name="window%d" % kt)
-            windows.append(window)
-
-        def dx_tile(kt, w1q, daq):
+        def dx_tile(starts, w1q, daq):
             codes, scales = w1q
             bank = psum.tile([P, C], F32, name="dx")
             for b in range(HB):
-                cols = slice(b * K + kt * P, b * K + kt * P + P)
+                cols = slice(starts[b], starts[b] + P)
                 nc.tensor.matmul_mx(out=bank[:], lhsT=codes[:, cols].bitcast(E4), lhsT_scale=scales[:, cols],
-                                    rhs=daq[b][0].bitcast(E5), rhs_scale=daq[b][1], start=(b == 0), stop=(b == HB - 1))
-            staged = ring.tile([P, C], F32, name="staged", bufs=6)
+                                    rhs=daq[b][0][:].bitcast(E5), rhs_scale=daq[b][1][:], start=(b == 0), stop=(b == HB - 1))
+            staged = keep.tile([P, C], F32, name="staged", bufs=5)
             nc.scalar.copy(out=staged[:], in_=bank[:])
             return staged
 
-        def scatter(e, kt, staged):
-            nc.vector.tensor_copy(out=windows[kt][:].indirect(offs_t[:, e * (C // 16):(e + 1) * (C // 16)]), in_=staged[:])
+        def dx_pair(w1q, daq):
+            return [dx_tile((c0, KC + c0), w1q, daq) for c0 in (0, P)]
 
-        load_dy(0)
-        load_gate(0)
-        for t in range(1, 4):
-            load_dy(t)
-        load_gate(1)
-        w2raw = load_w2(0)
-        a00 = load_a(0, 0)
-        a01 = load_a(0, 1)
-        w1raw0 = load_w1(0, 0)
-        w1raw1 = load_w1(0, 1)
+        windows = []
 
-        gq = make_g(0, gather(0), "s")
-        w2q0, w2q1 = make_w2(0, 0, w2raw, "v"), make_w2(0, 1, w2raw, "s")
-        w1q = make_w1(0, (w1raw0, w1raw1), ("s", "s"))
-        daq = (da_vector(0, 0, w2q0, gq, a00, "g"), da_vector(0, 1, w2q1, gq, a01, "v"))
+        def scatter_first(kb, staged):
+            window = at(kb, T, F32, "window%d" % len(windows))
+            windows.append(window)
+            nc.vector.tensor_copy(out=window[:].indirect(slots_of(0)), in_=staged[:])
 
-        w2raw = load_w2(1)
-        a10 = load_a(1, 0)
-        a11 = load_a(1, 1)
-        w1raw0 = load_w1(1, 0)
-        w1raw1 = load_w1(1, 1)
-
-        gq1 = make_g(1, gather(1), "gs")
-        scatter(0, 0, dx_tile(0, w1q, daq))
-        w2q0, w2q1 = make_w2(1, 0, w2raw, "s"), make_w2(1, 1, w2raw, "s")
-        for kt in (1, 2, 3):
-            scatter(0, kt, dx_tile(kt, w1q, daq))
-        da0 = da_split(1, 0, w2q0, gq1, make_mask(a10))
-        scatter(0, 4, dx_tile(4, w1q, daq))
-        w1q1 = make_w1(1, (w1raw0, w1raw1), ("s", "s"))
-        da1 = da_vector(1, 1, w2q1, gq1, a11, "s")
-        scatter(0, 5, dx_tile(5, w1q, daq))
-        for kt in range(KT):
-            scatter(1, kt, dx_tile(kt, w1q1, (da0, da1)))
+        def scatter_last(kt, staged):
+            nc.vector.tensor_copy(out=windows[kt][:].indirect(slots_of(1)), in_=staged[:])
             nc.sync.dma_start(out=out[kt * P:(kt + 1) * P, :], in_=windows[kt][:])
+
+        dy = [load_dy(0)]
+        gate0 = load_gate(0)
+        dy.extend(load_dy(t) for t in range(1, 4))
+        gate1 = load_gate(1)
+        w2r00 = load_w2(0, 0)
+        a00 = load_a(0, 0)
+        w2r01 = load_w2(0, 1)
+        w1r00 = load_w1(0, 0, KC)
+        a01 = load_a(0, 1)
+        w2r10 = load_w2(1, 0)
+        w1r01 = load_w1(0, KC, 2 * KC)
+        a10 = load_a(1, 0)
+        w2r11 = load_w2(1, 1)
+        a11 = load_a(1, 1)
+        w1r02 = load_w1(0, 2 * KC, 3 * KC)
+        w1r1 = load_w1(1, 0, K)
+
+        g0 = at(40, 4 * C, F32, "g0")
+        for t in range(4):
+            gather(0, t, g0, dy, gate0)
+        g1 = at(28, 5 * C, F32, "g1")
+        w2g = g1[:, 3 * C:5 * C].bitcast(BF16)
+        for t in range(3):
+            gather(1, t, g1, dy, gate1)
+        ggrp0 = at(48, 4 * C, BF16, "ggrp0")
+        group_rows(ggrp0[:], rows4(g0[:]), [("s", 384), ("v", 128)])
+        group_w2(w2g, w2r00, "s")
+        gq0 = quantize(ggrp0[:], E5, "g0")
+        w2q0 = quantize(w2g, E4, "w2q00")
+        gather(1, 3, g1, dy, gate1)
+        plain = at(20, 8 * C, BF16, "plain00")
+        w2g = plain[:, 2 * C:6 * C]
+        ggrp1 = plain[:, 4 * C:8 * C]
+        group_w2(w2g, w2r01, "s")
+        for t in (0, 1):
+            da_plane(plain, t, w2q0, gq0, a00)
+        w2q1 = quantize(w2g, E4, "w2q01")
+        for t in (2, 3):
+            da_plane(plain, t, w2q0, gq0, a00)
+        group_rows(ggrp1, rows4(g1[:, 0:4 * C]), [("g", C)])
+        w1g = at(52, 4 * C, BF16, "w1g00")
+        group_w1(w1g[:], w1r00, "ss")
+        dag0 = at(48, 4 * C, BF16, "dag00")
+        group_rows(dag0[:], rows4(plain[:, 0:4 * C]), [("s", C)])
+        plain = at(60, 4 * C, BF16, "plain01")
+        for t in range(4):
+            da_plane(plain, t, w2q1, gq0, a01)
+        w1q = quantize(w1g[:], E4, "w1q00", codes=at(40, C, U32, "w1q00_codes"))
+        da0 = [quantize(dag0[:], E5, "da00")]
+        dag1 = at(56, 4 * C, BF16, "dag01")
+        group_rows(dag1[:], rows4(plain[:]), [("s", 320), ("v", 192)])
+        da0.append(quantize(dag1[:], E5, "da01"))
+        gq1 = quantize(ggrp1, E5, "g1", codes=at(56, C, U32, "g1_codes"))
+
+        staged = dx_pair(w1q, da0)
+        scatter_first(48, staged[0])
+        w2g = at(20, 4 * C, BF16, "w2g10")
+        group_w2(w2g[:], w2r10, "g")
+        w1g = at(24, 4 * C, BF16, "w1g01")
+        group_w1(w1g[:], w1r01, "gs")
+        w1q = quantize(w1g[:], E4, "w1q01")
+        w2q0 = quantize(w2g[:], E4, "w2q10")
+        scatter_first(22, staged[1])
+
+        w2g = at(2, 4 * C, BF16, "w2g11")
+        group_w2(w2g[:], w2r11, "s")
+        staged = dx_pair(w1q, da0)
+        plain0 = at(52, 4 * C, BF16, "plain10")
+        for t in range(4):
+            nc.scalar.copy(out=plain0[:, t * C:(t + 1) * C], in_=dh_tile(w2q0, gq1, t)[:])
+        w2q1 = quantize(w2g[:], E4, "w2q11")
+        scatter_first(0, staged[0])
+
+        w1g = at(4, 16 * C, BF16, "w1g02")
+        group_w1(w1g[:, 0:4 * C], w1r02, "gg")
+        sign = at(40, 4 * C, BF16, "sign")
+        nc.scalar.activation(out=words4(sign[:]).rearrange("p (c i) t -> p c t i", i=4),
+                             in_=a10[:].rearrange("p t (c i) -> p c t i", i=4), func=ACT.Sign)
+        mask = at(60, 4 * C, BF16, "mask")
+        nc.scalar.activation(out=mask[:], in_=sign[:], func=ACT.Relu)
+        w1q = quantize(w1g[:, 0:4 * C], E4, "w1q02")
+        scatter_first(4, staged[1])
+
+        dag0 = at(8, 8 * C, BF16, "dag10")
+        nc.gpsimd.tensor_tensor(words4(dag0[:, 0:4 * C]), rows4(plain0[:]).rearrange("p t c -> p c t"), words4(mask[:]), MULT)
+        staged = dx_pair(w1q, da0)
+        plain1 = at(16, 4 * C, BF16, "plain11")
+        for t in range(4):
+            da_plane(plain1, t, w2q1, gq1, a11)
+        w1g = at(28, 12 * C, BF16, "w1g1")
+        w1w = words4(w1g[:])
+        interleave("s", w1w[:, 0:512, :], w1r1[0][:, :, 0:512])
+        interleave("s", w1w[:, 512 + K:HB * K, :], w1r1[0][:, :, 512:K])
+        interleave("s", w1w[:, 512:512 + K, :], w1r1[1][:])
+        da1 = [quantize(dag0[:, 0:4 * C], E5, "da10")]
+        scatter_first(8, staged[0])
+
+        dag1 = at(12, 4 * C, BF16, "dag11")
+        group_rows(dag1[:], rows4(plain1[:]), [("g", C)])
+        da1.append(quantize(dag1[:], E5, "da11"))
+        codes = keep.tile([P, HB * K], U32, name="w1q1_codes", align_bytes=64)
+        scales = keep.tile([P, HB * K], U8, name="w1q1_scales", align_bytes=64)
+        for c0, c1 in ((0, 512), (512, HB * K)):
+            nc.vector.quantize_mx(out=codes[:, c0:c1].bitcast(E4), scales=scales[:, c0:c1], in_=w1g[:, 4 * c0:4 * c1])
+        scatter_first(28, staged[1])
+        for kt in range(KT):
+            k0 = kt * P
+            scatter_last(kt, dx_tile((k0 if k0 < 512 else k0 + K, 512 + k0), (codes, scales), da1))

@@ -1,6 +1,7 @@
 from contextlib import ExitStack
 
 import concourse.mybir as mybir
+from concourse.masks import make_identity
 
 E, C, T = 2, 512, 1024
 K, H, N = 768, 1024, 512
@@ -68,9 +69,9 @@ def tile_moe_bdx_mlp_relu_kernel(tc, dyT, a, w2, w1, gate, offs, out):
             else:
                 copy_on(eng, dst.rearrange("p (t m j) -> p m j t", t=4, j=4), raw[:].rearrange("p j (m t) -> p m j t", t=4))
 
-        def group_w1(dst, raws, engs):
+        def group_w1(dst, raws, engs, c0=0):
             for b in range(HB):
-                interleave(engs[b], words4(dst)[:, b * KC:(b + 1) * KC, :], raws[b][:])
+                interleave(engs[b], words4(dst)[:, b * KC:(b + 1) * KC, :], raws[b][:, :, c0:c0 + KC])
 
         def quantize(grouped, fmt, name, codes=None):
             if codes is None:
@@ -92,6 +93,22 @@ def tile_moe_bdx_mlp_relu_kernel(tc, dyT, a, w2, w1, gate, offs, out):
             g = keep.tile([P, C], F32, name="gate%d" % e)
             nc.sync.dma_start(out=g[:], in_=gate[0:P, e * C:(e + 1) * C])
             return g
+
+        def load_gate_row(e, queue):
+            row = keep.tile([P, 4], F32, name="gate_row%d" % e)
+            queue.dma_start(out=row[:], in_=gate[e, e * C:(e + 1) * C].rearrange("(n m) -> n m", m=4))
+            return row
+
+        def spread_gate(e, row, ident):
+            bank = psum.tile([P, C], F32, name="dh")
+            for m in range(4):
+                nc.tensor.transpose(bank[:, m * P:(m + 1) * P], row[:, m:m + 1].to_broadcast([P, P]), ident[:])
+            g = keep.tile([P, C], F32, name="gate%d" % e)
+            nc.scalar.copy(out=g[:].rearrange("p (n m) -> p n m", m=4), in_=bank[:].rearrange("p (m n) -> p n m", m=4))
+            return g
+
+        def load_w1b(e, b, c0, c1):
+            return load_rows("w1raw%d%d_%d" % (e, b, c0), w1[e, b * 512:(b + 1) * 512, c0:c1])
 
         def load_rows(name, rows):
             raw = keep.tile([P, 4, rows.shape[1]], F32, name=name)
@@ -124,19 +141,22 @@ def tile_moe_bdx_mlp_relu_kernel(tc, dyT, a, w2, w1, gate, offs, out):
             bank = dh_tile(w2q, gq, t)
             nc.vector.scalar_tensor_tensor(out=plain[:, t * C:(t + 1) * C], in0=raw[:, t, :], scalar=0.0, in1=bank[:], op0=IS_GT, op1=MULT)
 
-        def dx_tile(starts, w1q, daq):
+        def dx_tile(starts, w1q, daq, kb=None):
             codes, scales = w1q
             bank = psum.tile([P, C], F32, name="dx")
             for b in range(HB):
                 cols = slice(starts[b], starts[b] + P)
                 nc.tensor.matmul_mx(out=bank[:], lhsT=codes[:, cols].bitcast(E4), lhsT_scale=scales[:, cols],
                                     rhs=daq[b][0][:].bitcast(E5), rhs_scale=daq[b][1][:], start=(b == 0), stop=(b == HB - 1))
-            staged = keep.tile([P, C], F32, name="staged", bufs=5)
+            if kb is None:
+                staged = keep.tile([P, C], F32, name="staged", bufs=4)
+            else:
+                staged = at(kb, C, F32, "staged%d" % kb)
             nc.scalar.copy(out=staged[:], in_=bank[:])
             return staged
 
-        def dx_pair(w1q, daq):
-            return [dx_tile((c0, KC + c0), w1q, daq) for c0 in (0, P)]
+        def dx_pair(w1q, daq, kb=None):
+            return [dx_tile((0, KC), w1q, daq, kb), dx_tile((P, KC + P), w1q, daq)]
 
         windows = []
 
@@ -149,111 +169,108 @@ def tile_moe_bdx_mlp_relu_kernel(tc, dyT, a, w2, w1, gate, offs, out):
             nc.vector.tensor_copy(out=windows[kt][:].indirect(slots_of(1)), in_=staged[:])
             nc.sync.dma_start(out=out[kt * P:(kt + 1) * P, :], in_=windows[kt][:])
 
+        ident = keep.tile([P, P], F32, name="ident")
+        make_identity(nc, ident[:])
+        row = load_gate_row(0, nc.scalar)
         dy = [load_dy(0)]
-        gate0 = load_gate(0)
+        gate0 = spread_gate(0, row, ident)
         dy.extend(load_dy(t) for t in range(1, 4))
-        gate1 = load_gate(1)
+        gate1 = spread_gate(1, load_gate_row(1, nc.sync), ident)
         w2r00 = load_w2(0, 0)
-        a00 = load_a(0, 0)
         w2r01 = load_w2(0, 1)
+        a00 = load_a(0, 0)
         w1r00 = load_w1(0, 0, KC)
         a01 = load_a(0, 1)
         w2r10 = load_w2(1, 0)
-        w1r01 = load_w1(0, KC, 2 * KC)
+        w1r0 = load_w1(0, KC, K)
         a10 = load_a(1, 0)
         w2r11 = load_w2(1, 1)
         a11 = load_a(1, 1)
-        w1r02 = load_w1(0, 2 * KC, 3 * KC)
         w1r1 = load_w1(1, 0, K)
 
         g0 = at(40, 4 * C, F32, "g0")
         for t in range(4):
             gather(0, t, g0, dy, gate0)
-        g1 = at(28, 5 * C, F32, "g1")
-        w2g = g1[:, 3 * C:5 * C].bitcast(BF16)
-        for t in range(3):
+        g1 = at(28, 4 * C, F32, "g1")
+        w2g = at(36, 4 * C, BF16, "w2g00")[:]
+        for t in range(4):
             gather(1, t, g1, dy, gate1)
         ggrp0 = at(48, 4 * C, BF16, "ggrp0")
-        group_rows(ggrp0[:], rows4(g0[:]), [("s", 384), ("v", 128)])
+        group_rows(ggrp0[:], rows4(g0[:]), [("s", C)])
         group_w2(w2g, w2r00, "s")
         gq0 = quantize(ggrp0[:], E5, "g0")
         w2q0 = quantize(w2g, E4, "w2q00")
-        gather(1, 3, g1, dy, gate1)
-        plain = at(20, 8 * C, BF16, "plain00")
-        w2g = plain[:, 2 * C:6 * C]
-        ggrp1 = plain[:, 4 * C:8 * C]
-        group_w2(w2g, w2r01, "s")
-        for t in (0, 1):
+        w2g = at(24, 4 * C, BF16, "w2g01")
+        group_w2(w2g[:], w2r01, "s")
+        w2q1 = quantize(w2g[:], E4, "w2q01")
+        plain = at(20, 4 * C, BF16, "plain00")
+        for t in range(4):
             da_plane(plain, t, w2q0, gq0, a00)
-        w2q1 = quantize(w2g, E4, "w2q01")
-        for t in (2, 3):
-            da_plane(plain, t, w2q0, gq0, a00)
-        group_rows(ggrp1, rows4(g1[:, 0:4 * C]), [("g", C)])
+        ggrp1 = at(24, 4 * C, BF16, "ggrp1")
+        group_rows(ggrp1[:], rows4(g1[:, 0:4 * C]), [("g", C)])
         w1g = at(52, 4 * C, BF16, "w1g00")
-        group_w1(w1g[:], w1r00, "ss")
+        interleave("s", words4(w1g[:])[:, 0:KC, :], w1r00[0][:])
+        interleave("s", words4(w1g[:])[:, KC:2 * KC, :], w1r00[1][:])
         dag0 = at(48, 4 * C, BF16, "dag00")
-        group_rows(dag0[:], rows4(plain[:, 0:4 * C]), [("s", C)])
+        group_rows(dag0[:], rows4(plain[:]), [("s", C)])
         plain = at(60, 4 * C, BF16, "plain01")
         for t in range(4):
             da_plane(plain, t, w2q1, gq0, a01)
-        w1q = quantize(w1g[:], E4, "w1q00", codes=at(40, C, U32, "w1q00_codes"))
+        w1q = quantize(w1g[:], E4, "w1q00", codes=at(28, C, U32, "w1q00_codes"))
         da0 = [quantize(dag0[:], E5, "da00")]
         dag1 = at(56, 4 * C, BF16, "dag01")
         group_rows(dag1[:], rows4(plain[:]), [("s", 320), ("v", 192)])
         da0.append(quantize(dag1[:], E5, "da01"))
-        gq1 = quantize(ggrp1, E5, "g1", codes=at(56, C, U32, "g1_codes"))
+        gq1 = quantize(ggrp1[:], E5, "g1", codes=at(56, C, U32, "g1_codes"))
 
         staged = dx_pair(w1q, da0)
         scatter_first(48, staged[0])
-        w2g = at(20, 4 * C, BF16, "w2g10")
-        group_w2(w2g[:], w2r10, "g")
         w1g = at(24, 4 * C, BF16, "w1g01")
-        group_w1(w1g[:], w1r01, "gs")
+        interleave("g", words4(w1g[:])[:, 0:KC, :], w1r0[0][:, :, 0:KC])
+        interleave("g", words4(w1g[:])[:, KC:KC + P, :], w1r0[1][:, :, 0:P])
+        w2g = at(28, 4 * C, BF16, "w2g10")
+        group_w2(w2g[:], w2r10, "s")
+        interleave("s", words4(w1g[:])[:, KC + P:2 * KC, :], w1r0[1][:, :, P:KC])
         w1q = quantize(w1g[:], E4, "w1q01")
         w2q0 = quantize(w2g[:], E4, "w2q10")
-        scatter_first(22, staged[1])
+        scatter_first(26, staged[1])
 
-        w2g = at(2, 4 * C, BF16, "w2g11")
-        group_w2(w2g[:], w2r11, "s")
-        staged = dx_pair(w1q, da0)
+        staged = dx_pair(w1q, da0, 72)
+        scatter_first(64, staged[0])
         plain0 = at(52, 4 * C, BF16, "plain10")
         for t in range(4):
             nc.scalar.copy(out=plain0[:, t * C:(t + 1) * C], in_=dh_tile(w2q0, gq1, t)[:])
-        w2q1 = quantize(w2g[:], E4, "w2q11")
-        scatter_first(0, staged[0])
-
-        w1g = at(4, 16 * C, BF16, "w1g02")
-        group_w1(w1g[:, 0:4 * C], w1r02, "gg")
-        sign = at(40, 4 * C, BF16, "sign")
+        w1g = at(30, 4 * C, BF16, "w1g02")
+        group_w1(w1g[:], w1r0, "gg", KC)
+        w2g = at(0, 16 * C, BF16, "w2g11")
+        group_w2(w2g[:, 0:4 * C], w2r11, "s")
+        sign = at(20, 4 * C, BF16, "sign")
         nc.scalar.activation(out=words4(sign[:]).rearrange("p (c i) t -> p c t i", i=4),
                              in_=a10[:].rearrange("p t (c i) -> p c t i", i=4), func=ACT.Sign)
         mask = at(60, 4 * C, BF16, "mask")
         nc.scalar.activation(out=mask[:], in_=sign[:], func=ACT.Relu)
-        w1q = quantize(w1g[:, 0:4 * C], E4, "w1q02")
-        scatter_first(4, staged[1])
+        w1q = quantize(w1g[:], E4, "w1q02", codes=at(71, C, U32, "w1q02_codes"))
+        w2q1 = quantize(w2g[:, 0:4 * C], E4, "w2q11", codes=at(73, C, U32, "w2q11_codes"))
+        scatter_first(0, staged[1])
 
-        dag0 = at(8, 8 * C, BF16, "dag10")
-        nc.gpsimd.tensor_tensor(words4(dag0[:, 0:4 * C]), rows4(plain0[:]).rearrange("p t c -> p c t"), words4(mask[:]), MULT)
-        staged = dx_pair(w1q, da0)
-        plain1 = at(16, 4 * C, BF16, "plain11")
+        dag0 = at(12, 4 * C, BF16, "dag10")
+        nc.gpsimd.tensor_tensor(words4(dag0[:]), rows4(plain0[:]).rearrange("p t c -> p c t"), words4(mask[:]), MULT)
+        staged = dx_pair(w1q, da0, 76)
+        plain1 = at(4, 4 * C, BF16, "plain11")
         for t in range(4):
             da_plane(plain1, t, w2q1, gq1, a11)
-        w1g = at(28, 12 * C, BF16, "w1g1")
-        w1w = words4(w1g[:])
-        interleave("s", w1w[:, 0:512, :], w1r1[0][:, :, 0:512])
-        interleave("s", w1w[:, 512 + K:HB * K, :], w1r1[0][:, :, 512:K])
-        interleave("s", w1w[:, 512:512 + K, :], w1r1[1][:])
-        da1 = [quantize(dag0[:, 0:4 * C], E5, "da10")]
         scatter_first(8, staged[0])
-
-        dag1 = at(12, 4 * C, BF16, "dag11")
-        group_rows(dag1[:], rows4(plain1[:]), [("g", C)])
-        da1.append(quantize(dag1[:], E5, "da11"))
-        codes = keep.tile([P, HB * K], U32, name="w1q1_codes", align_bytes=64)
-        scales = keep.tile([P, HB * K], U8, name="w1q1_scales", align_bytes=64)
-        for c0, c1 in ((0, 512), (512, HB * K)):
-            nc.vector.quantize_mx(out=codes[:, c0:c1].bitcast(E4), scales=scales[:, c0:c1], in_=w1g[:, 4 * c0:4 * c1])
-        scatter_first(28, staged[1])
+        w1g = [at(kb, 4 * C, BF16, "w1g1%d" % c) for c, kb in enumerate((40, 44))]
+        for c in (0, 1):
+            group_w1(w1g[c][:], w1r1, "ss", c * KC)
+        dag1 = at(16, 4 * C, BF16, "dag11")
+        group_rows(dag1[:], rows4(plain1[:]), [("s", C)])
+        w1q1 = [quantize(w1g[c][:], E4, "w1q1%d" % c, codes=at(75 + 2 * c, C, U32, "w1q1%d_codes" % c)) for c in (0, 1)]
+        da1 = [quantize(dag0[:], E5, "da10"), quantize(dag1[:], E5, "da11")]
+        scatter_first(14, staged[1])
+        w1g = at(36, 4 * C, BF16, "w1g12")
+        group_w1(w1g[:], w1r1, "ss", 2 * KC)
+        w1q1.append(quantize(w1g[:], E4, "w1q12"))
         for kt in range(KT):
-            k0 = kt * P
-            scatter_last(kt, dx_tile((k0 if k0 < 512 else k0 + K, 512 + k0), (codes, scales), da1))
+            c0 = (kt % 2) * P
+            scatter_last(kt, dx_tile((c0, KC + c0), w1q1[kt // 2], da1))

@@ -35,7 +35,7 @@ def tile_moe_bdx_mlp_relu_kernel(tc, dyT, a, w2, w1, gate, offs, out):
         psum = ctx.enter_context(tc.psum_pool(name="psum", bufs=4))
 
         def at(kb, width, dtype, name):
-            return placed.tile([P, width], dtype, name=name, offset=kb * KB, align_bytes=64)
+            return placed.tile([P, width], dtype, name=name, offset=int(kb * KB), align_bytes=64)
 
         def rows4(ap):
             return ap.rearrange("p (t c) -> p t c", t=4)
@@ -73,10 +73,13 @@ def tile_moe_bdx_mlp_relu_kernel(tc, dyT, a, w2, w1, gate, offs, out):
             for b in range(HB):
                 interleave(engs[b], words4(dst)[:, b * KC:(b + 1) * KC, :], raws[b][:, :, c0:c0 + KC])
 
-        def quantize(grouped, fmt, name, codes=None):
+        def quantize(grouped, fmt, name, codes=None, scales_kb=None):
             if codes is None:
                 codes = keep.tile([P, 512], U32, name=name + "_codes", align_bytes=64)
-            scales = keep.tile([P, 512], U8, name=name + "_scales", align_bytes=64)
+            if scales_kb is None:
+                scales = keep.tile([P, 512], U8, name=name + "_scales", align_bytes=64)
+            else:
+                scales = at(scales_kb, 512, U8, name + "_scales")
             nc.vector.quantize_mx(out=codes[:].bitcast(fmt), scales=scales[:], in_=grouped)
             return codes, scales
 
@@ -107,19 +110,31 @@ def tile_moe_bdx_mlp_relu_kernel(tc, dyT, a, w2, w1, gate, offs, out):
             nc.scalar.copy(out=g[:].rearrange("p (n m) -> p n m", m=4), in_=bank[:].rearrange("p (m n) -> p n m", m=4))
             return g
 
-        def load_w1b(e, b, c0, c1):
-            return load_rows("w1raw%d%d_%d" % (e, b, c0), w1[e, b * 512:(b + 1) * 512, c0:c1])
+        def load_w1b(e, b, c0, c1, kb=None):
+            return load_rows("w1raw%d%d_%d" % (e, b, c0), w1[e, b * 512:(b + 1) * 512, c0:c1], kb)
 
-        def load_rows(name, rows):
-            raw = keep.tile([P, 4, rows.shape[1]], F32, name=name)
+        def load_a_pair(e, b, t0, kb=None):
+            if kb is None:
+                raw = keep.tile([P, 2, C], F32, name="apair%d%d%d" % (e, b, t0))
+            else:
+                raw = placed.tile([P, 2, C], F32, name="apair%d%d%d" % (e, b, t0), offset=int(kb * KB), align_bytes=64)
+            rows = a[b * 512:(b + 1) * 512, e * C:(e + 1) * C].rearrange("(p j) c -> p j c", j=4)
+            nc.sync.dma_start(out=raw[:], in_=rows[:, t0:t0 + 2, :])
+            return raw
+
+        def load_rows(name, rows, kb=None):
+            if kb is None:
+                raw = keep.tile([P, 4, rows.shape[1]], F32, name=name)
+            else:
+                raw = placed.tile([P, 4, rows.shape[1]], F32, name=name, offset=int(kb * KB), align_bytes=64)
             nc.sync.dma_start(out=raw[:], in_=rows.rearrange("(p j) c -> p j c", j=4))
             return raw
 
-        def load_w2(e, b):
-            return load_rows("w2raw%d%d" % (e, b), w2[e, :, b * 512:(b + 1) * 512])
+        def load_w2(e, b, kb=None):
+            return load_rows("w2raw%d%d" % (e, b), w2[e, :, b * 512:(b + 1) * 512], kb)
 
-        def load_a(e, b):
-            return load_rows("araw%d%d" % (e, b), a[b * 512:(b + 1) * 512, e * C:(e + 1) * C])
+        def load_a(e, b, kb=None):
+            return load_rows("araw%d%d" % (e, b), a[b * 512:(b + 1) * 512, e * C:(e + 1) * C], kb)
 
         def load_w1(e, c0, c1):
             return [load_rows("w1raw%d%d_%d" % (e, b, c0), w1[e, b * 512:(b + 1) * 512, c0:c1]) for b in range(HB)]
@@ -130,8 +145,8 @@ def tile_moe_bdx_mlp_relu_kernel(tc, dyT, a, w2, w1, gate, offs, out):
         def gather(e, t, dst, dy, gate_t):
             nc.vector.tensor_tensor(dst[:, t * C:(t + 1) * C], dy[t][:].indirect(slots_of(e)), gate_t[:], MULT)
 
-        def dh_tile(w2q, gq, t):
-            bank = psum.tile([P, C], F32, name="dh")
+        def dh_tile(w2q, gq, t, linked=False):
+            bank = psum.tile([P, C], F32, name="link", bufs=1) if linked else psum.tile([P, C], F32, name="dh")
             cols = slice(t * P, (t + 1) * P)
             nc.tensor.matmul_mx(out=bank[:], lhsT=w2q[0][:, cols].bitcast(E4), lhsT_scale=w2q[1][:, cols],
                                 rhs=gq[0][:].bitcast(E5), rhs_scale=gq[1][:], start=True, stop=True)
@@ -139,11 +154,11 @@ def tile_moe_bdx_mlp_relu_kernel(tc, dyT, a, w2, w1, gate, offs, out):
 
         def da_plane(plain, t, w2q, gq, raw):
             bank = dh_tile(w2q, gq, t)
-            nc.vector.scalar_tensor_tensor(out=plain[:, t * C:(t + 1) * C], in0=raw[:, t, :], scalar=0.0, in1=bank[:], op0=IS_GT, op1=MULT)
+            nc.vector.scalar_tensor_tensor(out=plain[:, t * C:(t + 1) * C], in0=raw, scalar=0.0, in1=bank[:], op0=IS_GT, op1=MULT)
 
-        def dx_tile(starts, w1q, daq, kb=None):
+        def dx_tile(starts, w1q, daq, kb=None, linked=False):
             codes, scales = w1q
-            bank = psum.tile([P, C], F32, name="dx")
+            bank = psum.tile([P, C], F32, name="link", bufs=1) if linked else psum.tile([P, C], F32, name="dx", bufs=3)
             for b in range(HB):
                 cols = slice(starts[b], starts[b] + P)
                 nc.tensor.matmul_mx(out=bank[:], lhsT=codes[:, cols].bitcast(E4), lhsT_scale=scales[:, cols],
@@ -155,8 +170,8 @@ def tile_moe_bdx_mlp_relu_kernel(tc, dyT, a, w2, w1, gate, offs, out):
             nc.scalar.copy(out=staged[:], in_=bank[:])
             return staged
 
-        def dx_pair(w1q, daq, kb=None):
-            return [dx_tile((0, KC), w1q, daq, kb), dx_tile((P, KC + P), w1q, daq)]
+        def dx_pair(w1q, daq, linked=False):
+            return [dx_tile((0, KC), w1q, daq, None, linked), dx_tile((P, KC + P), w1q, daq)]
 
         windows = []
 
@@ -169,108 +184,121 @@ def tile_moe_bdx_mlp_relu_kernel(tc, dyT, a, w2, w1, gate, offs, out):
             nc.vector.tensor_copy(out=windows[kt][:].indirect(slots_of(1)), in_=staged[:])
             nc.sync.dma_start(out=out[kt * P:(kt + 1) * P, :], in_=windows[kt][:])
 
-        ident = keep.tile([P, P], F32, name="ident")
+        ident = at(26, P, F32, "ident")
         make_identity(nc, ident[:])
         row = load_gate_row(0, nc.scalar)
-        dy = [load_dy(0)]
+        dy = {1: load_dy(1)}
         gate0 = spread_gate(0, row, ident)
-        dy.extend(load_dy(t) for t in range(1, 4))
-        gate1 = spread_gate(1, load_gate_row(1, nc.sync), ident)
+        row = load_gate_row(1, nc.sync)
+        dy[2] = load_dy(2)
+        gate1 = spread_gate(1, row, ident)
         w2r00 = load_w2(0, 0)
+        dy[0] = load_dy(0)
+        dy[3] = load_dy(3)
         w2r01 = load_w2(0, 1)
         a00 = load_a(0, 0)
         w1r00 = load_w1(0, 0, KC)
         a01 = load_a(0, 1)
-        w2r10 = load_w2(1, 0)
-        w1r0 = load_w1(0, KC, K)
         a10 = load_a(1, 0)
+        w1r01 = [load_w1b(0, 0, KC, 2 * KC)]
+        w2r10 = load_w2(1, 0, 72)
+        w1r01.append(load_w1b(0, 1, KC, 2 * KC))
         w2r11 = load_w2(1, 1)
-        a11 = load_a(1, 1)
-        w1r1 = load_w1(1, 0, K)
+        w1r02 = [load_w1b(0, 0, 2 * KC, K), load_w1b(0, 1, 2 * KC, K, 82)]
+        a11 = [load_a_pair(1, 1, 0, 68), load_a_pair(1, 1, 2)]
+        w1r10 = [load_w1b(1, 0, 0, KC), load_w1b(1, 1, 0, KC, 102)]
+        w1r1 = [load_w1b(1, 0, KC, K, 94), load_w1b(1, 1, KC, K, 86)]
 
         g0 = at(40, 4 * C, F32, "g0")
-        for t in range(4):
-            gather(0, t, g0, dy, gate0)
-        g1 = at(28, 4 * C, F32, "g1")
-        w2g = at(36, 4 * C, BF16, "w2g00")[:]
-        for t in range(4):
-            gather(1, t, g1, dy, gate1)
-        ggrp0 = at(48, 4 * C, BF16, "ggrp0")
-        group_rows(ggrp0[:], rows4(g0[:]), [("s", C)])
+        arena = at(26, 6 * C, F32, "g1")
+        g1 = arena[:, C:5 * C]
+        w2g = arena[:, 0:2 * C].bitcast(BF16)
+        ggrp0 = arena[:, 4 * C:6 * C].bitcast(BF16)
+        for e, dst, gate_t in ((0, g0, gate0), (1, g1, gate1)):
+            for t in (1, 2):
+                gather(e, t, dst, dy, gate_t)
         group_w2(w2g, w2r00, "s")
-        gq0 = quantize(ggrp0[:], E5, "g0")
+        for t in (0, 3):
+            gather(0, t, g0, dy, gate0)
         w2q0 = quantize(w2g, E4, "w2q00")
-        w2g = at(24, 4 * C, BF16, "w2g01")
+        group_rows(ggrp0, rows4(g0[:]), [("s", 384), ("v", 128)])
+        gather(1, 0, g1, dy, gate1)
+        gq0 = quantize(ggrp0, E5, "g0")
+        gather(1, 3, g1, dy, gate1)
+        w2g = at(22, 4 * C, BF16, "w2g01")
         group_w2(w2g[:], w2r01, "s")
+        plain = at(16, 4 * C, BF16, "plain00")
         w2q1 = quantize(w2g[:], E4, "w2q01")
-        plain = at(20, 4 * C, BF16, "plain00")
         for t in range(4):
-            da_plane(plain, t, w2q0, gq0, a00)
-        ggrp1 = at(24, 4 * C, BF16, "ggrp1")
-        group_rows(ggrp1[:], rows4(g1[:, 0:4 * C]), [("g", C)])
+            da_plane(plain, t, w2q0, gq0, a00[:, t, :])
+        ggrp1 = at(22, 4 * C, BF16, "ggrp1")
+        group_rows(ggrp1[:], rows4(g1), [("g", C)])
         w1g = at(52, 4 * C, BF16, "w1g00")
-        interleave("s", words4(w1g[:])[:, 0:KC, :], w1r00[0][:])
-        interleave("s", words4(w1g[:])[:, KC:2 * KC, :], w1r00[1][:])
+        group_w1(w1g[:], w1r00, "ss")
         dag0 = at(48, 4 * C, BF16, "dag00")
         group_rows(dag0[:], rows4(plain[:]), [("s", C)])
         plain = at(60, 4 * C, BF16, "plain01")
         for t in range(4):
-            da_plane(plain, t, w2q1, gq0, a01)
-        w1q = quantize(w1g[:], E4, "w1q00", codes=at(28, C, U32, "w1q00_codes"))
+            da_plane(plain, t, w2q1, gq0, a01[:, t, :])
         da0 = [quantize(dag0[:], E5, "da00")]
-        dag1 = at(56, 4 * C, BF16, "dag01")
+        dag1 = at(14, 4 * C, BF16, "dag01")
         group_rows(dag1[:], rows4(plain[:]), [("s", 320), ("v", 192)])
+        w1q = quantize(w1g[:], E4, "w1q00", codes=at(31, C, U32, "w1q00_codes"), scales_kb=19)
         da0.append(quantize(dag1[:], E5, "da01"))
-        gq1 = quantize(ggrp1[:], E5, "g1", codes=at(56, C, U32, "g1_codes"))
+        gq1 = quantize(ggrp1[:], E5, "g1", scales_kb=63)
+
+        def sign_half(h, kb):
+            half = at(kb, 2 * C, BF16, "sign%d" % h)
+            nc.scalar.activation(out=words4(half[:]).rearrange("p (c i) t -> p c t i", i=4),
+                                 in_=a10[:, :, h * KC:(h + 1) * KC].rearrange("p t (c i) -> p c t i", i=4), func=ACT.Sign)
+            return half
 
         staged = dx_pair(w1q, da0)
         scatter_first(48, staged[0])
-        w1g = at(24, 4 * C, BF16, "w1g01")
-        interleave("g", words4(w1g[:])[:, 0:KC, :], w1r0[0][:, :, 0:KC])
-        interleave("g", words4(w1g[:])[:, KC:KC + P, :], w1r0[1][:, :, 0:P])
+        w1g = at(22, 4 * C, BF16, "w1g01")
+        group_w1(w1g[:], w1r01, "gg")
         w2g = at(28, 4 * C, BF16, "w2g10")
         group_w2(w2g[:], w2r10, "s")
-        interleave("s", words4(w1g[:])[:, KC + P:2 * KC, :], w1r0[1][:, :, P:KC])
-        w1q = quantize(w1g[:], E4, "w1q01")
-        w2q0 = quantize(w2g[:], E4, "w2q10")
-        scatter_first(26, staged[1])
+        w1q = quantize(w1g[:], E4, "w1q01", codes=at(72, C, U32, "w1q01_codes"), scales_kb=14)
+        w2q0 = quantize(w2g[:], E4, "w2q10", codes=at(80, C, U32, "w2q10_codes"))
+        scatter_first(22, staged[1])
 
-        staged = dx_pair(w1q, da0, 72)
+        w2g = at(32, 4 * C, BF16, "w2g11")
+        group_w2(w2g[:], w2r11, "s")
+        signs = [sign_half(0, 60), sign_half(1, 19)]
+        staged = dx_pair(w1q, da0, True)
         scatter_first(64, staged[0])
         plain0 = at(52, 4 * C, BF16, "plain10")
         for t in range(4):
-            nc.scalar.copy(out=plain0[:, t * C:(t + 1) * C], in_=dh_tile(w2q0, gq1, t)[:])
-        w1g = at(30, 4 * C, BF16, "w1g02")
-        group_w1(w1g[:], w1r0, "gg", KC)
-        w2g = at(0, 16 * C, BF16, "w2g11")
-        group_w2(w2g[:, 0:4 * C], w2r11, "s")
-        sign = at(20, 4 * C, BF16, "sign")
-        nc.scalar.activation(out=words4(sign[:]).rearrange("p (c i) t -> p c t i", i=4),
-                             in_=a10[:].rearrange("p t (c i) -> p c t i", i=4), func=ACT.Sign)
-        mask = at(60, 4 * C, BF16, "mask")
-        nc.scalar.activation(out=mask[:], in_=sign[:], func=ACT.Relu)
-        w1q = quantize(w1g[:], E4, "w1q02", codes=at(71, C, U32, "w1q02_codes"))
-        w2q1 = quantize(w2g[:, 0:4 * C], E4, "w2q11", codes=at(73, C, U32, "w2q11_codes"))
-        scatter_first(0, staged[1])
+            nc.scalar.copy(out=plain0[:, t * C:(t + 1) * C], in_=dh_tile(w2q0, gq1, t, t == 3)[:])
+        mask = at(14, 4 * C, BF16, "mask")
+        for h in range(2):
+            nc.scalar.activation(out=mask[:, 2 * h * C:2 * (h + 1) * C], in_=signs[h][:], func=ACT.Relu)
+        w1g = at(28, 4 * C, BF16, "w1g02")
+        group_w1(w1g[:], w1r02, "gg")
+        w1q = quantize(w1g[:], E4, "w1q02", scales_kb=81)
+        w2q1 = quantize(w2g[:], E4, "w2q11", scales_kb=81.75)
+        scatter_first(28, staged[1])
 
-        dag0 = at(12, 4 * C, BF16, "dag10")
+        dag0 = at(32, 4 * C, BF16, "dag10")
         nc.gpsimd.tensor_tensor(words4(dag0[:]), rows4(plain0[:]).rearrange("p t c -> p c t"), words4(mask[:]), MULT)
-        staged = dx_pair(w1q, da0, 76)
         plain1 = at(4, 4 * C, BF16, "plain11")
         for t in range(4):
-            da_plane(plain1, t, w2q1, gq1, a11)
-        scatter_first(8, staged[0])
-        w1g = [at(kb, 4 * C, BF16, "w1g1%d" % c) for c, kb in enumerate((40, 44))]
-        for c in (0, 1):
-            group_w1(w1g[c][:], w1r1, "ss", c * KC)
-        dag1 = at(16, 4 * C, BF16, "dag11")
+            da_plane(plain1, t, w2q1, gq1, a11[t // 2][:, t % 2, :])
+        staged = dx_pair(w1q, da0)
+        scatter_first(68, staged[0])
+        w1g = at(73, 4 * C, BF16, "w1g10")
+        group_w1(w1g[:], w1r10, "ss")
+        dag1 = at(102, 4 * C, BF16, "dag11")
         group_rows(dag1[:], rows4(plain1[:]), [("s", C)])
-        w1q1 = [quantize(w1g[c][:], E4, "w1q1%d" % c, codes=at(75 + 2 * c, C, U32, "w1q1%d_codes" % c)) for c in (0, 1)]
-        da1 = [quantize(dag0[:], E5, "da10"), quantize(dag1[:], E5, "da11")]
-        scatter_first(14, staged[1])
-        w1g = at(36, 4 * C, BF16, "w1g12")
-        group_w1(w1g[:], w1r1, "ss", 2 * KC)
-        w1q1.append(quantize(w1g[:], E4, "w1q12"))
+        da11 = quantize(dag1[:], E5, "da11", scales_kb=52)
+        da1 = [quantize(dag0[:], E5, "da10", scales_kb=4), da11]
+        w1q1 = [quantize(w1g[:], E4, "w1q10", codes=at(53, C, U32, "w1q10_codes"), scales_kb=5)]
+        scatter_first(33, staged[1])
+        for c, kb in ((1, 6), (2, 73)):
+            w1g = at(kb, 4 * C, BF16, "w1g1%d" % c)
+            group_w1(w1g[:], w1r1, "ss", (c - 1) * KC)
+            w1q1.append(quantize(w1g[:], E4, "w1q1%d" % c, scales_kb=31.5 + 0.5 * c))
         for kt in range(KT):
             c0 = (kt % 2) * P
-            scatter_last(kt, dx_tile((c0, KC + c0), w1q1[kt // 2], da1))
+            scatter_last(kt, dx_tile((c0, KC + c0), w1q1[kt // 2], da1, 86 + 2 * kt))

@@ -65,21 +65,22 @@ def tile_moe_bdx_mlp_relu_kernel(tc, dyT, a, w2, w1, gate, offs, out):
 
         def group_w2(dst, raw, eng):
             if eng == "g":
-                copy_on(eng, dst.rearrange("p (t m j) -> p t m j", t=4, j=4), raw[:].rearrange("p j (m t) -> p t m j", t=4))
+                copy_on(eng, dst.rearrange("p (t m j) -> p t m j", t=4, j=4), raw.rearrange("p j (m t) -> p t m j", t=4))
             else:
-                copy_on(eng, dst.rearrange("p (t m j) -> p m j t", t=4, j=4), raw[:].rearrange("p j (m t) -> p m j t", t=4))
+                copy_on(eng, dst.rearrange("p (t m j) -> p m j t", t=4, j=4), raw.rearrange("p j (m t) -> p m j t", t=4))
 
         def group_w1(dst, raws, engs, c0=0):
             for b in range(HB):
                 interleave(engs[b], words4(dst)[:, b * KC:(b + 1) * KC, :], raws[b][:, :, c0:c0 + KC])
 
         def quantize(grouped, fmt, name, codes=None, scales_kb=None):
+            width = grouped.shape[1] // 4
             if codes is None:
-                codes = keep.tile([P, 512], U32, name=name + "_codes", align_bytes=64)
+                codes = keep.tile([P, width], U32, name=name + "_codes", align_bytes=64)
             if scales_kb is None:
-                scales = keep.tile([P, 512], U8, name=name + "_scales", align_bytes=64)
+                scales = keep.tile([P, width], U8, name=name + "_scales", align_bytes=64)
             else:
-                scales = at(scales_kb, 512, U8, name + "_scales")
+                scales = at(scales_kb, width, U8, name + "_scales")
             nc.vector.quantize_mx(out=codes[:].bitcast(fmt), scales=scales[:], in_=grouped)
             return codes, scales
 
@@ -109,6 +110,9 @@ def tile_moe_bdx_mlp_relu_kernel(tc, dyT, a, w2, w1, gate, offs, out):
             g = keep.tile([P, C], F32, name="gate%d" % e)
             nc.scalar.copy(out=g[:].rearrange("p (n m) -> p n m", m=4), in_=bank[:].rearrange("p (m n) -> p n m", m=4))
             return g
+
+        def load_w2_whole(e):
+            return load_rows("w2raw%d" % e, w2[e])
 
         def load_w1b(e, b, c0, c1, kb=None):
             return load_rows("w1raw%d%d_%d" % (e, b, c0), w1[e, b * 512:(b + 1) * 512, c0:c1], kb)
@@ -156,13 +160,13 @@ def tile_moe_bdx_mlp_relu_kernel(tc, dyT, a, w2, w1, gate, offs, out):
             bank = dh_tile(w2q, gq, t)
             nc.vector.scalar_tensor_tensor(out=plain[:, t * C:(t + 1) * C], in0=raw, scalar=0.0, in1=bank[:], op0=IS_GT, op1=MULT)
 
-        def dx_tile(starts, w1q, daq, kb=None, linked=False):
-            codes, scales = w1q
+        def dx_tile(parts, daq, kb=None, linked=False, order=(0, 1)):
             bank = psum.tile([P, C], F32, name="link", bufs=1) if linked else psum.tile([P, C], F32, name="dx", bufs=3)
-            for b in range(HB):
-                cols = slice(starts[b], starts[b] + P)
+            for b in order:
+                codes, scales, c0 = parts[b]
+                cols = slice(c0, c0 + P)
                 nc.tensor.matmul_mx(out=bank[:], lhsT=codes[:, cols].bitcast(E4), lhsT_scale=scales[:, cols],
-                                    rhs=daq[b][0][:].bitcast(E5), rhs_scale=daq[b][1][:], start=(b == 0), stop=(b == HB - 1))
+                                    rhs=daq[b][0][:].bitcast(E5), rhs_scale=daq[b][1][:], start=(b == order[0]), stop=(b == order[1]))
             if kb is None:
                 staged = keep.tile([P, C], F32, name="staged", bufs=4)
             else:
@@ -170,8 +174,11 @@ def tile_moe_bdx_mlp_relu_kernel(tc, dyT, a, w2, w1, gate, offs, out):
             nc.scalar.copy(out=staged[:], in_=bank[:])
             return staged
 
+        def both(w1q, c0):
+            return [(w1q[0], w1q[1], b * KC + c0) for b in range(HB)]
+
         def dx_pair(w1q, daq, linked=False):
-            return [dx_tile((0, KC), w1q, daq, None, linked), dx_tile((P, KC + P), w1q, daq)]
+            return [dx_tile(both(w1q, 0), daq, None, linked), dx_tile(both(w1q, P), daq)]
 
         windows = []
 
@@ -197,17 +204,18 @@ def tile_moe_bdx_mlp_relu_kernel(tc, dyT, a, w2, w1, gate, offs, out):
         dy[3] = load_dy(3)
         w2r01 = load_w2(0, 1)
         a00 = load_a(0, 0)
-        w1r00 = load_w1(0, 0, KC)
+        w1r00 = [load_w1b(0, 0, 0, KC)]
         a01 = load_a(0, 1)
+        w1r00.append(load_w1b(0, 1, 0, KC, 119))
+        w2r10 = load_w2(1, 0)
+        w1r01 = [load_w1b(0, b, KC, 2 * KC, 76 + 4 * b) for b in range(HB)]
         a10 = load_a(1, 0)
-        w1r01 = [load_w1b(0, 0, KC, 2 * KC)]
-        w2r10 = load_w2(1, 0, 72)
-        w1r01.append(load_w1b(0, 1, KC, 2 * KC))
-        w2r11 = load_w2(1, 1)
-        w1r02 = [load_w1b(0, 0, 2 * KC, K), load_w1b(0, 1, 2 * KC, K, 82)]
-        a11 = [load_a_pair(1, 1, 0, 68), load_a_pair(1, 1, 2)]
-        w1r10 = [load_w1b(1, 0, 0, KC), load_w1b(1, 1, 0, KC, 102)]
-        w1r1 = [load_w1b(1, 0, KC, K, 94), load_w1b(1, 1, KC, K, 86)]
+        w2r11 = load_w2(1, 1, 111)
+        w1r02 = load_w1(0, 2 * KC, K)
+        a11 = [load_a_pair(1, 1, 0, 68), load_a_pair(1, 1, 2, 72)]
+        w1r1b0 = load_w1b(1, 0, 0, K, 91)
+        w1r10 = [w1r1b0[:, :, 0:KC], load_w1b(1, 1, 0, KC, 86)]
+        w1r1 = [w1r1b0[:, :, KC:K], load_w1b(1, 1, KC, K, 103)]
 
         g0 = at(40, 4 * C, F32, "g0")
         arena = at(26, 6 * C, F32, "g1")
@@ -217,35 +225,40 @@ def tile_moe_bdx_mlp_relu_kernel(tc, dyT, a, w2, w1, gate, offs, out):
         for e, dst, gate_t in ((0, g0, gate0), (1, g1, gate1)):
             for t in (1, 2):
                 gather(e, t, dst, dy, gate_t)
-        group_w2(w2g, w2r00, "s")
+        group_w2(w2g, w2r00[:], "s")
         for t in (0, 3):
             gather(0, t, g0, dy, gate0)
         w2q0 = quantize(w2g, E4, "w2q00")
-        group_rows(ggrp0, rows4(g0[:]), [("s", 384), ("v", 128)])
+        group_rows(ggrp0, rows4(g0[:]), [("s", 320), ("v", 192)])
         gather(1, 0, g1, dy, gate1)
         gq0 = quantize(ggrp0, E5, "g0")
         gather(1, 3, g1, dy, gate1)
         w2g = at(22, 4 * C, BF16, "w2g01")
-        group_w2(w2g[:], w2r01, "s")
+        group_w2(w2g[:], w2r01[:], "s")
         plain = at(16, 4 * C, BF16, "plain00")
         w2q1 = quantize(w2g[:], E4, "w2q01")
         for t in range(4):
             da_plane(plain, t, w2q0, gq0, a00[:, t, :])
+        w1g0 = at(52, 2 * C, BF16, "w1g000")
+        interleave("s", words4(w1g0[:]), w1r00[0][:])
         ggrp1 = at(22, 4 * C, BF16, "ggrp1")
-        group_rows(ggrp1[:], rows4(g1), [("g", C)])
-        w1g = at(52, 4 * C, BF16, "w1g00")
-        group_w1(w1g[:], w1r00, "ss")
+        group_rows(ggrp1[:], rows4(g1), [("g", 256), ("s", 256)])
         dag0 = at(48, 4 * C, BF16, "dag00")
-        group_rows(dag0[:], rows4(plain[:]), [("s", C)])
+        group_rows(dag0[:], rows4(plain[:]), [("s", 320), ("g", 192)])
+        w1g1 = at(18, 2 * C, BF16, "w1g001")
+        interleave("s", words4(w1g1[:]), w1r00[1][:])
         plain = at(60, 4 * C, BF16, "plain01")
         for t in range(4):
             da_plane(plain, t, w2q1, gq0, a01[:, t, :])
+        w1qa = quantize(w1g0[:], E4, "w1q000", scales_kb=17.5)
         da0 = [quantize(dag0[:], E5, "da00")]
-        dag1 = at(14, 4 * C, BF16, "dag01")
-        group_rows(dag1[:], rows4(plain[:]), [("s", 320), ("v", 192)])
-        w1q = quantize(w1g[:], E4, "w1q00", codes=at(31, C, U32, "w1q00_codes"), scales_kb=19)
+        dag1 = at(13.5, 4 * C, BF16, "dag01")
+        group_rows(dag1[:], rows4(plain[:]), [("v", 384), ("s", 128)])
+        w1qb = quantize(w1g1[:], E4, "w1q001")
         da0.append(quantize(dag1[:], E5, "da01"))
         gq1 = quantize(ggrp1[:], E5, "g1", scales_kb=63)
+        staged = [dx_tile([(w1qa[0], w1qa[1], 0), (w1qb[0], w1qb[1], 0)], da0),
+                  dx_tile([(w1qa[0], w1qa[1], P), (w1qb[0], w1qb[1], P)], da0, order=(1, 0))]
 
         def sign_half(h, kb):
             half = at(kb, 2 * C, BF16, "sign%d" % h)
@@ -253,52 +266,52 @@ def tile_moe_bdx_mlp_relu_kernel(tc, dyT, a, w2, w1, gate, offs, out):
                                  in_=a10[:, :, h * KC:(h + 1) * KC].rearrange("p t (c i) -> p c t i", i=4), func=ACT.Sign)
             return half
 
-        staged = dx_pair(w1q, da0)
+        w2g = at(119, 4 * C, BF16, "w2g10")
+        group_w2(w2g[:], w2r10[:], "s")
+        w2q0 = quantize(w2g[:], E4, "w2q10", codes=at(38, C, U32, "w2q10_codes"))
         scatter_first(48, staged[0])
-        w1g = at(22, 4 * C, BF16, "w1g01")
-        group_w1(w1g[:], w1r01, "gg")
-        w2g = at(28, 4 * C, BF16, "w2g10")
-        group_w2(w2g[:], w2r10, "s")
-        w1q = quantize(w1g[:], E4, "w1q01", codes=at(72, C, U32, "w1q01_codes"), scales_kb=14)
-        w2q0 = quantize(w2g[:], E4, "w2q10", codes=at(80, C, U32, "w2q10_codes"))
-        scatter_first(22, staged[1])
-
-        w2g = at(32, 4 * C, BF16, "w2g11")
-        group_w2(w2g[:], w2r11, "s")
-        signs = [sign_half(0, 60), sign_half(1, 19)]
-        staged = dx_pair(w1q, da0, True)
-        scatter_first(64, staged[0])
+        w1g = at(119, 4 * C, BF16, "w1g01")
+        group_w1(w1g[:], w1r01, "gs")
         plain0 = at(52, 4 * C, BF16, "plain10")
         for t in range(4):
-            nc.scalar.copy(out=plain0[:, t * C:(t + 1) * C], in_=dh_tile(w2q0, gq1, t, t == 3)[:])
-        mask = at(14, 4 * C, BF16, "mask")
-        for h in range(2):
-            nc.scalar.activation(out=mask[:, 2 * h * C:2 * (h + 1) * C], in_=signs[h][:], func=ACT.Relu)
-        w1g = at(28, 4 * C, BF16, "w1g02")
-        group_w1(w1g[:], w1r02, "gg")
-        w1q = quantize(w1g[:], E4, "w1q02", scales_kb=81)
-        w2q1 = quantize(w2g[:], E4, "w2q11", scales_kb=81.75)
-        scatter_first(28, staged[1])
+            nc.scalar.copy(out=plain0[:, t * C:(t + 1) * C], in_=dh_tile(w2q0, gq1, t)[:])
+        w1q = quantize(w1g[:], E4, "w1q01", codes=at(43, C, U32, "w1q01_codes"), scales_kb=13.75)
+        scatter_first(78, staged[1])
 
-        dag0 = at(32, 4 * C, BF16, "dag10")
-        nc.gpsimd.tensor_tensor(words4(dag0[:]), rows4(plain0[:]).rearrange("p t c -> p c t"), words4(mask[:]), MULT)
+        staged = dx_pair(w1q, da0)
+        scatter_first(64, staged[0])
+        signs = [sign_half(0, 39)]
+        w2g = at(10, 4 * C, BF16, "w2g11")
+        group_w2(w2g[:], w2r11[:], "s")
+        mask = at(14, 4 * C, BF16, "mask")
+        nc.scalar.activation(out=mask[:, 0:2 * C], in_=signs[0][:], func=ACT.Relu)
+        signs.append(sign_half(1, 44))
+        nc.scalar.activation(out=mask[:, 2 * C:4 * C], in_=signs[1][:], func=ACT.Relu)
+        w1g = at(119, 4 * C, BF16, "w1g02")
+        group_w1(w1g[:], w1r02, "gg")
+        w1q = quantize(w1g[:], E4, "w1q02", codes=at(111, C, U32, "w1q02_codes"))
+        w2q1 = quantize(w2g[:], E4, "w2q11")
+        scatter_first(119, staged[1])
+
+        staged = dx_pair(w1q, da0)
+        dag0 = at(10, 4 * C, BF16, "dag10")
+        for h in range(2):
+            half = slice(h * KC, (h + 1) * KC)
+            nc.gpsimd.tensor_tensor(words4(dag0[:])[:, half, :], rows4(plain0[:])[:, :, half].rearrange("p t c -> p c t"), words4(mask[:])[:, half, :], MULT)
         plain1 = at(4, 4 * C, BF16, "plain11")
         for t in range(4):
             da_plane(plain1, t, w2q1, gq1, a11[t // 2][:, t % 2, :])
-        staged = dx_pair(w1q, da0)
         scatter_first(68, staged[0])
-        w1g = at(73, 4 * C, BF16, "w1g10")
+        w1g = at(112, 4 * C, BF16, "w1g10")
         group_w1(w1g[:], w1r10, "ss")
-        dag1 = at(102, 4 * C, BF16, "dag11")
+        dag1 = at(86, 4 * C, BF16, "dag11")
         group_rows(dag1[:], rows4(plain1[:]), [("s", C)])
-        da11 = quantize(dag1[:], E5, "da11", scales_kb=52)
-        da1 = [quantize(dag0[:], E5, "da10", scales_kb=4), da11]
-        w1q1 = [quantize(w1g[:], E4, "w1q10", codes=at(53, C, U32, "w1q10_codes"), scales_kb=5)]
-        scatter_first(33, staged[1])
-        for c, kb in ((1, 6), (2, 73)):
+        w1q1 = [quantize(w1g[:], E4, "w1q10", codes=at(53, C, U32, "w1q10_codes"), scales_kb=72)]
+        da1 = [quantize(dag0[:], E5, "da10", scales_kb=73), quantize(dag1[:], E5, "da11")]
+        scatter_first(2, staged[1])
+        for c, kb, engs in ((1, 6, "ss"), (2, 87, "gs")):
             w1g = at(kb, 4 * C, BF16, "w1g1%d" % c)
-            group_w1(w1g[:], w1r1, "ss", (c - 1) * KC)
-            w1q1.append(quantize(w1g[:], E4, "w1q1%d" % c, scales_kb=31.5 + 0.5 * c))
+            group_w1(w1g[:], w1r1, engs, (c - 1) * KC)
+            w1q1.append(quantize(w1g[:], E4, "w1q1%d" % c, scales_kb=85.5 + 0.5 * c))
         for kt in range(KT):
-            c0 = (kt % 2) * P
-            scatter_last(kt, dx_tile((c0, KC + c0), w1q1[kt // 2], da1, 86 + 2 * kt))
+            scatter_last(kt, dx_tile(both(w1q1[kt // 2], (kt % 2) * P), da1, (103, 105, 107, 109, 91, 93)[kt]))

@@ -21,10 +21,17 @@ IS_GT = mybir.AluOpType.is_gt
 ACT = mybir.ActivationFunctionType
 
 P = 128
-HB = H // 512
+PASS = 512
+HB = H // PASS
 KT = K // P
-KC = 256
+KC = 2 * P
+HALF = C // 2
 KB = 1024
+
+G0_ON_VECTOR = 192
+G1_ON_GPSIMD = 256
+DA00_ON_GPSIMD = 192
+DA01_ON_VECTOR = 448
 
 
 def tile_moe_bdx_mlp_relu_kernel(tc, dyT, a, w2, w1, gate, offs, out):
@@ -34,156 +41,118 @@ def tile_moe_bdx_mlp_relu_kernel(tc, dyT, a, w2, w1, gate, offs, out):
         placed = ctx.enter_context(tc.tile_pool(name="placed", bufs=1))
         psum = ctx.enter_context(tc.psum_pool(name="psum", bufs=4))
 
-        def at(kb, width, dtype, name):
-            return placed.tile([P, width], dtype, name=name, offset=int(kb * KB), align_bytes=64)
+        def at(kb, shape, dtype, name):
+            return placed.tile([P] + shape, dtype, name=name, offset=int(kb * KB), align_bytes=64)
 
-        def rows4(ap):
+        def grouped_at(kb, name, columns=C):
+            return at(kb, [4 * columns], BF16, name)
+
+        def planes(ap):
             return ap.rearrange("p (t c) -> p t c", t=4)
 
-        def words4(ap):
+        def words(ap):
             return ap.rearrange("p (c t) -> p c t", t=4)
 
-        def copy_on(eng, out_ap, in_ap):
-            if eng == "v":
-                nc.vector.tensor_copy(out=out_ap, in_=in_ap)
-            elif eng == "s":
-                nc.scalar.copy(out=out_ap, in_=in_ap)
-            else:
-                nc.gpsimd.tensor_scalar(out=out_ap, in0=in_ap, scalar1=1.0, scalar2=0.0, op0=MULT, op1=ADD)
+        def four_neighbours(dst, src):
+            return dst.rearrange("p (c i) t -> p c t i", i=4), src.rearrange("p t (c i) -> p c t i", i=4)
 
-        def interleave(eng, dst, src):
-            if eng == "g":
-                copy_on(eng, dst, src.rearrange("p t c -> p c t"))
-            else:
-                copy_on(eng, dst.rearrange("p (c i) t -> p c t i", i=4), src.rearrange("p t (c i) -> p c t i", i=4))
+        def on_scalar(dst, src):
+            dst_view, src_view = four_neighbours(dst, src)
+            nc.scalar.copy(out=dst_view, in_=src_view)
 
-        def group_rows(dst, src, shares):
-            c0 = 0
-            for eng, width in shares:
-                interleave(eng, words4(dst)[:, c0:c0 + width, :], src[:, :, c0:c0 + width])
-                c0 = c0 + width
+        def on_vector(dst, src):
+            dst_view, src_view = four_neighbours(dst, src)
+            nc.vector.tensor_copy(out=dst_view, in_=src_view)
 
-        def group_w2(dst, raw, eng):
-            if eng == "g":
-                copy_on(eng, dst.rearrange("p (t m j) -> p t m j", t=4, j=4), raw.rearrange("p j (m t) -> p t m j", t=4))
-            else:
-                copy_on(eng, dst.rearrange("p (t m j) -> p m j t", t=4, j=4), raw.rearrange("p j (m t) -> p m j t", t=4))
+        def on_gpsimd(dst, src):
+            nc.gpsimd.tensor_scalar(out=dst, in0=src.rearrange("p t c -> p c t"), scalar1=1.0, scalar2=0.0, op0=MULT, op1=ADD)
 
-        def group_w1(dst, raws, engs, c0=0):
+        def interleave_split(dst, src, first, width, second):
+            first(words(dst)[:, 0:width, :], src[:, :, 0:width])
+            second(words(dst)[:, width:C, :], src[:, :, width:C])
+
+        def group_w2(dst, raw):
+            nc.scalar.copy(out=dst.rearrange("p (t m j) -> p m j t", t=4, j=4), in_=raw[:].rearrange("p j (m t) -> p m j t", t=4))
+
+        def group_w1(dst, raws, copies, c0=0):
             for b in range(HB):
-                interleave(engs[b], words4(dst)[:, b * KC:(b + 1) * KC, :], raws[b][:, :, c0:c0 + KC])
+                copies[b](words(dst)[:, b * KC:(b + 1) * KC, :], raws[b][:, :, c0:c0 + KC])
 
-        def quantize(grouped, fmt, name, codes=None, scales_kb=None):
+        def quantize(grouped, fmt, name, codes_kb=None, scales_kb=None):
             width = grouped.shape[1] // 4
-            if codes is None:
+            if codes_kb is None:
                 codes = keep.tile([P, width], U32, name=name + "_codes", align_bytes=64)
+            else:
+                codes = at(codes_kb, [width], U32, name + "_codes")
             if scales_kb is None:
                 scales = keep.tile([P, width], U8, name=name + "_scales", align_bytes=64)
             else:
-                scales = at(scales_kb, width, U8, name + "_scales")
+                scales = at(scales_kb, [width], U8, name + "_scales")
             nc.vector.quantize_mx(out=codes[:].bitcast(fmt), scales=scales[:], in_=grouped)
             return codes, scales
 
-        offs_t = keep.tile([P, E * C // 16], U16, name="offs_t")
-        nc.sync.dma_start(offs_t[:], offs)
-        dy_view = dyT.rearrange("(p t) j -> p t j", t=4)
+        def load(name, view, kb=None):
+            shape = list(view.shape[1:])
+            raw = keep.tile([P] + shape, F32, name=name) if kb is None else at(kb, shape, F32, name)
+            nc.sync.dma_start(out=raw[:], in_=view)
+            return raw
+
+        def by_planes(rows):
+            return rows.rearrange("(p t) c -> p t c", t=4)
 
         def load_dy(t):
-            plane = at(4 * t, T, F32, "dy%d" % t)
-            nc.sync.dma_start(out=plane[:], in_=dy_view[:, t, :])
-            return plane
-
-        def load_gate(e):
-            g = keep.tile([P, C], F32, name="gate%d" % e)
-            nc.sync.dma_start(out=g[:], in_=gate[0:P, e * C:(e + 1) * C])
-            return g
-
-        def load_gate_row(e, queue):
-            row = keep.tile([P, 4], F32, name="gate_row%d" % e)
-            queue.dma_start(out=row[:], in_=gate[e, e * C:(e + 1) * C].rearrange("(n m) -> n m", m=4))
-            return row
-
-        def spread_gate(e, row, ident):
-            bank = psum.tile([P, C], F32, name="dh")
-            for m in range(4):
-                nc.tensor.transpose(bank[:, m * P:(m + 1) * P], row[:, m:m + 1].to_broadcast([P, P]), ident[:])
-            g = keep.tile([P, C], F32, name="gate%d" % e)
-            nc.scalar.copy(out=g[:].rearrange("p (n m) -> p n m", m=4), in_=bank[:].rearrange("p (m n) -> p n m", m=4))
-            return g
-
-        def load_w2_whole(e):
-            return load_rows("w2raw%d" % e, w2[e])
-
-        def load_w1b(e, b, c0, c1, kb=None):
-            return load_rows("w1raw%d%d_%d" % (e, b, c0), w1[e, b * 512:(b + 1) * 512, c0:c1], kb)
-
-        def load_a_pair(e, b, t0, kb=None):
-            if kb is None:
-                raw = keep.tile([P, 2, C], F32, name="apair%d%d%d" % (e, b, t0))
-            else:
-                raw = placed.tile([P, 2, C], F32, name="apair%d%d%d" % (e, b, t0), offset=int(kb * KB), align_bytes=64)
-            rows = a[b * 512:(b + 1) * 512, e * C:(e + 1) * C].rearrange("(p j) c -> p j c", j=4)
-            nc.sync.dma_start(out=raw[:], in_=rows[:, t0:t0 + 2, :])
-            return raw
-
-        def load_rows(name, rows, kb=None):
-            if kb is None:
-                raw = keep.tile([P, 4, rows.shape[1]], F32, name=name)
-            else:
-                raw = placed.tile([P, 4, rows.shape[1]], F32, name=name, offset=int(kb * KB), align_bytes=64)
-            nc.sync.dma_start(out=raw[:], in_=rows.rearrange("(p j) c -> p j c", j=4))
-            return raw
+            return load("dy%d" % t, by_planes(dyT)[:, t, :], 4 * t)
 
         def load_w2(e, b, kb=None):
-            return load_rows("w2raw%d%d" % (e, b), w2[e, :, b * 512:(b + 1) * 512], kb)
+            return load("w2raw%d%d" % (e, b), by_planes(w2[e, :, b * PASS:(b + 1) * PASS]), kb)
 
-        def load_a(e, b, kb=None):
-            return load_rows("araw%d%d" % (e, b), a[b * 512:(b + 1) * 512, e * C:(e + 1) * C], kb)
+        def a_planes(e, b):
+            return by_planes(a[b * PASS:(b + 1) * PASS, e * C:(e + 1) * C])
 
-        def load_w1(e, c0, c1):
-            return [load_rows("w1raw%d%d_%d" % (e, b, c0), w1[e, b * 512:(b + 1) * 512, c0:c1]) for b in range(HB)]
+        def load_w1(e, b, c0, c1, kb=None):
+            return load("w1raw%d%d_%d" % (e, b, c0), by_planes(w1[e, b * PASS:(b + 1) * PASS, c0:c1]), kb)
 
         def slots_of(e):
             return offs_t[:, e * (C // 16):(e + 1) * (C // 16)]
 
-        def gather(e, t, dst, dy, gate_t):
-            nc.vector.tensor_tensor(dst[:, t * C:(t + 1) * C], dy[t][:].indirect(slots_of(e)), gate_t[:], MULT)
+        def gather(e, t, dst, gate_ap):
+            nc.vector.tensor_tensor(dst[:, t * C:(t + 1) * C], dy[t][:].indirect(slots_of(e)), gate_ap, MULT)
 
-        def dh_tile(w2q, gq, t, linked=False):
-            bank = psum.tile([P, C], F32, name="link", bufs=1) if linked else psum.tile([P, C], F32, name="dh")
+        def copy_gate(dst, bank):
+            nc.scalar.copy(out=dst.rearrange("p (n m) -> p n m", m=4), in_=bank[:].rearrange("p (m n) -> p n m", m=4))
+
+        def dh_plane(w2q, gq, t):
+            bank = psum.tile([P, C], F32, name="dh")
             cols = slice(t * P, (t + 1) * P)
             nc.tensor.matmul_mx(out=bank[:], lhsT=w2q[0][:, cols].bitcast(E4), lhsT_scale=w2q[1][:, cols],
                                 rhs=gq[0][:].bitcast(E5), rhs_scale=gq[1][:], start=True, stop=True)
             return bank
 
-        def da_plane(plain, t, w2q, gq, raw):
-            bank = dh_tile(w2q, gq, t)
-            nc.vector.scalar_tensor_tensor(out=plain[:, t * C:(t + 1) * C], in0=raw, scalar=0.0, in1=bank[:], op0=IS_GT, op1=MULT)
+        def da_plane(dst, t, w2q, gq, a_plane):
+            bank = dh_plane(w2q, gq, t)
+            nc.vector.scalar_tensor_tensor(out=dst[:, t * C:(t + 1) * C], in0=a_plane, scalar=0.0, in1=bank[:], op0=IS_GT, op1=MULT)
 
-        def dx_tile(parts, daq, kb=None, linked=False, order=(0, 1)):
-            bank = psum.tile([P, C], F32, name="link", bufs=1) if linked else psum.tile([P, C], F32, name="dx", bufs=3)
+        def dx_tile(parts, daq, kb=None, order=(0, 1)):
+            bank = psum.tile([P, C], F32, name="dx", bufs=3)
             for b in order:
                 codes, scales, c0 = parts[b]
                 cols = slice(c0, c0 + P)
                 nc.tensor.matmul_mx(out=bank[:], lhsT=codes[:, cols].bitcast(E4), lhsT_scale=scales[:, cols],
                                     rhs=daq[b][0][:].bitcast(E5), rhs_scale=daq[b][1][:], start=(b == order[0]), stop=(b == order[1]))
-            if kb is None:
-                staged = keep.tile([P, C], F32, name="staged", bufs=4)
-            else:
-                staged = at(kb, C, F32, "staged%d" % kb)
+            staged = keep.tile([P, C], F32, name="staged", bufs=4) if kb is None else at(kb, [C], F32, "staged%d" % kb)
             nc.scalar.copy(out=staged[:], in_=bank[:])
             return staged
 
-        def both(w1q, c0):
+        def chunk_parts(w1q, c0):
             return [(w1q[0], w1q[1], b * KC + c0) for b in range(HB)]
 
-        def dx_pair(w1q, daq, linked=False):
-            return [dx_tile(both(w1q, 0), daq, None, linked), dx_tile(both(w1q, P), daq)]
+        def dx_pair(w1q, daq):
+            return [dx_tile(chunk_parts(w1q, c0), daq) for c0 in (0, P)]
 
         windows = []
 
         def scatter_first(kb, staged):
-            window = at(kb, T, F32, "window%d" % len(windows))
+            window = at(kb, [T], F32, "window%d" % len(windows))
             windows.append(window)
             nc.vector.tensor_copy(out=window[:].indirect(slots_of(0)), in_=staged[:])
 
@@ -191,127 +160,141 @@ def tile_moe_bdx_mlp_relu_kernel(tc, dyT, a, w2, w1, gate, offs, out):
             nc.vector.tensor_copy(out=windows[kt][:].indirect(slots_of(1)), in_=staged[:])
             nc.sync.dma_start(out=out[kt * P:(kt + 1) * P, :], in_=windows[kt][:])
 
-        ident = at(26, P, F32, "ident")
+        def sign_half(h, kb):
+            half = grouped_at(kb, "sign%d" % h, HALF)
+            dst_view, src_view = four_neighbours(words(half[:]), a10[:, :, h * HALF:(h + 1) * HALF])
+            nc.scalar.activation(out=dst_view, in_=src_view, func=ACT.Sign)
+            return half
+
+        offs_t = keep.tile([P, E * C // 16], U16, name="offs_t")
+        nc.sync.dma_start(offs_t[:], offs)
+        ident = at(26, [P], F32, "ident")
         make_identity(nc, ident[:])
-        row = load_gate_row(0, nc.scalar)
+        gate_row = load("gate_row1", gate[1, C:2 * C].rearrange("(n m) -> n m", m=4))
         dy = {1: load_dy(1)}
-        gate0 = spread_gate(0, row, ident)
-        row = load_gate_row(1, nc.sync)
+        gate0 = load("gate0", gate[0:P, 0:C])
         dy[2] = load_dy(2)
-        gate1 = spread_gate(1, row, ident)
+        gate_bank = psum.tile([P, C], F32, name="dh")
+        for m in range(4):
+            nc.tensor.transpose(gate_bank[:, m * P:(m + 1) * P], gate_row[:, m:m + 1].to_broadcast([P, P]), ident[:])
         w2r00 = load_w2(0, 0)
         dy[0] = load_dy(0)
         dy[3] = load_dy(3)
         w2r01 = load_w2(0, 1)
-        a00 = load_a(0, 0)
-        w1r00 = [load_w1b(0, 0, 0, KC)]
-        a01 = load_a(0, 1)
-        w1r00.append(load_w1b(0, 1, 0, KC, 119))
+        a00 = load("araw00", a_planes(0, 0))
+        w1r00 = [load_w1(0, 0, 0, KC)]
+        a01 = load("araw01", a_planes(0, 1))
+        w1r00.append(load_w1(0, 1, 0, KC, 119))
         w2r10 = load_w2(1, 0)
-        w1r01 = [load_w1b(0, b, KC, 2 * KC, 76 + 4 * b) for b in range(HB)]
-        a10 = load_a(1, 0)
+        w1r01 = [load_w1(0, b, KC, 2 * KC, 76 + 4 * b) for b in range(HB)]
+        a10 = load("araw10", a_planes(1, 0))
         w2r11 = load_w2(1, 1, 111)
-        w1r02 = load_w1(0, 2 * KC, K)
-        a11 = [load_a_pair(1, 1, 0, 68), load_a_pair(1, 1, 2, 72)]
-        w1r1b0 = load_w1b(1, 0, 0, K, 91)
-        w1r10 = [w1r1b0[:, :, 0:KC], load_w1b(1, 1, 0, KC, 86)]
-        w1r1 = [w1r1b0[:, :, KC:K], load_w1b(1, 1, KC, K, 103)]
+        w1r02 = [load_w1(0, b, 2 * KC, K) for b in range(HB)]
+        a11 = [load("apair11%d" % t, a_planes(1, 1)[:, t:t + 2, :], 68 + 2 * t) for t in (0, 2)]
+        w1r1b0 = load_w1(1, 0, 0, K, 91)
+        w1r10 = [w1r1b0[:, :, 0:KC], load_w1(1, 1, 0, KC, 86)]
+        w1r1 = [w1r1b0[:, :, KC:K], load_w1(1, 1, KC, K, 103)]
 
-        g0 = at(40, 4 * C, F32, "g0")
-        arena = at(26, 6 * C, F32, "g1")
-        g1 = arena[:, C:5 * C]
-        w2g = arena[:, 0:2 * C].bitcast(BF16)
-        ggrp0 = arena[:, 4 * C:6 * C].bitcast(BF16)
-        for e, dst, gate_t in ((0, g0, gate0), (1, g1, gate1)):
-            for t in (1, 2):
-                gather(e, t, dst, dy, gate_t)
-        group_w2(w2g, w2r00[:], "s")
+        g0 = at(40, [4 * C], F32, "g0")
+        shared = at(26, [6 * C], F32, "g1")
+        g1 = shared[:, C:5 * C]
+        w2g00 = shared[:, 0:2 * C].bitcast(BF16)
+        ggrp0 = shared[:, 4 * C:6 * C].bitcast(BF16)
+        for t in (1, 2):
+            gather(0, t, g0, gate0[:])
+        for t, later in ((1, 0), (2, 3)):
+            parked = g0[:, later * C:(later + 1) * C]
+            copy_gate(parked, gate_bank)
+            gather(1, t, g1, parked)
+        gate1 = keep.tile([P, C], F32, name="gate1")
+        copy_gate(gate1[:], gate_bank)
+        group_w2(w2g00, w2r00)
         for t in (0, 3):
-            gather(0, t, g0, dy, gate0)
-        w2q0 = quantize(w2g, E4, "w2q00")
-        group_rows(ggrp0, rows4(g0[:]), [("s", 320), ("v", 192)])
-        gather(1, 0, g1, dy, gate1)
+            gather(0, t, g0, gate0[:])
+        w2q00 = quantize(w2g00, E4, "w2q00")
+        interleave_split(ggrp0, planes(g0[:]), on_scalar, C - G0_ON_VECTOR, on_vector)
+        gather(1, 0, g1, gate1[:])
         gq0 = quantize(ggrp0, E5, "g0")
-        gather(1, 3, g1, dy, gate1)
-        w2g = at(22, 4 * C, BF16, "w2g01")
-        group_w2(w2g[:], w2r01[:], "s")
-        plain = at(16, 4 * C, BF16, "plain00")
-        w2q1 = quantize(w2g[:], E4, "w2q01")
+        gather(1, 3, g1, gate1[:])
+
+        w2g01 = grouped_at(22, "w2g01")
+        group_w2(w2g01[:], w2r01)
+        da00_planes = grouped_at(16, "plain00")
+        w2q01 = quantize(w2g01[:], E4, "w2q01")
         for t in range(4):
-            da_plane(plain, t, w2q0, gq0, a00[:, t, :])
-        w1g0 = at(52, 2 * C, BF16, "w1g000")
-        interleave("s", words4(w1g0[:]), w1r00[0][:])
-        ggrp1 = at(22, 4 * C, BF16, "ggrp1")
-        group_rows(ggrp1[:], rows4(g1), [("g", 256), ("s", 256)])
-        dag0 = at(48, 4 * C, BF16, "dag00")
-        group_rows(dag0[:], rows4(plain[:]), [("s", 320), ("g", 192)])
-        w1g1 = at(18, 2 * C, BF16, "w1g001")
-        interleave("s", words4(w1g1[:]), w1r00[1][:])
-        plain = at(60, 4 * C, BF16, "plain01")
+            da_plane(da00_planes, t, w2q00, gq0, a00[:, t, :])
+        w1g000 = grouped_at(52, "w1g000", KC)
+        on_scalar(words(w1g000[:]), w1r00[0][:])
+        ggrp1 = grouped_at(22, "ggrp1")
+        interleave_split(ggrp1[:], planes(g1), on_gpsimd, G1_ON_GPSIMD, on_scalar)
+        dag00 = grouped_at(48, "dag00")
+        interleave_split(dag00[:], planes(da00_planes[:]), on_scalar, C - DA00_ON_GPSIMD, on_gpsimd)
+        w1g001 = grouped_at(18, "w1g001", KC)
+        on_scalar(words(w1g001[:]), w1r00[1][:])
+        da01_planes = grouped_at(60, "plain01")
         for t in range(4):
-            da_plane(plain, t, w2q1, gq0, a01[:, t, :])
-        w1qa = quantize(w1g0[:], E4, "w1q000", scales_kb=17.5)
-        da0 = [quantize(dag0[:], E5, "da00")]
-        dag1 = at(13.5, 4 * C, BF16, "dag01")
-        group_rows(dag1[:], rows4(plain[:]), [("v", 384), ("s", 128)])
-        w1qb = quantize(w1g1[:], E4, "w1q001")
-        da0.append(quantize(dag1[:], E5, "da01"))
+            da_plane(da01_planes, t, w2q01, gq0, a01[:, t, :])
+        w1q000 = quantize(w1g000[:], E4, "w1q000", scales_kb=17.5)
+        daq0 = [quantize(dag00[:], E5, "da00")]
+        dag01 = grouped_at(13.5, "dag01")
+        interleave_split(dag01[:], planes(da01_planes[:]), on_vector, DA01_ON_VECTOR, on_scalar)
+        w1q001 = quantize(w1g001[:], E4, "w1q001")
+        daq0.append(quantize(dag01[:], E5, "da01"))
         gq1 = quantize(ggrp1[:], E5, "g1", scales_kb=63)
-        staged = [dx_tile([(w1qa[0], w1qa[1], 0), (w1qb[0], w1qb[1], 0)], da0),
-                  dx_tile([(w1qa[0], w1qa[1], P), (w1qb[0], w1qb[1], P)], da0, order=(1, 0))]
+        staged = [dx_tile([w1q000 + (c0,), w1q001 + (c0,)], daq0, order=order) for c0, order in ((0, (0, 1)), (P, (1, 0)))]
 
-        def sign_half(h, kb):
-            half = at(kb, 2 * C, BF16, "sign%d" % h)
-            nc.scalar.activation(out=words4(half[:]).rearrange("p (c i) t -> p c t i", i=4),
-                                 in_=a10[:, :, h * KC:(h + 1) * KC].rearrange("p t (c i) -> p c t i", i=4), func=ACT.Sign)
-            return half
-
-        w2g = at(119, 4 * C, BF16, "w2g10")
-        group_w2(w2g[:], w2r10[:], "s")
-        w2q0 = quantize(w2g[:], E4, "w2q10", codes=at(38, C, U32, "w2q10_codes"))
+        w2g10 = grouped_at(119, "w2g10")
+        group_w2(w2g10[:], w2r10)
+        w2q10 = quantize(w2g10[:], E4, "w2q10", codes_kb=38)
         scatter_first(48, staged[0])
-        w1g = at(119, 4 * C, BF16, "w1g01")
-        group_w1(w1g[:], w1r01, "gs")
-        plain0 = at(52, 4 * C, BF16, "plain10")
+        w1g01 = grouped_at(119, "w1g01")
+        group_w1(w1g01[:], w1r01, (on_gpsimd, on_scalar))
+        dh10_planes = grouped_at(52, "plain10")
         for t in range(4):
-            nc.scalar.copy(out=plain0[:, t * C:(t + 1) * C], in_=dh_tile(w2q0, gq1, t)[:])
-        w1q = quantize(w1g[:], E4, "w1q01", codes=at(43, C, U32, "w1q01_codes"), scales_kb=13.75)
+            nc.scalar.copy(out=dh10_planes[:, t * C:(t + 1) * C], in_=dh_plane(w2q10, gq1, t)[:])
+        w1q01 = quantize(w1g01[:], E4, "w1q01", codes_kb=43, scales_kb=13.75)
+
         scatter_first(78, staged[1])
-
-        staged = dx_pair(w1q, da0)
+        staged = dx_pair(w1q01, daq0)
         scatter_first(64, staged[0])
-        signs = [sign_half(0, 39)]
-        w2g = at(10, 4 * C, BF16, "w2g11")
-        group_w2(w2g[:], w2r11[:], "s")
-        mask = at(14, 4 * C, BF16, "mask")
-        nc.scalar.activation(out=mask[:, 0:2 * C], in_=signs[0][:], func=ACT.Relu)
-        signs.append(sign_half(1, 44))
-        nc.scalar.activation(out=mask[:, 2 * C:4 * C], in_=signs[1][:], func=ACT.Relu)
-        w1g = at(119, 4 * C, BF16, "w1g02")
-        group_w1(w1g[:], w1r02, "gg")
-        w1q = quantize(w1g[:], E4, "w1q02", codes=at(111, C, U32, "w1q02_codes"))
-        w2q1 = quantize(w2g[:], E4, "w2q11")
-        scatter_first(119, staged[1])
+        sign0 = sign_half(0, 39)
+        w2g11 = grouped_at(10, "w2g11")
+        group_w2(w2g11[:], w2r11)
+        mask = grouped_at(14, "mask")
+        nc.scalar.activation(out=mask[:, 0:4 * HALF], in_=sign0[:], func=ACT.Relu)
+        sign1 = sign_half(1, 44)
+        nc.scalar.activation(out=mask[:, 4 * HALF:4 * C], in_=sign1[:], func=ACT.Relu)
+        w1g02 = grouped_at(119, "w1g02")
+        group_w1(w1g02[:], w1r02, (on_gpsimd, on_gpsimd))
+        w1q02 = quantize(w1g02[:], E4, "w1q02", codes_kb=111)
+        w2q11 = quantize(w2g11[:], E4, "w2q11")
 
-        staged = dx_pair(w1q, da0)
-        dag0 = at(10, 4 * C, BF16, "dag10")
+        scatter_first(119, staged[1])
+        staged = dx_pair(w1q02, daq0)
+        dag10 = grouped_at(10, "dag10")
         for h in range(2):
-            half = slice(h * KC, (h + 1) * KC)
-            nc.gpsimd.tensor_tensor(words4(dag0[:])[:, half, :], rows4(plain0[:])[:, :, half].rearrange("p t c -> p c t"), words4(mask[:])[:, half, :], MULT)
-        plain1 = at(4, 4 * C, BF16, "plain11")
+            half = slice(h * HALF, (h + 1) * HALF)
+            nc.gpsimd.tensor_tensor(words(dag10[:])[:, half, :], planes(dh10_planes[:])[:, :, half].rearrange("p t c -> p c t"),
+                                    words(mask[:])[:, half, :], MULT)
+        da11_planes = grouped_at(4, "plain11")
         for t in range(4):
-            da_plane(plain1, t, w2q1, gq1, a11[t // 2][:, t % 2, :])
+            da_plane(da11_planes, t, w2q11, gq1, a11[t // 2][:, t % 2, :])
         scatter_first(68, staged[0])
-        w1g = at(112, 4 * C, BF16, "w1g10")
-        group_w1(w1g[:], w1r10, "ss")
-        dag1 = at(86, 4 * C, BF16, "dag11")
-        group_rows(dag1[:], rows4(plain1[:]), [("s", C)])
-        w1q1 = [quantize(w1g[:], E4, "w1q10", codes=at(53, C, U32, "w1q10_codes"), scales_kb=72)]
-        da1 = [quantize(dag0[:], E5, "da10", scales_kb=73), quantize(dag1[:], E5, "da11")]
+        w1g10 = grouped_at(112, "w1g10")
+        group_w1(w1g10[:], w1r10, (on_scalar, on_scalar))
+        dag11 = grouped_at(86, "dag11")
+        on_scalar(words(dag11[:]), planes(da11_planes[:]))
+        w1q1 = [quantize(w1g10[:], E4, "w1q10", codes_kb=53, scales_kb=72)]
+        daq1 = [quantize(dag10[:], E5, "da10", scales_kb=73), quantize(dag11[:], E5, "da11")]
+
         scatter_first(2, staged[1])
-        for c, kb, engs in ((1, 6, "ss"), (2, 87, "gs")):
-            w1g = at(kb, 4 * C, BF16, "w1g1%d" % c)
-            group_w1(w1g[:], w1r1, engs, (c - 1) * KC)
-            w1q1.append(quantize(w1g[:], E4, "w1q1%d" % c, scales_kb=85.5 + 0.5 * c))
+        w1g11 = grouped_at(6, "w1g11")
+        group_w1(w1g11[:], w1r1, (on_scalar, on_scalar), 0)
+        w1q1.append(quantize(w1g11[:], E4, "w1q11", scales_kb=86))
+        w1g12 = grouped_at(87, "w1g12")
+        group_w1(w1g12[:], w1r1, (on_gpsimd, on_scalar), KC)
+        w1q1.append(quantize(w1g12[:], E4, "w1q12", scales_kb=86.5))
+
         for kt in range(KT):
-            scatter_last(kt, dx_tile(both(w1q1[kt // 2], (kt % 2) * P), da1, (103, 105, 107, 109, 91, 93)[kt]))
+            kb = 103 + 2 * kt if kt < 4 else 91 + 2 * (kt - 4)
+            scatter_last(kt, dx_tile(chunk_parts(w1q1[kt // 2], (kt % 2) * P), daq1, kb))

@@ -112,8 +112,8 @@ def tile_moe_bdx_mlp_relu_kernel(tc, dyT, a, w2, w1, gate, offs, out):
         def load_w1(e, b, c0, c1, kb=None):
             return load("w1raw%d%d_%d" % (e, b, c0), by_planes(w1[e, b * PASS:(b + 1) * PASS, c0:c1]), kb)
 
-        def slots_of(e):
-            return offs_t[:, e * (C // 16):(e + 1) * (C // 16)]
+        def slots_of(e, s0=0, s1=C):
+            return offs_t[:, (e * C + s0) // 16:(e * C + s1) // 16]
 
         def gather(e, t, dst, gate_ap):
             nc.vector.tensor_tensor(dst[:, t * C:(t + 1) * C], dy[t][:].indirect(slots_of(e)), gate_ap, MULT)
@@ -132,22 +132,33 @@ def tile_moe_bdx_mlp_relu_kernel(tc, dyT, a, w2, w1, gate, offs, out):
             bank = dh_plane(w2q, gq, t)
             nc.vector.scalar_tensor_tensor(out=dst[:, t * C:(t + 1) * C], in0=a_plane, scalar=0.0, in1=bank[:], op0=IS_GT, op1=MULT)
 
-        def dx_tile(parts, daq, kb=None, order=(0, 1)):
-            bank = psum.tile([P, C], F32, name="dx", bufs=3)
+        def dx_bank(parts, daq, order=(0, 1), tag="dx"):
+            bank = psum.tile([P, C], F32, name=tag)
             for b in order:
                 codes, scales, c0 = parts[b]
                 cols = slice(c0, c0 + P)
                 nc.tensor.matmul_mx(out=bank[:], lhsT=codes[:, cols].bitcast(E4), lhsT_scale=scales[:, cols],
                                     rhs=daq[b][0][:].bitcast(E5), rhs_scale=daq[b][1][:], start=(b == order[0]), stop=(b == order[1]))
-            staged = keep.tile([P, C], F32, name="staged", bufs=4) if kb is None else at(kb, [C], F32, "staged%d" % kb)
-            nc.scalar.copy(out=staged[:], in_=bank[:])
+            return bank
+
+        def dx_tile(parts, daq, order=(0, 1), tag="dx"):
+            staged = keep.tile([P, C], F32, name="staged", bufs=4)
+            nc.scalar.copy(out=staged[:], in_=dx_bank(parts, daq, order, tag)[:])
             return staged
+
+        def stage_half(bank, h, kb=None):
+            staged = keep.tile([P, HALF], F32, name="staged_half", bufs=4) if kb is None else at(kb, [HALF], F32, "staged_held")
+            nc.scalar.copy(out=staged[:], in_=bank[:, h * HALF:(h + 1) * HALF])
+            return staged
+
+        def scatter_half(kt, e, h, staged):
+            nc.vector.tensor_copy(out=windows[kt][:].indirect(slots_of(e, h * HALF, (h + 1) * HALF)), in_=staged[:])
+
+        def store(kt):
+            nc.sync.dma_start(out=out[kt * P:(kt + 1) * P, :], in_=windows[kt][:])
 
         def chunk_parts(w1q, c0):
             return [(w1q[0], w1q[1], b * KC + c0) for b in range(HB)]
-
-        def dx_pair(w1q, daq):
-            return [dx_tile(chunk_parts(w1q, c0), daq) for c0 in (0, P)]
 
         windows = []
 
@@ -156,15 +167,36 @@ def tile_moe_bdx_mlp_relu_kernel(tc, dyT, a, w2, w1, gate, offs, out):
             windows.append(window)
             nc.vector.tensor_copy(out=window[:].indirect(slots_of(0)), in_=staged[:])
 
-        def scatter_last(kt, staged):
-            nc.vector.tensor_copy(out=windows[kt][:].indirect(slots_of(1)), in_=staged[:])
-            nc.sync.dma_start(out=out[kt * P:(kt + 1) * P, :], in_=windows[kt][:])
-
-        def sign_half(h, kb):
-            half = grouped_at(kb, "sign%d" % h, HALF)
-            dst_view, src_view = four_neighbours(words(half[:]), a10[:, :, h * HALF:(h + 1) * HALF])
+        def sign_into(dst, a_part):
+            dst_view, src_view = four_neighbours(words(dst), a_part)
             nc.scalar.activation(out=dst_view, in_=src_view, func=ACT.Sign)
-            return half
+
+        def mask_of(sign, kb, name):
+            mask = grouped_at(kb, "mask" + name, HALF)
+            nc.scalar.activation(out=mask[:], in_=sign[:], func=ACT.Relu)
+            return mask
+
+        def round_dh11(banks, h):
+            for t in range(4):
+                nc.scalar.copy(out=dh_planes[:, 1, t, h * HALF:(h + 1) * HALF], in_=banks[t][:, h * HALF:(h + 1) * HALF])
+
+        def product(b, mask, kb, name):
+            da = grouped_at(kb, "dag" + name, HALF)
+            nc.gpsimd.tensor_tensor(words(da[:]), dh_planes[:, b, :, 0:HALF].rearrange("p t c -> p c t"), words(mask[:]), MULT)
+            return da
+
+        def quarter_sign(sign, q, b):
+            sign_into(sign[:, b * C:(b + 1) * C], second[b][:, :, q * P:(q + 1) * P])
+
+        def quarter_product(q, mask):
+            slots = slice(q * P, (q + 1) * P)
+            nc.gpsimd.tensor_tensor(dag_second[:].rearrange("p (b c t) -> p b c t", b=HB, t=4)[:, :, slots, :],
+                                    dh_planes[:, :, :, HALF + q * P:HALF + (q + 1) * P].rearrange("p b t c -> p b c t"),
+                                    mask[:].rearrange("p (b c t) -> p b c t", b=HB, t=4), MULT)
+
+        def quantize_half(da, b, h):
+            cols = slice(h * HALF, (h + 1) * HALF)
+            nc.vector.quantize_mx(out=daq[b][0][:, cols].bitcast(E5), scales=daq[b][1][:, cols], in_=da)
 
         offs_t = keep.tile([P, E * C // 16], U16, name="offs_t")
         nc.sync.dma_start(offs_t[:], offs)
@@ -187,13 +219,13 @@ def tile_moe_bdx_mlp_relu_kernel(tc, dyT, a, w2, w1, gate, offs, out):
         w1r00.append(load_w1(0, 1, 0, KC, 119))
         w2r10 = load_w2(1, 0)
         w1r01 = [load_w1(0, b, KC, 2 * KC, 76 + 4 * b) for b in range(HB)]
-        a10 = load("araw10", a_planes(1, 0))
-        w2r11 = load_w2(1, 1, 111)
+        first = [load("afirst10", a_planes(1, 0)[:, :, 0:HALF])]
         w1r02 = [load_w1(0, b, 2 * KC, K) for b in range(HB)]
-        a11 = [load("apair11%d" % t, a_planes(1, 1)[:, t:t + 2, :], 68 + 2 * t) for t in (0, 2)]
-        w1r1b0 = load_w1(1, 0, 0, K, 91)
-        w1r10 = [w1r1b0[:, :, 0:KC], load_w1(1, 1, 0, KC, 86)]
-        w1r1 = [w1r1b0[:, :, KC:K], load_w1(1, 1, KC, K, 103)]
+        w2r11 = load_w2(1, 1, 111)
+        first.append(load("afirst11", a_planes(1, 1)[:, :, 0:HALF], 68))
+        w1r10 = [load_w1(1, 0, 0, 2 * KC, 92), load_w1(1, 1, 0, 2 * KC, 84)]
+        second = [load("asecond10", a_planes(1, 0)[:, :, HALF:C]), load("asecond11", a_planes(1, 1)[:, :, HALF:C], 72)]
+        w1r11 = [load_w1(1, b, 2 * KC, K, 100 + 4 * b) for b in range(HB)]
 
         g0 = at(40, [4 * C], F32, "g0")
         shared = at(26, [6 * C], F32, "g1")
@@ -235,66 +267,84 @@ def tile_moe_bdx_mlp_relu_kernel(tc, dyT, a, w2, w1, gate, offs, out):
         for t in range(4):
             da_plane(da01_planes, t, w2q01, gq0, a01[:, t, :])
         w1q000 = quantize(w1g000[:], E4, "w1q000", scales_kb=17.5)
-        daq0 = [quantize(dag00[:], E5, "da00")]
+        daq = [quantize(dag00[:], E5, "da00")]
         dag01 = grouped_at(13.5, "dag01")
         interleave_split(dag01[:], planes(da01_planes[:]), on_vector, DA01_ON_VECTOR, on_scalar)
         w1q001 = quantize(w1g001[:], E4, "w1q001")
-        daq0.append(quantize(dag01[:], E5, "da01"))
+        daq.append(quantize(dag01[:], E5, "da01"))
         gq1 = quantize(ggrp1[:], E5, "g1", scales_kb=63)
-        staged = [dx_tile([w1q000 + (c0,), w1q001 + (c0,)], daq0, order=order) for c0, order in ((0, (0, 1)), (P, (1, 0)))]
+        staged = [dx_tile([w1q000 + (c0,), w1q001 + (c0,)], daq, order=order) for c0, order in ((0, (0, 1)), (P, (1, 0)))]
 
         w2g10 = grouped_at(119, "w2g10")
         group_w2(w2g10[:], w2r10)
         w2q10 = quantize(w2g10[:], E4, "w2q10", codes_kb=38)
         scatter_first(48, staged[0])
         w1g01 = grouped_at(119, "w1g01")
-        group_w1(w1g01[:], w1r01, (on_gpsimd, on_scalar))
-        dh10_planes = grouped_at(52, "plain10")
+        on_gpsimd(words(w1g01[:])[:, 0:KC, :], w1r01[0][:])
+        on_gpsimd(words(w1g01[:])[:, KC:KC + P, :], w1r01[1][:, :, 0:P])
+        on_scalar(words(w1g01[:])[:, KC + P:2 * KC, :], w1r01[1][:, :, P:KC])
+        banks = [dh_plane(w2q10, gq1, t) for t in range(4)]
+        dh = grouped_at(52, "dh_planes", HB * C)
+        dh_planes = dh[:].rearrange("p (b t c) -> p b t c", b=HB, t=4)
         for t in range(4):
-            nc.scalar.copy(out=dh10_planes[:, t * C:(t + 1) * C], in_=dh_plane(w2q10, gq1, t)[:])
+            nc.scalar.copy(out=dh_planes[:, 0, t, :], in_=banks[t][:])
         w1q01 = quantize(w1g01[:], E4, "w1q01", codes_kb=43, scales_kb=13.75)
 
         scatter_first(78, staged[1])
-        staged = dx_pair(w1q01, daq0)
-        scatter_first(64, staged[0])
-        sign0 = sign_half(0, 39)
-        w2g11 = grouped_at(10, "w2g11")
-        group_w2(w2g11[:], w2r11)
-        mask = grouped_at(14, "mask")
-        nc.scalar.activation(out=mask[:, 0:4 * HALF], in_=sign0[:], func=ACT.Relu)
-        sign1 = sign_half(1, 44)
-        nc.scalar.activation(out=mask[:, 4 * HALF:4 * C], in_=sign1[:], func=ACT.Relu)
         w1g02 = grouped_at(119, "w1g02")
         group_w1(w1g02[:], w1r02, (on_gpsimd, on_gpsimd))
+        sign = grouped_at(39, "sign100", HALF)
+        sign_into(sign[:], first[0][:])
+        staged = [dx_tile(chunk_parts(w1q01, 0), daq)]
+        scatter_first(64, staged[0])
+        dag100 = product(0, mask_of(sign, 14, "100"), 8, "100")
+        staged.append(dx_tile(chunk_parts(w1q01, P), daq))
+        w2g11 = grouped_at(10, "w2g11")
+        group_w2(w2g11[:], w2r11)
         w1q02 = quantize(w1g02[:], E4, "w1q02", codes_kb=111)
         w2q11 = quantize(w2g11[:], E4, "w2q11")
 
         scatter_first(119, staged[1])
-        staged = dx_pair(w1q02, daq0)
-        dag10 = grouped_at(10, "dag10")
-        for h in range(2):
-            half = slice(h * HALF, (h + 1) * HALF)
-            nc.gpsimd.tensor_tensor(words(dag10[:])[:, half, :], planes(dh10_planes[:])[:, :, half].rearrange("p t c -> p c t"),
-                                    words(mask[:])[:, half, :], MULT)
-        da11_planes = grouped_at(4, "plain11")
-        for t in range(4):
-            da_plane(da11_planes, t, w2q11, gq1, a11[t // 2][:, t % 2, :])
-        scatter_first(68, staged[0])
-        w1g10 = grouped_at(112, "w1g10")
-        group_w1(w1g10[:], w1r10, (on_scalar, on_scalar))
-        dag11 = grouped_at(86, "dag11")
-        on_scalar(words(dag11[:]), planes(da11_planes[:]))
-        w1q1 = [quantize(w1g10[:], E4, "w1q10", codes_kb=53, scales_kb=72)]
-        daq1 = [quantize(dag10[:], E5, "da10", scales_kb=73), quantize(dag11[:], E5, "da11")]
+        sign = grouped_at(44, "sign110", HALF)
+        sign_into(sign[:], first[1][:])
+        mask110 = mask_of(sign, 82, "110")
+        w1g10 = grouped_at(10, "w1g10", 2 * C)
+        on_gpsimd(words(w1g10[:])[:, 0:C, :], w1r10[0][:])
+        banks = [dh_plane(w2q11, gq1, t) for t in range(4)]
+        round_dh11(banks, 0)
+        dag110 = product(1, mask110, 0, "110")
+        scatter_first(60, dx_tile(chunk_parts(w1q02, 0), daq))
+        round_dh11(banks, 1)
+        on_scalar(words(w1g10[:])[:, C:2 * C, :], w1r10[1][:])
+        staged = dx_tile(chunk_parts(w1q02, P), daq, tag="dh")
+        signs = [grouped_at(87 + 2 * q, "sign_quarter%d" % q, HALF) for q in range(2)]
+        for q, b in ((0, 0), (0, 1), (1, 0)):
+            quarter_sign(signs[q], q, b)
+        quantize_half(dag100[:], 0, 0)
+        w1q10 = [quantize(w1g10[:, 0:4 * C], E4, "w1q100", scales_kb=82)]
+        quantize_half(dag110[:], 1, 0)
+        w1q10.append(quantize(w1g10[:, 4 * C:8 * C], E4, "w1q101", scales_kb=82.5))
 
-        scatter_first(2, staged[1])
-        w1g11 = grouped_at(6, "w1g11")
-        group_w1(w1g11[:], w1r1, (on_scalar, on_scalar), 0)
-        w1q1.append(quantize(w1g11[:], E4, "w1q11", scales_kb=86))
-        w1g12 = grouped_at(87, "w1g12")
-        group_w1(w1g12[:], w1r1, (on_gpsimd, on_scalar), KC)
-        w1q1.append(quantize(w1g12[:], E4, "w1q12", scales_kb=86.5))
+        scatter_first(83, staged)
+        dag_second = grouped_at(10, "dag_second")
+        quarter_product(0, mask_of(signs[0], 18, "quarter0"))
+        banks = [dx_bank([q + (kt * P,) for q in w1q10], daq) for kt in range(4)]
+        scatter_half(0, 1, 0, stage_half(banks[0], 0))
+        quarter_sign(signs[1], 1, 1)
+        scatter_half(1, 1, 0, stage_half(banks[1], 0))
+        quarter_product(1, mask_of(signs[1], 20, "quarter1"))
+        scatter_half(2, 1, 0, stage_half(banks[2], 0))
+        w1g11 = grouped_at(89, "w1g11")
+        group_w1(w1g11[:], w1r11, (on_scalar, on_scalar))
+        for b in range(HB):
+            quantize_half(dag_second[:, b * 4 * HALF:(b + 1) * 4 * HALF], b, 1)
+        w1q11 = quantize(w1g11[:], E4, "w1q11", scales_kb=54)
 
-        for kt in range(KT):
-            kb = 103 + 2 * kt if kt < 4 else 91 + 2 * (kt - 4)
-            scatter_last(kt, dx_tile(chunk_parts(w1q1[kt // 2], (kt % 2) * P), daq1, kb))
+        scatter_half(3, 1, 0, stage_half(banks[3], 0, 20))
+        for kt in range(4):
+            scatter_half(kt, 1, 1, stage_half(dx_bank([q + (kt * P,) for q in w1q10], daq), 1))
+            store(kt)
+        for kt in range(4, KT):
+            staged = dx_tile(chunk_parts(w1q11, (kt - 4) * P), daq)
+            nc.vector.tensor_copy(out=windows[kt][:].indirect(slots_of(1)), in_=staged[:])
+            store(kt)

@@ -28,10 +28,9 @@ KC = 2 * P
 HALF = C // 2
 KB = 1024
 
-G0_ON_VECTOR = 192
 G1_ON_GPSIMD = 256
-DA00_ON_GPSIMD = 192
-DA01_ON_VECTOR = 448
+W1_ON_GPSIMD = 160
+DA01_ON_SCALAR = 192
 
 
 def tile_moe_bdx_mlp_relu_kernel(tc, dyT, a, w2, w1, gate, offs, out):
@@ -115,8 +114,8 @@ def tile_moe_bdx_mlp_relu_kernel(tc, dyT, a, w2, w1, gate, offs, out):
         def slots_of(e, s0=0, s1=C):
             return offs_t[:, (e * C + s0) // 16:(e * C + s1) // 16]
 
-        def gather(e, t, dst, gate_ap):
-            nc.vector.tensor_tensor(dst[:, t * C:(t + 1) * C], dy[t][:].indirect(slots_of(e)), gate_ap, MULT)
+        def gather(e, t, dst, gate_ap, s0=0, s1=C):
+            nc.vector.tensor_tensor(dst[:, t * C + s0:t * C + s1], dy[t][:].indirect(slots_of(e, s0, s1)), gate_ap[:, s0:s1], MULT)
 
         def copy_gate(dst, bank):
             nc.scalar.copy(out=dst.rearrange("p (n m) -> p n m", m=4), in_=bank[:].rearrange("p (m n) -> p n m", m=4))
@@ -128,9 +127,11 @@ def tile_moe_bdx_mlp_relu_kernel(tc, dyT, a, w2, w1, gate, offs, out):
                                 rhs=gq[0][:].bitcast(E5), rhs_scale=gq[1][:], start=True, stop=True)
             return bank
 
-        def da_plane(dst, t, w2q, gq, a_plane):
-            bank = dh_plane(w2q, gq, t)
-            nc.vector.scalar_tensor_tensor(out=dst[:, t * C:(t + 1) * C], in0=a_plane, scalar=0.0, in1=bank[:], op0=IS_GT, op1=MULT)
+        def da_block(dst, w2q, gq, a_pairs):
+            banks = [dh_plane(w2q, gq, t) for t in range(4)]
+            for t, s0, s1 in [(0, 0, C), (1, 0, C)] + [(t, s0, s0 + HALF) for s0 in (0, HALF) for t in (2, 3)]:
+                nc.vector.scalar_tensor_tensor(out=dst[:, t * C + s0:t * C + s1], in0=a_pairs[t // 2][:, t % 2, s0:s1], scalar=0.0,
+                                               in1=banks[t][:, s0:s1], op0=IS_GT, op1=MULT)
 
         def dx_bank(parts, daq, order=(0, 1), tag="dx"):
             bank = psum.tile([P, C], F32, name=tag)
@@ -200,11 +201,13 @@ def tile_moe_bdx_mlp_relu_kernel(tc, dyT, a, w2, w1, gate, offs, out):
 
         offs_t = keep.tile([P, E * C // 16], U16, name="offs_t")
         nc.sync.dma_start(offs_t[:], offs)
-        ident = at(26, [P], F32, "ident")
+        ident = at(27, [P], F32, "ident")
         make_identity(nc, ident[:])
-        gate_row = load("gate_row1", gate[1, C:2 * C].rearrange("(n m) -> n m", m=4))
         dy = {1: load_dy(1)}
-        gate0 = load("gate0", gate[0:P, 0:C])
+        g_planes = at(28, [7 * C], F32, "g_planes")
+        gate0 = g_planes[:, 0:C]
+        nc.sync.dma_start(out=gate0, in_=gate[0:P, 0:C])
+        gate_row = load("gate_row1", gate[1, C:2 * C].rearrange("(n m) -> n m", m=4))
         dy[2] = load_dy(2)
         gate_bank = psum.tile([P, C], F32, name="dh")
         for m in range(4):
@@ -213,9 +216,9 @@ def tile_moe_bdx_mlp_relu_kernel(tc, dyT, a, w2, w1, gate, offs, out):
         dy[0] = load_dy(0)
         dy[3] = load_dy(3)
         w2r01 = load_w2(0, 1)
-        a00 = load("araw00", a_planes(0, 0))
+        a00 = [load("apair00%d" % t, a_planes(0, 0)[:, t:t + 2, :]) for t in (0, 2)]
         w1r00 = [load_w1(0, 0, 0, KC)]
-        a01 = load("araw01", a_planes(0, 1))
+        a01 = [load("apair01%d" % t, a_planes(0, 1)[:, t:t + 2, :]) for t in (0, 2)]
         w1r00.append(load_w1(0, 1, 0, KC, 119))
         w2r10 = load_w2(1, 0)
         w1r01 = [load_w1(0, b, KC, 2 * KC, 76 + 4 * b) for b in range(HB)]
@@ -223,57 +226,60 @@ def tile_moe_bdx_mlp_relu_kernel(tc, dyT, a, w2, w1, gate, offs, out):
         w1r02 = [load_w1(0, b, 2 * KC, K) for b in range(HB)]
         w2r11 = load_w2(1, 1, 111)
         first.append(load("afirst11", a_planes(1, 1)[:, :, 0:HALF], 68))
+        second = [load("asecond10", a_planes(1, 0)[:, :, HALF:C])]
         w1r10 = [load_w1(1, 0, 0, 2 * KC, 92), load_w1(1, 1, 0, 2 * KC, 84)]
-        second = [load("asecond10", a_planes(1, 0)[:, :, HALF:C]), load("asecond11", a_planes(1, 1)[:, :, HALF:C], 72)]
+        second.append(load("asecond11", a_planes(1, 1)[:, :, HALF:C], 72))
         w1r11 = [load_w1(1, b, 2 * KC, K, 100 + 4 * b) for b in range(HB)]
 
-        g0 = at(40, [4 * C], F32, "g0")
-        shared = at(26, [6 * C], F32, "g1")
-        g1 = shared[:, C:5 * C]
-        w2g00 = shared[:, 0:2 * C].bitcast(BF16)
-        ggrp0 = shared[:, 4 * C:6 * C].bitcast(BF16)
+        g1 = g_planes[:, 0:4 * C]
+        g0 = g_planes[:, 3 * C:7 * C]
         for t in (1, 2):
-            gather(0, t, g0, gate0[:])
+            gather(0, t, g0, gate0)
         for t, later in ((1, 0), (2, 3)):
             parked = g0[:, later * C:(later + 1) * C]
             copy_gate(parked, gate_bank)
             gather(1, t, g1, parked)
         gate1 = keep.tile([P, C], F32, name="gate1")
         copy_gate(gate1[:], gate_bank)
-        group_w2(w2g00, w2r00)
-        for t in (0, 3):
-            gather(0, t, g0, gate0[:])
-        w2q00 = quantize(w2g00, E4, "w2q00")
-        interleave_split(ggrp0, planes(g0[:]), on_scalar, C - G0_ON_VECTOR, on_vector)
+        w2g00 = grouped_at(24, "w2g00")
+        group_w2(w2g00[:], w2r00)
+        gather(0, 0, g0, gate0)
+        for s0 in (0, HALF):
+            gather(0, 3, g0, gate0, s0, s0 + HALF)
+        w2q00 = quantize(w2g00[:], E4, "w2q00")
+        ggrp0 = grouped_at(42, "ggrp0")
+        interleave_split(ggrp0[:], planes(g0), on_scalar, HALF, on_scalar)
         gather(1, 0, g1, gate1[:])
-        gq0 = quantize(ggrp0, E5, "g0")
+        gq0 = quantize(ggrp0[:], E5, "g0")
         gather(1, 3, g1, gate1[:])
 
         w2g01 = grouped_at(22, "w2g01")
         group_w2(w2g01[:], w2r01)
         da00_planes = grouped_at(16, "plain00")
         w2q01 = quantize(w2g01[:], E4, "w2q01")
-        for t in range(4):
-            da_plane(da00_planes, t, w2q00, gq0, a00[:, t, :])
-        w1g000 = grouped_at(52, "w1g000", KC)
-        on_scalar(words(w1g000[:]), w1r00[0][:])
+        da_block(da00_planes, w2q00, gq0, a00)
+        w1g00 = grouped_at(52, "w1g00")
+        by_tiles = w1g00[:].rearrange("p (u b c i t) -> p b u c t i", u=2, b=HB, i=4, t=4)
+
+        def cast_w1g00(b):
+            nc.scalar.copy(out=by_tiles[:, b, :, :, :, :], in_=w1r00[b][:].rearrange("p t (u c i) -> p u c t i", u=2, i=4))
+
+        cast_w1g00(0)
         ggrp1 = grouped_at(22, "ggrp1")
         interleave_split(ggrp1[:], planes(g1), on_gpsimd, G1_ON_GPSIMD, on_scalar)
         dag00 = grouped_at(48, "dag00")
-        interleave_split(dag00[:], planes(da00_planes[:]), on_scalar, C - DA00_ON_GPSIMD, on_gpsimd)
-        w1g001 = grouped_at(18, "w1g001", KC)
-        on_scalar(words(w1g001[:]), w1r00[1][:])
+        interleave_split(dag00[:], planes(da00_planes[:]), on_scalar, HALF, on_gpsimd)
+        cast_w1g00(1)
         da01_planes = grouped_at(60, "plain01")
-        for t in range(4):
-            da_plane(da01_planes, t, w2q01, gq0, a01[:, t, :])
-        w1q000 = quantize(w1g000[:], E4, "w1q000", scales_kb=17.5)
+        da_block(da01_planes, w2q01, gq0, a01)
         daq = [quantize(dag00[:], E5, "da00")]
         dag01 = grouped_at(13.5, "dag01")
-        interleave_split(dag01[:], planes(da01_planes[:]), on_vector, DA01_ON_VECTOR, on_scalar)
-        w1q001 = quantize(w1g001[:], E4, "w1q001")
+        interleave_split(dag01[:], planes(da01_planes[:]), on_scalar, DA01_ON_SCALAR, on_vector)
+        w1q00 = [quantize(w1g00[:, 0:2 * C], E4, "w1q000")]
         daq.append(quantize(dag01[:], E5, "da01"))
         gq1 = quantize(ggrp1[:], E5, "g1", scales_kb=63)
-        staged = [dx_tile([w1q000 + (c0,), w1q001 + (c0,)], daq, order=order) for c0, order in ((0, (0, 1)), (P, (1, 0)))]
+        w1q00.append(quantize(w1g00[:, 2 * C:4 * C], E4, "w1q001", scales_kb=62.5))
+        staged = [dx_tile([q + (b * P,) for b in range(HB)], daq) for q in w1q00]
 
         w2g10 = grouped_at(119, "w2g10")
         group_w2(w2g10[:], w2r10)
@@ -281,8 +287,8 @@ def tile_moe_bdx_mlp_relu_kernel(tc, dyT, a, w2, w1, gate, offs, out):
         scatter_first(48, staged[0])
         w1g01 = grouped_at(119, "w1g01")
         on_gpsimd(words(w1g01[:])[:, 0:KC, :], w1r01[0][:])
-        on_gpsimd(words(w1g01[:])[:, KC:KC + P, :], w1r01[1][:, :, 0:P])
-        on_scalar(words(w1g01[:])[:, KC + P:2 * KC, :], w1r01[1][:, :, P:KC])
+        on_gpsimd(words(w1g01[:])[:, KC:KC + W1_ON_GPSIMD, :], w1r01[1][:, :, 0:W1_ON_GPSIMD])
+        on_scalar(words(w1g01[:])[:, KC + W1_ON_GPSIMD:2 * KC, :], w1r01[1][:, :, W1_ON_GPSIMD:KC])
         banks = [dh_plane(w2q10, gq1, t) for t in range(4)]
         dh = grouped_at(52, "dh_planes", HB * C)
         dh_planes = dh[:].rearrange("p (b t c) -> p b t c", b=HB, t=4)
@@ -307,19 +313,22 @@ def tile_moe_bdx_mlp_relu_kernel(tc, dyT, a, w2, w1, gate, offs, out):
         scatter_first(119, staged[1])
         sign = grouped_at(44, "sign110", HALF)
         sign_into(sign[:], first[1][:])
+        signs = [grouped_at(46, "sign_quarter0", HALF)]
+        quarter_sign(signs[0], 0, 0)
         mask110 = mask_of(sign, 82, "110")
+        staged = dx_tile(chunk_parts(w1q02, 0), daq)
         w1g10 = grouped_at(10, "w1g10", 2 * C)
         on_gpsimd(words(w1g10[:])[:, 0:C, :], w1r10[0][:])
         banks = [dh_plane(w2q11, gq1, t) for t in range(4)]
         round_dh11(banks, 0)
         dag110 = product(1, mask110, 0, "110")
-        scatter_first(60, dx_tile(chunk_parts(w1q02, 0), daq))
+        scatter_first(60, staged)
         round_dh11(banks, 1)
         on_scalar(words(w1g10[:])[:, C:2 * C, :], w1r10[1][:])
         staged = dx_tile(chunk_parts(w1q02, P), daq, tag="dh")
-        signs = [grouped_at(87 + 2 * q, "sign_quarter%d" % q, HALF) for q in range(2)]
-        for q, b in ((0, 0), (0, 1), (1, 0)):
-            quarter_sign(signs[q], q, b)
+        signs.append(grouped_at(89, "sign_quarter1", HALF))
+        quarter_sign(signs[0], 0, 1)
+        quarter_sign(signs[1], 1, 0)
         quantize_half(dag100[:], 0, 0)
         w1q10 = [quantize(w1g10[:, 0:4 * C], E4, "w1q100", scales_kb=82)]
         quantize_half(dag110[:], 1, 0)
@@ -329,9 +338,9 @@ def tile_moe_bdx_mlp_relu_kernel(tc, dyT, a, w2, w1, gate, offs, out):
         dag_second = grouped_at(10, "dag_second")
         quarter_product(0, mask_of(signs[0], 18, "quarter0"))
         banks = [dx_bank([q + (kt * P,) for q in w1q10], daq) for kt in range(4)]
-        scatter_half(0, 1, 0, stage_half(banks[0], 0))
         quarter_sign(signs[1], 1, 1)
-        scatter_half(1, 1, 0, stage_half(banks[1], 0))
+        for kt in range(2):
+            scatter_half(kt, 1, 0, stage_half(banks[kt], 0))
         quarter_product(1, mask_of(signs[1], 20, "quarter1"))
         scatter_half(2, 1, 0, stage_half(banks[2], 0))
         w1g11 = grouped_at(89, "w1g11")

@@ -28,7 +28,7 @@ KC = 2 * P
 HALF = C // 2
 KB = 1024
 
-G1_ON_GPSIMD = 256
+G1_ON_GPSIMD = 192
 W1_ON_GPSIMD = 160
 DA01_ON_SCALAR = 192
 
@@ -120,15 +120,15 @@ def tile_moe_bdx_mlp_relu_kernel(tc, dyT, a, w2, w1, gate, offs, out):
         def copy_gate(dst, bank):
             nc.scalar.copy(out=dst.rearrange("p (n m) -> p n m", m=4), in_=bank[:].rearrange("p (m n) -> p n m", m=4))
 
-        def dh_plane(w2q, gq, t):
-            bank = psum.tile([P, C], F32, name="dh")
+        def dh_plane(w2q, gq, t, tag="dh"):
+            bank = psum.tile([P, C], F32, name=tag)
             cols = slice(t * P, (t + 1) * P)
             nc.tensor.matmul_mx(out=bank[:], lhsT=w2q[0][:, cols].bitcast(E4), lhsT_scale=w2q[1][:, cols],
                                 rhs=gq[0][:].bitcast(E5), rhs_scale=gq[1][:], start=True, stop=True)
             return bank
 
-        def da_block(dst, w2q, gq, a_pairs):
-            banks = [dh_plane(w2q, gq, t) for t in range(4)]
+        def da_block(dst, w2q, gq, a_pairs, tag):
+            banks = [dh_plane(w2q, gq, t, tag) for t in range(4)]
             for t, s0, s1 in [(0, 0, C), (1, 0, C)] + [(t, s0, s0 + HALF) for s0 in (0, HALF) for t in (2, 3)]:
                 nc.vector.scalar_tensor_tensor(out=dst[:, t * C + s0:t * C + s1], in0=a_pairs[t // 2][:, t % 2, s0:s1], scalar=0.0,
                                                in1=banks[t][:, s0:s1], op0=IS_GT, op1=MULT)
@@ -215,7 +215,9 @@ def tile_moe_bdx_mlp_relu_kernel(tc, dyT, a, w2, w1, gate, offs, out):
         w2r00 = load_w2(0, 0)
         dy[0] = load_dy(0)
         dy[3] = load_dy(3)
-        w2r01 = load_w2(0, 1)
+        w2r01_da00 = keep.tile([P, 4 * C + HALF], F32, name="w2r01_da00")
+        w2r01 = planes(w2r01_da00[:, HALF:HALF + 4 * C])
+        nc.sync.dma_start(out=w2r01, in_=by_planes(w2[0, :, PASS:2 * PASS]))
         a00 = [load("apair00%d" % t, a_planes(0, 0)[:, t:t + 2, :]) for t in (0, 2)]
         w1r00 = [load_w1(0, 0, 0, KC)]
         a01 = [load("apair01%d" % t, a_planes(0, 1)[:, t:t + 2, :]) for t in (0, 2)]
@@ -227,8 +229,9 @@ def tile_moe_bdx_mlp_relu_kernel(tc, dyT, a, w2, w1, gate, offs, out):
         w2r11 = load_w2(1, 1, 111)
         first.append(load("afirst11", a_planes(1, 1)[:, :, 0:HALF], 68))
         second = [load("asecond10", a_planes(1, 0)[:, :, HALF:C])]
-        w1r10 = [load_w1(1, 0, 0, 2 * KC, 92), load_w1(1, 1, 0, 2 * KC, 84)]
+        w1r10 = [load_w1(1, 0, 0, 2 * KC, 92)]
         second.append(load("asecond11", a_planes(1, 1)[:, :, HALF:C], 72))
+        w1r10.append(load_w1(1, 1, 0, 2 * KC, 84))
         w1r11 = [load_w1(1, b, 2 * KC, K, 100 + 4 * b) for b in range(HB)]
 
         g1 = g_planes[:, 0:4 * C]
@@ -253,11 +256,13 @@ def tile_moe_bdx_mlp_relu_kernel(tc, dyT, a, w2, w1, gate, offs, out):
         gq0 = quantize(ggrp0[:], E5, "g0")
         gather(1, 3, g1, gate1[:])
 
-        w2g01 = grouped_at(22, "w2g01")
-        group_w2(w2g01[:], w2r01)
-        da00_planes = grouped_at(16, "plain00")
-        w2q01 = quantize(w2g01[:], E4, "w2q01")
-        da_block(da00_planes, w2q00, gq0, a00)
+        both = grouped_at(20, "w2g01_ggrp1", 2 * C - G1_ON_GPSIMD)
+        w2g01 = both[:, 0:4 * C]
+        ggrp1 = both[:, 4 * (C - G1_ON_GPSIMD):4 * (2 * C - G1_ON_GPSIMD)]
+        group_w2(w2g01, w2r01)
+        da00_planes = w2r01_da00[:, 0:2 * C].bitcast(BF16)
+        w2q01 = quantize(w2g01, E4, "w2q01")
+        da_block(da00_planes, w2q00, gq0, a00, "dh")
         w1g00 = grouped_at(52, "w1g00")
         by_tiles = w1g00[:].rearrange("p (u b c i t) -> p b u c t i", u=2, b=HB, i=4, t=4)
 
@@ -265,48 +270,50 @@ def tile_moe_bdx_mlp_relu_kernel(tc, dyT, a, w2, w1, gate, offs, out):
             nc.scalar.copy(out=by_tiles[:, b, :, :, :, :], in_=w1r00[b][:].rearrange("p t (u c i) -> p u c t i", u=2, i=4))
 
         cast_w1g00(0)
-        ggrp1 = grouped_at(22, "ggrp1")
-        interleave_split(ggrp1[:], planes(g1), on_gpsimd, G1_ON_GPSIMD, on_scalar)
+        interleave_split(ggrp1, planes(g1), on_gpsimd, G1_ON_GPSIMD, on_scalar)
         dag00 = grouped_at(48, "dag00")
-        interleave_split(dag00[:], planes(da00_planes[:]), on_scalar, HALF, on_gpsimd)
+        interleave_split(dag00[:], planes(da00_planes), on_scalar, HALF, on_gpsimd)
         cast_w1g00(1)
         da01_planes = grouped_at(60, "plain01")
-        da_block(da01_planes, w2q01, gq0, a01)
+        da_block(da01_planes, w2q01, gq0, a01, "dx")
         daq = [quantize(dag00[:], E5, "da00")]
         dag01 = grouped_at(13.5, "dag01")
         interleave_split(dag01[:], planes(da01_planes[:]), on_scalar, DA01_ON_SCALAR, on_vector)
         w1q00 = [quantize(w1g00[:, 0:2 * C], E4, "w1q000")]
         daq.append(quantize(dag01[:], E5, "da01"))
-        gq1 = quantize(ggrp1[:], E5, "g1", scales_kb=63)
+        gq1 = quantize(ggrp1, E5, "g1", scales_kb=63)
         w1q00.append(quantize(w1g00[:, 2 * C:4 * C], E4, "w1q001", scales_kb=62.5))
-        staged = [dx_tile([q + (b * P,) for b in range(HB)], daq) for q in w1q00]
+        staged = dx_tile([w1q00[0] + (b * P,) for b in range(HB)], daq)
 
         w2g10 = grouped_at(119, "w2g10")
         group_w2(w2g10[:], w2r10)
         w2q10 = quantize(w2g10[:], E4, "w2q10", codes_kb=38)
-        scatter_first(48, staged[0])
+        scatter_first(48, staged)
         w1g01 = grouped_at(119, "w1g01")
         on_gpsimd(words(w1g01[:])[:, 0:KC, :], w1r01[0][:])
         on_gpsimd(words(w1g01[:])[:, KC:KC + W1_ON_GPSIMD, :], w1r01[1][:, :, 0:W1_ON_GPSIMD])
         on_scalar(words(w1g01[:])[:, KC + W1_ON_GPSIMD:2 * KC, :], w1r01[1][:, :, W1_ON_GPSIMD:KC])
+        staged = dx_tile([w1q00[1] + (b * P,) for b in range(HB)], daq)
+        sign = grouped_at(40, "sign100", HALF)
+        sign_into(sign[:], first[0][:])
         banks = [dh_plane(w2q10, gq1, t) for t in range(4)]
         dh = grouped_at(52, "dh_planes", HB * C)
         dh_planes = dh[:].rearrange("p (b t c) -> p b t c", b=HB, t=4)
         for t in range(4):
+            if t == 2:
+                mask100 = mask_of(sign, 16, "100")
             nc.scalar.copy(out=dh_planes[:, 0, t, :], in_=banks[t][:])
         w1q01 = quantize(w1g01[:], E4, "w1q01", codes_kb=43, scales_kb=13.75)
 
-        scatter_first(78, staged[1])
+        scatter_first(78, staged)
         w1g02 = grouped_at(119, "w1g02")
         group_w1(w1g02[:], w1r02, (on_gpsimd, on_gpsimd))
-        sign = grouped_at(39, "sign100", HALF)
-        sign_into(sign[:], first[0][:])
         staged = [dx_tile(chunk_parts(w1q01, 0), daq)]
         scatter_first(64, staged[0])
-        dag100 = product(0, mask_of(sign, 14, "100"), 8, "100")
-        staged.append(dx_tile(chunk_parts(w1q01, P), daq))
+        dag100 = product(0, mask100, 8, "100")
         w2g11 = grouped_at(10, "w2g11")
         group_w2(w2g11[:], w2r11)
+        staged.append(dx_tile(chunk_parts(w1q01, P), daq))
         w1q02 = quantize(w1g02[:], E4, "w1q02", codes_kb=111)
         w2q11 = quantize(w2g11[:], E4, "w2q11")
 
@@ -316,19 +323,21 @@ def tile_moe_bdx_mlp_relu_kernel(tc, dyT, a, w2, w1, gate, offs, out):
         signs = [grouped_at(46, "sign_quarter0", HALF)]
         quarter_sign(signs[0], 0, 0)
         mask110 = mask_of(sign, 82, "110")
+        quarter_sign(signs[0], 0, 1)
         staged = dx_tile(chunk_parts(w1q02, 0), daq)
         w1g10 = grouped_at(10, "w1g10", 2 * C)
         on_gpsimd(words(w1g10[:])[:, 0:C, :], w1r10[0][:])
         banks = [dh_plane(w2q11, gq1, t) for t in range(4)]
         round_dh11(banks, 0)
         dag110 = product(1, mask110, 0, "110")
-        scatter_first(60, staged)
+        scatter_first(4, staged)
         round_dh11(banks, 1)
         on_scalar(words(w1g10[:])[:, C:2 * C, :], w1r10[1][:])
         staged = dx_tile(chunk_parts(w1q02, P), daq, tag="dh")
+        mask_quarter0 = mask_of(signs[0], 87, "quarter0")
         signs.append(grouped_at(89, "sign_quarter1", HALF))
-        quarter_sign(signs[0], 0, 1)
-        quarter_sign(signs[1], 1, 0)
+        for b in range(HB):
+            quarter_sign(signs[1], 1, b)
         quantize_half(dag100[:], 0, 0)
         w1q10 = [quantize(w1g10[:, 0:4 * C], E4, "w1q100", scales_kb=82)]
         quantize_half(dag110[:], 1, 0)
@@ -336,9 +345,8 @@ def tile_moe_bdx_mlp_relu_kernel(tc, dyT, a, w2, w1, gate, offs, out):
 
         scatter_first(83, staged)
         dag_second = grouped_at(10, "dag_second")
-        quarter_product(0, mask_of(signs[0], 18, "quarter0"))
+        quarter_product(0, mask_quarter0)
         banks = [dx_bank([q + (kt * P,) for q in w1q10], daq) for kt in range(4)]
-        quarter_sign(signs[1], 1, 1)
         for kt in range(2):
             scatter_half(kt, 1, 0, stage_half(banks[kt], 0))
         quarter_product(1, mask_of(signs[1], 20, "quarter1"))

@@ -28,9 +28,9 @@ KC = 2 * P
 HALF = C // 2
 KB = 1024
 
-G1_ON_GPSIMD = 192
-W1_ON_GPSIMD = 160
-DA01_ON_SCALAR = 192
+G1_ON_GPSIMD = 256
+W1_FIRST_ON_GPSIMD = 192
+W1_LAST_ON_GPSIMD = 144
 
 
 def tile_moe_bdx_mlp_relu_kernel(tc, dyT, a, w2, w1, gate, offs, out):
@@ -70,8 +70,9 @@ def tile_moe_bdx_mlp_relu_kernel(tc, dyT, a, w2, w1, gate, offs, out):
             first(words(dst)[:, 0:width, :], src[:, :, 0:width])
             second(words(dst)[:, width:C, :], src[:, :, width:C])
 
-        def group_w2(dst, raw):
-            nc.scalar.copy(out=dst.rearrange("p (t m j) -> p m j t", t=4, j=4), in_=raw[:].rearrange("p j (m t) -> p m j t", t=4))
+        def group_w2(dst, raw, t0=0, t1=4):
+            nc.scalar.copy(out=dst.rearrange("p (t m j) -> p m j t", t=4, j=4)[:, :, :, t0:t1],
+                           in_=raw[:].rearrange("p j (m t) -> p m j t", t=4)[:, :, :, t0:t1])
 
         def group_w1(dst, raws, copies, c0=0):
             for b in range(HB):
@@ -127,11 +128,8 @@ def tile_moe_bdx_mlp_relu_kernel(tc, dyT, a, w2, w1, gate, offs, out):
                                 rhs=gq[0][:].bitcast(E5), rhs_scale=gq[1][:], start=True, stop=True)
             return bank
 
-        def da_block(dst, w2q, gq, a_pairs, tag):
-            banks = [dh_plane(w2q, gq, t, tag) for t in range(4)]
-            for t, s0, s1 in [(0, 0, C), (1, 0, C)] + [(t, s0, s0 + HALF) for s0 in (0, HALF) for t in (2, 3)]:
-                nc.vector.scalar_tensor_tensor(out=dst[:, t * C + s0:t * C + s1], in0=a_pairs[t // 2][:, t % 2, s0:s1], scalar=0.0,
-                                               in1=banks[t][:, s0:s1], op0=IS_GT, op1=MULT)
+        def relu_product(dst, a_pairs, banks, t, s0, s1):
+            nc.vector.scalar_tensor_tensor(out=dst, in0=a_pairs[t // 2][:, t % 2, s0:s1], scalar=0.0, in1=banks[t][:, s0:s1], op0=IS_GT, op1=MULT)
 
         def dx_bank(parts, daq, order=(0, 1), tag="dx"):
             bank = psum.tile([P, C], F32, name=tag)
@@ -221,9 +219,11 @@ def tile_moe_bdx_mlp_relu_kernel(tc, dyT, a, w2, w1, gate, offs, out):
         a00 = [load("apair00%d" % t, a_planes(0, 0)[:, t:t + 2, :]) for t in (0, 2)]
         w1r00 = [load_w1(0, 0, 0, KC)]
         a01 = [load("apair01%d" % t, a_planes(0, 1)[:, t:t + 2, :]) for t in (0, 2)]
-        w1r00.append(load_w1(0, 1, 0, KC, 119))
+        w1r00.append(load_w1(0, 1, 0, KC))
         w2r10 = load_w2(1, 0)
-        w1r01 = [load_w1(0, b, KC, 2 * KC, 76 + 4 * b) for b in range(HB)]
+        w1r01 = at(76, [HB, 4, KC], F32, "w1raw0_256")
+        for b in range(HB):
+            nc.sync.dma_start(out=w1r01[:, b, :, :], in_=by_planes(w1[0, b * PASS:(b + 1) * PASS, KC:2 * KC]))
         first = [load("afirst10", a_planes(1, 0)[:, :, 0:HALF])]
         w1r02 = [load_w1(0, b, 2 * KC, K) for b in range(HB)]
         w2r11 = load_w2(1, 1, 111)
@@ -256,60 +256,85 @@ def tile_moe_bdx_mlp_relu_kernel(tc, dyT, a, w2, w1, gate, offs, out):
         gq0 = quantize(ggrp0[:], E5, "g0")
         gather(1, 3, g1, gate1[:])
 
-        both = grouped_at(20, "w2g01_ggrp1", 2 * C - G1_ON_GPSIMD)
-        w2g01 = both[:, 0:4 * C]
-        ggrp1 = both[:, 4 * (C - G1_ON_GPSIMD):4 * (2 * C - G1_ON_GPSIMD)]
+        w1g01_at = HALF - 16
+        w2g10_at = w1g01_at + C - W1_LAST_ON_GPSIMD
+        chain = grouped_at(119, "chain", w2g10_at + HALF + C)
+
+        def link(start, columns=C):
+            return chain[:, 4 * start:4 * (start + columns)]
+
+        da010 = link(P, HALF)
+        dag011 = link(0, HALF)
+        w1g001 = link(HALF, KC)
+        w1g01 = link(w1g01_at)
+        w2g10 = link(w2g10_at)
+        ggrp1 = link(w2g10_at + HALF)
+        w2g01 = link(w2g10_at + HALF + G1_ON_GPSIMD - C)
         group_w2(w2g01, w2r01)
         da00_planes = w2r01_da00[:, 0:2 * C].bitcast(BF16)
         w2q01 = quantize(w2g01, E4, "w2q01")
-        da_block(da00_planes, w2q00, gq0, a00, "dh")
-        w1g00 = grouped_at(52, "w1g00")
-        by_tiles = w1g00[:].rearrange("p (u b c i t) -> p b u c t i", u=2, b=HB, i=4, t=4)
+        banks = [dh_plane(w2q00, gq0, t) for t in range(4)]
+        for t, s0, s1 in [(0, 0, C), (1, 0, C)] + [(t, s0, s0 + HALF) for s0 in (0, HALF) for t in (2, 3)]:
+            relu_product(da00_planes[:, t * C + s0:t * C + s1], a00, banks, t, s0, s1)
+        w1g000 = grouped_at(52, "w1g000", KC)
 
-        def cast_w1g00(b):
-            nc.scalar.copy(out=by_tiles[:, b, :, :, :, :], in_=w1r00[b][:].rearrange("p t (u c i) -> p u c t i", u=2, i=4))
+        def cast_first(dst, u, b):
+            on_scalar(words(dst)[:, (1 - b) * P:(2 - b) * P, :], w1r00[b][:, :, u * P:(u + 1) * P])
 
-        cast_w1g00(0)
+        cast_first(w1g000[:], 0, 0)
+        cast_first(w1g001, 1, 0)
         interleave_split(ggrp1, planes(g1), on_gpsimd, G1_ON_GPSIMD, on_scalar)
         dag00 = grouped_at(48, "dag00")
         interleave_split(dag00[:], planes(da00_planes), on_scalar, HALF, on_gpsimd)
-        cast_w1g00(1)
-        da01_planes = grouped_at(60, "plain01")
-        da_block(da01_planes, w2q01, gq0, a01, "dx")
-        daq = [quantize(dag00[:], E5, "da00")]
-        dag01 = grouped_at(13.5, "dag01")
-        interleave_split(dag01[:], planes(da01_planes[:]), on_scalar, DA01_ON_SCALAR, on_vector)
-        w1q00 = [quantize(w1g00[:, 0:2 * C], E4, "w1q000")]
-        daq.append(quantize(dag01[:], E5, "da01"))
-        gq1 = quantize(ggrp1, E5, "g1", scales_kb=63)
-        w1q00.append(quantize(w1g00[:, 2 * C:4 * C], E4, "w1q001", scales_kb=62.5))
-        staged = dx_tile([w1q00[0] + (b * P,) for b in range(HB)], daq)
+        cast_first(w1g000[:], 0, 1)
+        da01 = [da010, grouped_at(60, "da011", HALF)[:]]
+        banks = [dh_plane(w2q01, gq0, t, "dx") for t in range(4)]
+        pieces = [(0, 0), (0, 1)] + [(t, h) for h in range(2) for t in (1, 2, 3)]
+        for t, h in pieces[:-1]:
+            relu_product(planes(da01[h])[:, t, :], a01, banks, t, h * HALF, (h + 1) * HALF)
+        w1q00 = [quantize(w1g000[:], E4, "w1q000")]
+        da00 = quantize(dag00[:], E5, "da00")
+        relu_product(planes(da01[1])[:, 3, :], a01, banks, 3, HALF, C)
+        daq = [da00, gq0]
+        dag010 = grouped_at(2, "dag010", HALF)
+        on_scalar(words(dag010[:]), planes(da01[0]))
+        quantize_half(dag010[:], 1, 0)
+        first_parts = [w1q00[0] + ((1 - b) * P,) for b in range(HB)]
+        first_bank = dx_bank(first_parts, daq)
+        on_vector(words(dag011), planes(da01[1]))
+        group_w2(w2g10, w2r10, 0, 2)
+        cast_first(w1g001, 1, 1)
+        gq1 = quantize(ggrp1, E5, "g1", scales_kb=2)
+        quantize_half(dag011, 1, 1)
+        w1q00.append(quantize(w1g001, E4, "w1q001"))
 
-        w2g10 = grouped_at(119, "w2g10")
-        group_w2(w2g10[:], w2r10)
-        w2q10 = quantize(w2g10[:], E4, "w2q10", codes_kb=38)
-        scatter_first(48, staged)
-        w1g01 = grouped_at(119, "w1g01")
-        on_gpsimd(words(w1g01[:])[:, 0:KC, :], w1r01[0][:])
-        on_gpsimd(words(w1g01[:])[:, KC:KC + W1_ON_GPSIMD, :], w1r01[1][:, :, 0:W1_ON_GPSIMD])
-        on_scalar(words(w1g01[:])[:, KC + W1_ON_GPSIMD:2 * KC, :], w1r01[1][:, :, W1_ON_GPSIMD:KC])
-        staged = dx_tile([w1q00[1] + (b * P,) for b in range(HB)], daq)
+        windows.append(at(48, [T], F32, "window0"))
+        scatter_half(0, 0, 0, stage_half(first_bank, 0))
+        on_gpsimd(words(w1g01)[:, 0:W1_FIRST_ON_GPSIMD, :], w1r01[:, 0, :, 0:W1_FIRST_ON_GPSIMD])
+        group_w2(w2g10, w2r10, 2, 4)
+        w2q10 = quantize(w2g10, E4, "w2q10")
+        scatter_half(0, 0, 1, stage_half(dx_bank(first_parts, daq, order=(1, 0)), 1))
+        on_gpsimd(words(w1g01)[:, C - W1_LAST_ON_GPSIMD:C, :], w1r01[:, 1, :, KC - W1_LAST_ON_GPSIMD:KC])
+        on_scalar(words(w1g01)[:, W1_FIRST_ON_GPSIMD:KC, :], w1r01[:, 0, :, W1_FIRST_ON_GPSIMD:KC])
+        on_scalar(words(w1g01)[:, KC:C - W1_LAST_ON_GPSIMD, :], w1r01[:, 1, :, 0:KC - W1_LAST_ON_GPSIMD])
+        staged = dx_tile([w1q00[1] + ((1 - b) * P,) for b in range(HB)], daq)
         sign = grouped_at(40, "sign100", HALF)
         sign_into(sign[:], first[0][:])
         banks = [dh_plane(w2q10, gq1, t) for t in range(4)]
         dh = grouped_at(52, "dh_planes", HB * C)
         dh_planes = dh[:].rearrange("p (b t c) -> p b t c", b=HB, t=4)
-        for t in range(4):
+        for t in range(3):
             if t == 2:
                 mask100 = mask_of(sign, 16, "100")
             nc.scalar.copy(out=dh_planes[:, 0, t, :], in_=banks[t][:])
-        w1q01 = quantize(w1g01[:], E4, "w1q01", codes_kb=43, scales_kb=13.75)
+        w1q01 = quantize(w1g01, E4, "w1q01", codes_kb=43, scales_kb=13.75)
 
         scatter_first(78, staged)
         w1g02 = grouped_at(119, "w1g02")
         group_w1(w1g02[:], w1r02, (on_gpsimd, on_gpsimd))
         staged = [dx_tile(chunk_parts(w1q01, 0), daq)]
         scatter_first(64, staged[0])
+        nc.scalar.copy(out=dh_planes[:, 0, 3, :], in_=banks[3][:])
         dag100 = product(0, mask100, 8, "100")
         w2g11 = grouped_at(10, "w2g11")
         group_w2(w2g11[:], w2r11)
@@ -323,7 +348,6 @@ def tile_moe_bdx_mlp_relu_kernel(tc, dyT, a, w2, w1, gate, offs, out):
         signs = [grouped_at(46, "sign_quarter0", HALF)]
         quarter_sign(signs[0], 0, 0)
         mask110 = mask_of(sign, 82, "110")
-        quarter_sign(signs[0], 0, 1)
         staged = dx_tile(chunk_parts(w1q02, 0), daq)
         w1g10 = grouped_at(10, "w1g10", 2 * C)
         on_gpsimd(words(w1g10[:])[:, 0:C, :], w1r10[0][:])
@@ -334,6 +358,7 @@ def tile_moe_bdx_mlp_relu_kernel(tc, dyT, a, w2, w1, gate, offs, out):
         round_dh11(banks, 1)
         on_scalar(words(w1g10[:])[:, C:2 * C, :], w1r10[1][:])
         staged = dx_tile(chunk_parts(w1q02, P), daq, tag="dh")
+        quarter_sign(signs[0], 0, 1)
         mask_quarter0 = mask_of(signs[0], 87, "quarter0")
         signs.append(grouped_at(89, "sign_quarter1", HALF))
         for b in range(HB):

@@ -74,9 +74,9 @@ def tile_moe_bdx_mlp_relu_kernel(tc, dyT, a, w2, w1, gate, offs, out):
             nc.scalar.copy(out=dst.rearrange("p (t m j) -> p m j t", t=4, j=4)[:, :, :, t0:t1],
                            in_=raw[:].rearrange("p j (m t) -> p m j t", t=4)[:, :, :, t0:t1])
 
-        def group_w1(dst, raws, copies, c0=0):
+        def group_w1(dst, raws, copy):
             for b in range(HB):
-                copies[b](words(dst)[:, b * KC:(b + 1) * KC, :], raws[b][:, :, c0:c0 + KC])
+                copy(words(dst)[:, b * KC:(b + 1) * KC, :], raws[b][:, :, 0:KC])
 
         def quantize(grouped, fmt, name, codes_kb=None, scales_kb=None):
             width = grouped.shape[1] // 4
@@ -140,9 +140,9 @@ def tile_moe_bdx_mlp_relu_kernel(tc, dyT, a, w2, w1, gate, offs, out):
                                     rhs=daq[b][0][:].bitcast(E5), rhs_scale=daq[b][1][:], start=(b == order[0]), stop=(b == order[1]))
             return bank
 
-        def dx_tile(parts, daq, order=(0, 1), tag="dx"):
+        def dx_tile(parts, daq, tag="dx"):
             staged = keep.tile([P, C], F32, name="staged", bufs=4)
-            nc.scalar.copy(out=staged[:], in_=dx_bank(parts, daq, order, tag)[:])
+            nc.scalar.copy(out=staged[:], in_=dx_bank(parts, daq, tag=tag)[:])
             return staged
 
         def stage_half(bank, h, kb=None):
@@ -197,11 +197,11 @@ def tile_moe_bdx_mlp_relu_kernel(tc, dyT, a, w2, w1, gate, offs, out):
             cols = slice(h * HALF, (h + 1) * HALF)
             nc.vector.quantize_mx(out=daq[b][0][:, cols].bitcast(E5), scales=daq[b][1][:, cols], in_=da)
 
-        offs_t = keep.tile([P, E * C // 16], U16, name="offs_t")
-        nc.sync.dma_start(offs_t[:], offs)
         ident = at(27, [P], F32, "ident")
         make_identity(nc, ident[:])
         dy = {1: load_dy(1)}
+        offs_t = keep.tile([P, E * C // 16], U16, name="offs_t")
+        nc.sync.dma_start(offs_t[:], offs)
         g_planes = at(28, [7 * C], F32, "g_planes")
         gate0 = g_planes[:, 0:C]
         nc.sync.dma_start(out=gate0, in_=gate[0:P, 0:C])
@@ -331,7 +331,7 @@ def tile_moe_bdx_mlp_relu_kernel(tc, dyT, a, w2, w1, gate, offs, out):
 
         scatter_first(78, staged)
         w1g02 = grouped_at(119, "w1g02")
-        group_w1(w1g02[:], w1r02, (on_gpsimd, on_gpsimd))
+        group_w1(w1g02[:], w1r02, on_gpsimd)
         staged = [dx_tile(chunk_parts(w1q01, 0), daq)]
         scatter_first(64, staged[0])
         nc.scalar.copy(out=dh_planes[:, 0, 3, :], in_=banks[3][:])
@@ -377,7 +377,7 @@ def tile_moe_bdx_mlp_relu_kernel(tc, dyT, a, w2, w1, gate, offs, out):
         quarter_product(1, mask_of(signs[1], 20, "quarter1"))
         scatter_half(2, 1, 0, stage_half(banks[2], 0))
         w1g11 = grouped_at(89, "w1g11")
-        group_w1(w1g11[:], w1r11, (on_scalar, on_scalar))
+        group_w1(w1g11[:], w1r11, on_scalar)
         for b in range(HB):
             quantize_half(dag_second[:, b * 4 * HALF:(b + 1) * 4 * HALF], b, 1)
         w1q11 = quantize(w1g11[:], E4, "w1q11", scales_kb=54)

@@ -10,6 +10,7 @@ BYTES = 4 * (N * T + H * E * C + E * N * H + E * H * K + E * C + K * T) + 2 * 12
 
 F32 = mybir.dt.float32
 BF16 = mybir.dt.bfloat16
+I32 = mybir.dt.int32
 U32 = mybir.dt.uint32
 U16 = mybir.dt.uint16
 U8 = mybir.dt.uint8
@@ -18,7 +19,7 @@ E5 = mybir.dt.float8_e5m2_x4
 MULT = mybir.AluOpType.mult
 ADD = mybir.AluOpType.add
 IS_GT = mybir.AluOpType.is_gt
-ACT = mybir.ActivationFunctionType
+COPY = mybir.ActivationFunctionType.Copy
 
 P = 128
 PASS = 512
@@ -28,23 +29,16 @@ KC = 2 * P
 HALF = C // 2
 KB = 1024
 
-G1_ON_GPSIMD = 256
-W1_FIRST_ON_GPSIMD = 192
-W1_LAST_ON_GPSIMD = 144
-
 
 def tile_moe_bdx_mlp_relu_kernel(tc, dyT, a, w2, w1, gate, offs, out):
     nc = tc.nc
     with ExitStack() as ctx:
         keep = ctx.enter_context(tc.tile_pool(name="keep", bufs=1))
         placed = ctx.enter_context(tc.tile_pool(name="placed", bufs=1))
-        psum = ctx.enter_context(tc.psum_pool(name="psum", bufs=4))
+        psum = ctx.enter_context(tc.psum_pool(name="psum", bufs=1))
 
         def at(kb, shape, dtype, name):
             return placed.tile([P] + shape, dtype, name=name, offset=int(kb * KB), align_bytes=64)
-
-        def grouped_at(kb, name, columns=C):
-            return at(kb, [4 * columns], BF16, name)
 
         def planes(ap):
             return ap.rearrange("p (t c) -> p t c", t=4)
@@ -56,40 +50,32 @@ def tile_moe_bdx_mlp_relu_kernel(tc, dyT, a, w2, w1, gate, offs, out):
             return dst.rearrange("p (c i) t -> p c t i", i=4), src.rearrange("p t (c i) -> p c t i", i=4)
 
         def on_scalar(dst, src):
-            dst_view, src_view = four_neighbours(dst, src)
-            nc.scalar.copy(out=dst_view, in_=src_view)
+            nc.scalar.copy(out=dst, in_=src)
 
         def on_vector(dst, src):
+            nc.vector.tensor_copy(out=dst, in_=src)
+
+        def interleave(copy, dst, src):
             dst_view, src_view = four_neighbours(dst, src)
-            nc.vector.tensor_copy(out=dst_view, in_=src_view)
+            copy(dst_view, src_view)
 
-        def on_gpsimd(dst, src):
-            nc.gpsimd.tensor_scalar(out=dst, in0=src.rearrange("p t c -> p c t"), scalar1=1.0, scalar2=0.0, op0=MULT, op1=ADD)
+        def grouped_tile(name, bufs):
+            return keep.tile([P, 4 * C], BF16, name=name, bufs=bufs, align_bytes=64)
 
-        def interleave_split(dst, src, first, width, second):
-            first(words(dst)[:, 0:width, :], src[:, :, 0:width])
-            second(words(dst)[:, width:C, :], src[:, :, width:C])
+        def group_w2(copy, raw):
+            dst = grouped_tile("wgroup", 3)
+            copy(dst[:].rearrange("p (t m j) -> p m j t", t=4, j=4), raw[:].rearrange("p j (m t) -> p m j t", t=4))
+            return dst
 
-        def group_w2(dst, raw, t0=0, t1=4):
-            nc.scalar.copy(out=dst.rearrange("p (t m j) -> p m j t", t=4, j=4)[:, :, :, t0:t1],
-                           in_=raw[:].rearrange("p j (m t) -> p m j t", t=4)[:, :, :, t0:t1])
-
-        def group_w1(dst, raws, copy):
-            for b in range(HB):
-                copy(words(dst)[:, b * KC:(b + 1) * KC, :], raws[b][:, :, 0:KC])
-
-        def quantize(grouped, fmt, name, codes_kb=None, scales_kb=None):
-            width = grouped.shape[1] // 4
-            if codes_kb is None:
-                codes = keep.tile([P, width], U32, name=name + "_codes", align_bytes=64)
-            else:
-                codes = at(codes_kb, [width], U32, name + "_codes")
-            if scales_kb is None:
-                scales = keep.tile([P, width], U8, name=name + "_scales", align_bytes=64)
-            else:
-                scales = at(scales_kb, [width], U8, name + "_scales")
-            nc.vector.quantize_mx(out=codes[:].bitcast(fmt), scales=scales[:], in_=grouped)
+        def mx_pair(name, width=C):
+            codes = keep.tile([P, width], U32, name=name + "_codes", align_bytes=64)
+            scales = keep.tile([P, width], U8, name=name + "_scales", align_bytes=64)
             return codes, scales
+
+        def quantize(pair, fmt, grouped, c0=0):
+            cols = slice(c0, c0 + grouped.shape[1] // 4)
+            nc.vector.quantize_mx(out=pair[0][:, cols].bitcast(fmt), scales=pair[1][:, cols], in_=grouped)
+            return pair
 
         def load(name, view, kb=None):
             shape = list(view.shape[1:])
@@ -103,290 +89,138 @@ def tile_moe_bdx_mlp_relu_kernel(tc, dyT, a, w2, w1, gate, offs, out):
         def load_dy(t):
             return load("dy%d" % t, by_planes(dyT)[:, t, :], 4 * t)
 
-        def load_w2(e, b, kb=None):
-            return load("w2raw%d%d" % (e, b), by_planes(w2[e, :, b * PASS:(b + 1) * PASS]), kb)
+        def load_w2(e, b):
+            return load("w2raw%d%d" % (e, b), by_planes(w2[e, :, b * PASS:(b + 1) * PASS]))
 
-        def a_planes(e, b):
-            return by_planes(a[b * PASS:(b + 1) * PASS, e * C:(e + 1) * C])
+        def load_a(e, b, s0, s1):
+            return load("a%d%d_%d" % (e, b, s0), by_planes(a[b * PASS:(b + 1) * PASS, e * C + s0:e * C + s1]))
 
-        def load_w1(e, b, c0, c1, kb=None):
-            return load("w1raw%d%d_%d" % (e, b, c0), by_planes(w1[e, b * PASS:(b + 1) * PASS, c0:c1]), kb)
+        def load_w1(e, b, c0, c1):
+            return load("w1raw%d%d_%d" % (e, b, c0), by_planes(w1[e, b * PASS:(b + 1) * PASS, c0:c1]))
 
         def slots_of(e, s0=0, s1=C):
             return offs_t[:, (e * C + s0) // 16:(e * C + s1) // 16]
 
-        def gather(e, t, dst, gate_ap, s0=0, s1=C):
-            nc.vector.tensor_tensor(dst[:, t * C + s0:t * C + s1], dy[t][:].indirect(slots_of(e, s0, s1)), gate_ap[:, s0:s1], MULT)
+        def relu_half(w2q, gq, a_part, daq, h):
+            cols = slice(h * HALF, (h + 1) * HALF)
+            pairs = keep.tile([P, 2, HALF, 2], BF16, name="pairs", bufs=3, align_bytes=64)
+            for u in range(2):
+                bank = psum.tile([P, 2, HALF], F32, name="dh", bufs=3)
+                for s in range(2):
+                    t = 2 * u + s
+                    nc.tensor.matmul_mx(out=bank[:, s, :], lhsT=w2q[0][:, t * P:(t + 1) * P].bitcast(E4), lhsT_scale=w2q[1][:, t * P:(t + 1) * P],
+                                        rhs=gq[0][:, cols].bitcast(E5), rhs_scale=gq[1][:, cols], start=True, stop=True)
+                nc.vector.scalar_tensor_tensor(out=pairs[:, u, :, :], in0=a_part[:, 2 * u:2 * u + 2, :].rearrange("p s c -> p c s"), scalar=0.0,
+                                               in1=bank[:].rearrange("p s c -> p c s"), op0=IS_GT, op1=MULT)
+            grouped = keep.tile([P, 4 * HALF], BF16, name="dagroup", bufs=3, align_bytes=64)
+            pair_words = pairs[:].rearrange("p u c s -> p u (c s)").bitcast(I32)
+            nc.vector.tensor_copy(out=grouped[:].bitcast(I32).rearrange("p (c i u) -> p c u i", i=4, u=2),
+                                  in_=pair_words.rearrange("p u (c i) -> p c u i", i=4))
+            quantize(daq, E5, grouped[:], h * HALF)
 
-        def copy_gate(dst, bank):
-            nc.scalar.copy(out=dst.rearrange("p (n m) -> p n m", m=4), in_=bank[:].rearrange("p (m n) -> p n m", m=4))
+        def w1_chunk(name, raws, copies):
+            dst = grouped_tile("wgroup", 3)
+            for b in range(HB):
+                interleave(copies[b], words(dst[:])[:, b * KC:(b + 1) * KC, :], raws[b])
+            return quantize(mx_pair(name), E4, dst[:])
 
-        def dh_plane(w2q, gq, t, tag="dh"):
-            bank = psum.tile([P, C], F32, name=tag)
-            cols = slice(t * P, (t + 1) * P)
-            nc.tensor.matmul_mx(out=bank[:], lhsT=w2q[0][:, cols].bitcast(E4), lhsT_scale=w2q[1][:, cols],
-                                rhs=gq[0][:].bitcast(E5), rhs_scale=gq[1][:], start=True, stop=True)
-            return bank
-
-        def relu_product(dst, a_pairs, banks, t, s0, s1):
-            nc.vector.scalar_tensor_tensor(out=dst, in0=a_pairs[t // 2][:, t % 2, s0:s1], scalar=0.0, in1=banks[t][:, s0:s1], op0=IS_GT, op1=MULT)
-
-        def dx_bank(parts, daq, order=(0, 1), tag="dx"):
-            bank = psum.tile([P, C], F32, name=tag)
-            for b in order:
+        def dx_bank(parts, daq, s0, s1):
+            bank = psum.tile([P, C], F32, name="dx", bufs=4)
+            for b in range(HB):
                 codes, scales, c0 = parts[b]
-                cols = slice(c0, c0 + P)
-                nc.tensor.matmul_mx(out=bank[:], lhsT=codes[:, cols].bitcast(E4), lhsT_scale=scales[:, cols],
-                                    rhs=daq[b][0][:].bitcast(E5), rhs_scale=daq[b][1][:], start=(b == order[0]), stop=(b == order[1]))
+                nc.tensor.matmul_mx(out=bank[:, 0:s1 - s0], lhsT=codes[:, c0:c0 + P].bitcast(E4), lhsT_scale=scales[:, c0:c0 + P],
+                                    rhs=daq[b][0][:, s0:s1].bitcast(E5), rhs_scale=daq[b][1][:, s0:s1], start=(b == 0), stop=(b == HB - 1))
             return bank
 
-        def dx_tile(parts, daq, tag="dx"):
-            staged = keep.tile([P, C], F32, name="staged", bufs=4)
-            nc.scalar.copy(out=staged[:], in_=dx_bank(parts, daq, tag=tag)[:])
-            return staged
+        def chunk_parts(w1q, u):
+            return [(w1q[0], w1q[1], b * KC + u * P) for b in range(HB)]
 
-        def stage_half(bank, h, kb=None):
-            staged = keep.tile([P, HALF], F32, name="staged_half", bufs=4) if kb is None else at(kb, [HALF], F32, "staged_held")
-            nc.scalar.copy(out=staged[:], in_=bank[:, h * HALF:(h + 1) * HALF])
-            return staged
+        def scalar_result(kt, e, parts, daq, s0=0, s1=C):
+            staged = keep.tile([P, C], F32, name="staged_scalar", bufs=2)
+            nc.scalar.copy(out=staged[:, 0:s1 - s0], in_=dx_bank(parts, daq, s0, s1)[:, 0:s1 - s0])
+            for s in range(s0, s1, HALF):
+                nc.scalar.activation(out=windows[kt][:].indirect(slots_of(e, s, s + HALF)), in_=staged[:, s - s0:s - s0 + HALF], func=COPY)
 
-        def scatter_half(kt, e, h, staged):
-            nc.vector.tensor_copy(out=windows[kt][:].indirect(slots_of(e, h * HALF, (h + 1) * HALF)), in_=staged[:])
+        def vector_result(kt, e, parts, daq, staged):
+            nc.vector.tensor_copy(out=staged[:], in_=dx_bank(parts, daq, 0, C)[:])
+            nc.vector.tensor_copy(out=windows[kt][:].indirect(slots_of(e)), in_=staged[:])
 
         def store(kt):
             nc.sync.dma_start(out=out[kt * P:(kt + 1) * P, :], in_=windows[kt][:])
 
-        def chunk_parts(w1q, c0):
-            return [(w1q[0], w1q[1], b * KC + c0) for b in range(HB)]
-
-        windows = []
-
-        def scatter_first(kb, staged):
-            window = at(kb, [T], F32, "window%d" % len(windows))
-            windows.append(window)
-            nc.vector.tensor_copy(out=window[:].indirect(slots_of(0)), in_=staged[:])
-
-        def sign_into(dst, a_part):
-            dst_view, src_view = four_neighbours(words(dst), a_part)
-            nc.scalar.activation(out=dst_view, in_=src_view, func=ACT.Sign)
-
-        def mask_of(sign, kb, name):
-            mask = grouped_at(kb, "mask" + name, HALF)
-            nc.scalar.activation(out=mask[:], in_=sign[:], func=ACT.Relu)
-            return mask
-
-        def round_dh11(banks, h):
-            for t in range(4):
-                nc.scalar.copy(out=dh_planes[:, 1, t, h * HALF:(h + 1) * HALF], in_=banks[t][:, h * HALF:(h + 1) * HALF])
-
-        def product(b, mask, kb, name):
-            da = grouped_at(kb, "dag" + name, HALF)
-            nc.gpsimd.tensor_tensor(words(da[:]), dh_planes[:, b, :, 0:HALF].rearrange("p t c -> p c t"), words(mask[:]), MULT)
-            return da
-
-        def quarter_sign(sign, q, b):
-            sign_into(sign[:, b * C:(b + 1) * C], second[b][:, :, q * P:(q + 1) * P])
-
-        def quarter_product(q, mask):
-            slots = slice(q * P, (q + 1) * P)
-            nc.gpsimd.tensor_tensor(dag_second[:].rearrange("p (b c t) -> p b c t", b=HB, t=4)[:, :, slots, :],
-                                    dh_planes[:, :, :, HALF + q * P:HALF + (q + 1) * P].rearrange("p b t c -> p b c t"),
-                                    mask[:].rearrange("p (b c t) -> p b c t", b=HB, t=4), MULT)
-
-        def quantize_half(da, b, h):
-            cols = slice(h * HALF, (h + 1) * HALF)
-            nc.vector.quantize_mx(out=daq[b][0][:, cols].bitcast(E5), scales=daq[b][1][:, cols], in_=da)
-
-        ident = at(27, [P], F32, "ident")
+        ident = keep.tile([P, P], F32, name="ident")
         make_identity(nc, ident[:])
-        dy = {1: load_dy(1)}
+        dy = {0: load_dy(0)}
         offs_t = keep.tile([P, E * C // 16], U16, name="offs_t")
         nc.sync.dma_start(offs_t[:], offs)
-        g_planes = at(28, [7 * C], F32, "g_planes")
-        gate0 = g_planes[:, 0:C]
-        nc.sync.dma_start(out=gate0, in_=gate[0:P, 0:C])
+        gate0 = load("gate0", gate[0:P, 0:C])
         gate_row = load("gate_row1", gate[1, C:2 * C].rearrange("(n m) -> n m", m=4))
-        dy[2] = load_dy(2)
-        gate_bank = psum.tile([P, C], F32, name="dh")
+        for t in range(1, 4):
+            dy[t] = load_dy(t)
+        gate_bank = psum.tile([P, C], F32, name="gates")
         for m in range(4):
             nc.tensor.transpose(gate_bank[:, m * P:(m + 1) * P], gate_row[:, m:m + 1].to_broadcast([P, P]), ident[:])
-        w2r00 = load_w2(0, 0)
-        dy[0] = load_dy(0)
-        dy[3] = load_dy(3)
-        w2r01_da00 = keep.tile([P, 4 * C + HALF], F32, name="w2r01_da00")
-        w2r01 = planes(w2r01_da00[:, HALF:HALF + 4 * C])
-        nc.sync.dma_start(out=w2r01, in_=by_planes(w2[0, :, PASS:2 * PASS]))
-        a00 = [load("apair00%d" % t, a_planes(0, 0)[:, t:t + 2, :]) for t in (0, 2)]
-        w1r00 = [load_w1(0, 0, 0, KC)]
-        a01 = [load("apair01%d" % t, a_planes(0, 1)[:, t:t + 2, :]) for t in (0, 2)]
-        w1r00.append(load_w1(0, 1, 0, KC))
-        w2r10 = load_w2(1, 0)
-        w1r01 = at(76, [HB, 4, KC], F32, "w1raw0_256")
+        w2r0 = [load_w2(0, b) for b in range(HB)]
+        a0 = [[load_a(0, b, 0, HALF) for b in range(HB)]]
+        w1r0 = [[load_w1(0, b, 0, KC) for b in range(HB)]]
+        a0.append([load_a(0, b, HALF, C) for b in range(HB)])
+        for c in (1, 2):
+            w1r0.append([load_w1(0, b, c * KC, (c + 1) * KC) for b in range(HB)])
+        w2r1 = [load_w2(1, b) for b in range(HB)]
+        a1 = [load_a(1, b, 0, C) for b in range(HB)]
+        w1r1 = [load_w1(1, b, 0, 2 * KC) for b in range(HB)]
+        w1r1_last = [load_w1(1, b, 2 * KC, K) for b in range(HB)]
+
+        g0 = at(16, [4 * C], F32, "g0")
+        g1 = at(24, [4 * C], F32, "g1")
+        for t in range(4):
+            nc.vector.tensor_tensor(g0[:, t * C:(t + 1) * C], dy[t][:].indirect(slots_of(0)), gate0[:], MULT)
+            nc.scalar.activation(out=g1[:, t * C:(t + 1) * C], in_=dy[t][:].indirect(slots_of(1)), func=COPY)
+        ggroup = grouped_tile("ggroup", 2)
+        interleave(on_vector, words(ggroup[:]), planes(g0[:]))
+        gq0 = quantize(mx_pair("gq0"), E5, ggroup[:])
+        w2q0 = [quantize(mx_pair("w2q00"), E4, group_w2(on_scalar, w2r0[0])[:])]
+        ggroup = grouped_tile("ggroup", 2)
+        dst_view, src_view = four_neighbours(words(ggroup[:]), planes(g1[:]))
+        nc.vector.tensor_tensor(dst_view, src_view, gate_bank[:].rearrange("p (m n) -> p n m", m=4).unsqueeze(2).to_broadcast([P, P, 4, 4]), MULT)
+        gq1 = quantize(mx_pair("gq1"), E5, ggroup[:])
+        w2q0.append(quantize(mx_pair("w2q01"), E4, group_w2(on_scalar, w2r0[1])[:]))
+
+        windows = [at(4 * kt, [T], F32, "window%d" % kt) for kt in range(KT)]
+
+        daq0 = [mx_pair("daq0%d" % b) for b in range(HB)]
         for b in range(HB):
-            nc.sync.dma_start(out=w1r01[:, b, :, :], in_=by_planes(w1[0, b * PASS:(b + 1) * PASS, KC:2 * KC]))
-        first = [load("afirst10", a_planes(1, 0)[:, :, 0:HALF])]
-        w1r02 = [load_w1(0, b, 2 * KC, K) for b in range(HB)]
-        w2r11 = load_w2(1, 1, 111)
-        first.append(load("afirst11", a_planes(1, 1)[:, :, 0:HALF], 68))
-        second = [load("asecond10", a_planes(1, 0)[:, :, HALF:C])]
-        w1r10 = [load_w1(1, 0, 0, 2 * KC, 92)]
-        second.append(load("asecond11", a_planes(1, 1)[:, :, HALF:C], 72))
-        w1r10.append(load_w1(1, 1, 0, 2 * KC, 84))
-        w1r11 = [load_w1(1, b, 2 * KC, K, 100 + 4 * b) for b in range(HB)]
-
-        g1 = g_planes[:, 0:4 * C]
-        g0 = g_planes[:, 3 * C:7 * C]
-        for t in (1, 2):
-            gather(0, t, g0, gate0)
-        for t, later in ((1, 0), (2, 3)):
-            parked = g0[:, later * C:(later + 1) * C]
-            copy_gate(parked, gate_bank)
-            gather(1, t, g1, parked)
-        gate1 = keep.tile([P, C], F32, name="gate1")
-        copy_gate(gate1[:], gate_bank)
-        w2g00 = grouped_at(24, "w2g00")
-        group_w2(w2g00[:], w2r00)
-        gather(0, 0, g0, gate0)
-        for s0 in (0, HALF):
-            gather(0, 3, g0, gate0, s0, s0 + HALF)
-        w2q00 = quantize(w2g00[:], E4, "w2q00")
-        ggrp0 = grouped_at(42, "ggrp0")
-        interleave_split(ggrp0[:], planes(g0), on_scalar, HALF, on_scalar)
-        gather(1, 0, g1, gate1[:])
-        gq0 = quantize(ggrp0[:], E5, "g0")
-        gather(1, 3, g1, gate1[:])
-
-        w1g01_at = HALF - 16
-        w2g10_at = w1g01_at + C - W1_LAST_ON_GPSIMD
-        chain = grouped_at(119, "chain", w2g10_at + HALF + C)
-
-        def link(start, columns=C):
-            return chain[:, 4 * start:4 * (start + columns)]
-
-        da010 = link(P, HALF)
-        dag011 = link(0, HALF)
-        w1g001 = link(HALF, KC)
-        w1g01 = link(w1g01_at)
-        w2g10 = link(w2g10_at)
-        ggrp1 = link(w2g10_at + HALF)
-        w2g01 = link(w2g10_at + HALF + G1_ON_GPSIMD - C)
-        group_w2(w2g01, w2r01)
-        da00_planes = w2r01_da00[:, 0:2 * C].bitcast(BF16)
-        w2q01 = quantize(w2g01, E4, "w2q01")
-        banks = [dh_plane(w2q00, gq0, t) for t in range(4)]
-        for t, s0, s1 in [(0, 0, C), (1, 0, C)] + [(t, s0, s0 + HALF) for s0 in (0, HALF) for t in (2, 3)]:
-            relu_product(da00_planes[:, t * C + s0:t * C + s1], a00, banks, t, s0, s1)
-        w1g000 = grouped_at(52, "w1g000", KC)
-
-        def cast_first(dst, u, b):
-            on_scalar(words(dst)[:, (1 - b) * P:(2 - b) * P, :], w1r00[b][:, :, u * P:(u + 1) * P])
-
-        cast_first(w1g000[:], 0, 0)
-        cast_first(w1g001, 1, 0)
-        interleave_split(ggrp1, planes(g1), on_gpsimd, G1_ON_GPSIMD, on_scalar)
-        dag00 = grouped_at(48, "dag00")
-        interleave_split(dag00[:], planes(da00_planes), on_scalar, HALF, on_gpsimd)
-        cast_first(w1g000[:], 0, 1)
-        da01 = [da010, grouped_at(60, "da011", HALF)[:]]
-        banks = [dh_plane(w2q01, gq0, t, "dx") for t in range(4)]
-        pieces = [(0, 0), (0, 1)] + [(t, h) for h in range(2) for t in (1, 2, 3)]
-        for t, h in pieces[:-1]:
-            relu_product(planes(da01[h])[:, t, :], a01, banks, t, h * HALF, (h + 1) * HALF)
-        w1q00 = [quantize(w1g000[:], E4, "w1q000")]
-        da00 = quantize(dag00[:], E5, "da00")
-        relu_product(planes(da01[1])[:, 3, :], a01, banks, 3, HALF, C)
-        daq = [da00, gq0]
-        dag010 = grouped_at(2, "dag010", HALF)
-        on_scalar(words(dag010[:]), planes(da01[0]))
-        quantize_half(dag010[:], 1, 0)
-        first_parts = [w1q00[0] + ((1 - b) * P,) for b in range(HB)]
-        first_bank = dx_bank(first_parts, daq)
-        on_vector(words(dag011), planes(da01[1]))
-        group_w2(w2g10, w2r10, 0, 2)
-        cast_first(w1g001, 1, 1)
-        gq1 = quantize(ggrp1, E5, "g1", scales_kb=2)
-        quantize_half(dag011, 1, 1)
-        w1q00.append(quantize(w1g001, E4, "w1q001"))
-
-        windows.append(at(48, [T], F32, "window0"))
-        scatter_half(0, 0, 0, stage_half(first_bank, 0))
-        on_gpsimd(words(w1g01)[:, 0:W1_FIRST_ON_GPSIMD, :], w1r01[:, 0, :, 0:W1_FIRST_ON_GPSIMD])
-        group_w2(w2g10, w2r10, 2, 4)
-        w2q10 = quantize(w2g10, E4, "w2q10")
-        scatter_half(0, 0, 1, stage_half(dx_bank(first_parts, daq, order=(1, 0)), 1))
-        on_gpsimd(words(w1g01)[:, C - W1_LAST_ON_GPSIMD:C, :], w1r01[:, 1, :, KC - W1_LAST_ON_GPSIMD:KC])
-        on_scalar(words(w1g01)[:, W1_FIRST_ON_GPSIMD:KC, :], w1r01[:, 0, :, W1_FIRST_ON_GPSIMD:KC])
-        on_scalar(words(w1g01)[:, KC:C - W1_LAST_ON_GPSIMD, :], w1r01[:, 1, :, 0:KC - W1_LAST_ON_GPSIMD])
-        staged = dx_tile([w1q00[1] + ((1 - b) * P,) for b in range(HB)], daq)
-        sign = grouped_at(40, "sign100", HALF)
-        sign_into(sign[:], first[0][:])
-        banks = [dh_plane(w2q10, gq1, t) for t in range(4)]
-        dh = grouped_at(52, "dh_planes", HB * C)
-        dh_planes = dh[:].rearrange("p (b t c) -> p b t c", b=HB, t=4)
-        for t in range(3):
-            if t == 2:
-                mask100 = mask_of(sign, 16, "100")
-            nc.scalar.copy(out=dh_planes[:, 0, t, :], in_=banks[t][:])
-        w1q01 = quantize(w1g01, E4, "w1q01", codes_kb=43, scales_kb=13.75)
-
-        scatter_first(78, staged)
-        w1g02 = grouped_at(119, "w1g02")
-        group_w1(w1g02[:], w1r02, on_gpsimd)
-        staged = [dx_tile(chunk_parts(w1q01, 0), daq)]
-        scatter_first(64, staged[0])
-        nc.scalar.copy(out=dh_planes[:, 0, 3, :], in_=banks[3][:])
-        dag100 = product(0, mask100, 8, "100")
-        w2g11 = grouped_at(10, "w2g11")
-        group_w2(w2g11[:], w2r11)
-        staged.append(dx_tile(chunk_parts(w1q01, P), daq))
-        w1q02 = quantize(w1g02[:], E4, "w1q02", codes_kb=111)
-        w2q11 = quantize(w2g11[:], E4, "w2q11")
-
-        scatter_first(119, staged[1])
-        sign = grouped_at(44, "sign110", HALF)
-        sign_into(sign[:], first[1][:])
-        signs = [grouped_at(46, "sign_quarter0", HALF)]
-        quarter_sign(signs[0], 0, 0)
-        mask110 = mask_of(sign, 82, "110")
-        staged = dx_tile(chunk_parts(w1q02, 0), daq)
-        w1g10 = grouped_at(10, "w1g10", 2 * C)
-        on_gpsimd(words(w1g10[:])[:, 0:C, :], w1r10[0][:])
-        banks = [dh_plane(w2q11, gq1, t) for t in range(4)]
-        round_dh11(banks, 0)
-        dag110 = product(1, mask110, 0, "110")
-        scatter_first(4, staged)
-        round_dh11(banks, 1)
-        on_scalar(words(w1g10[:])[:, C:2 * C, :], w1r10[1][:])
-        staged = dx_tile(chunk_parts(w1q02, P), daq, tag="dh")
-        quarter_sign(signs[0], 0, 1)
-        mask_quarter0 = mask_of(signs[0], 87, "quarter0")
-        signs.append(grouped_at(89, "sign_quarter1", HALF))
+            relu_half(w2q0[b], gq0, a0[0][b][:], daq0[b], 0)
+        w1q = w1_chunk("w1q00", [r[:] for r in w1r0[0]], [on_scalar, on_scalar])
+        for u in range(2):
+            scalar_result(u, 0, chunk_parts(w1q, u), daq0, 0, HALF)
         for b in range(HB):
-            quarter_sign(signs[1], 1, b)
-        quantize_half(dag100[:], 0, 0)
-        w1q10 = [quantize(w1g10[:, 0:4 * C], E4, "w1q100", scales_kb=82)]
-        quantize_half(dag110[:], 1, 0)
-        w1q10.append(quantize(w1g10[:, 4 * C:8 * C], E4, "w1q101", scales_kb=82.5))
+            relu_half(w2q0[b], gq0, a0[1][b][:], daq0[b], 1)
+        for u in range(2):
+            scalar_result(u, 0, chunk_parts(w1q, u), daq0, HALF, C)
+        for c in (1, 2):
+            w1q = w1_chunk("w1q0%d" % c, [r[:] for r in w1r0[c]], [on_vector, on_vector])
+            for u in range(2):
+                scalar_result(2 * c + u, 0, chunk_parts(w1q, u), daq0)
 
-        scatter_first(83, staged)
-        dag_second = grouped_at(10, "dag_second")
-        quarter_product(0, mask_quarter0)
-        banks = [dx_bank([q + (kt * P,) for q in w1q10], daq) for kt in range(4)]
-        for kt in range(2):
-            scatter_half(kt, 1, 0, stage_half(banks[kt], 0))
-        quarter_product(1, mask_of(signs[1], 20, "quarter1"))
-        scatter_half(2, 1, 0, stage_half(banks[2], 0))
-        w1g11 = grouped_at(89, "w1g11")
-        group_w1(w1g11[:], w1r11, on_scalar)
+        w2q1 = [quantize(mx_pair("w2q1%d" % b), E4, group_w2(on_vector, w2r1[b])[:]) for b in range(HB)]
+        daq1 = [mx_pair("daq1%d" % b) for b in range(HB)]
         for b in range(HB):
-            quantize_half(dag_second[:, b * 4 * HALF:(b + 1) * 4 * HALF], b, 1)
-        w1q11 = quantize(w1g11[:], E4, "w1q11", scales_kb=54)
-
-        scatter_half(3, 1, 0, stage_half(banks[3], 0, 20))
-        for kt in range(4):
-            scatter_half(kt, 1, 1, stage_half(dx_bank([q + (kt * P,) for q in w1q10], daq), 1))
-            store(kt)
-        for kt in range(4, KT):
-            staged = dx_tile(chunk_parts(w1q11, (kt - 4) * P), daq)
-            nc.vector.tensor_copy(out=windows[kt][:].indirect(slots_of(1)), in_=staged[:])
+            for h in range(2):
+                relu_half(w2q1[b], gq1, a1[b][:, :, h * HALF:(h + 1) * HALF], daq1[b], h)
+        w1q1 = []
+        for b in range(HB):
+            dst = grouped_tile("wgroup", 3)
+            interleave(on_vector, words(dst[:]), w1r1[b][:])
+            w1q1.append(quantize(mx_pair("w1q1%d" % b), E4, dst[:]))
+        dst = at(24, [4 * C], BF16, "w1group_last")
+        for b in range(HB):
+            interleave(on_vector, words(dst[:])[:, b * KC:(b + 1) * KC, :], w1r1_last[b][:])
+        w1q1_last = quantize(mx_pair("w1q12"), E4, dst[:])
+        parts = [[q + (kt * P,) for q in w1q1] for kt in range(4)] + [chunk_parts(w1q1_last, u) for u in range(2)]
+        for kt in range(KT):
+            if kt % 2 == 0:
+                scalar_result(kt, 1, parts[kt], daq1)
+            else:
+                vector_result(kt, 1, parts[kt], daq1, at(24 + 2 * (kt // 2 % 2), [C], F32, "staged_vector%d" % kt))
             store(kt)

@@ -28,6 +28,7 @@ KT = K // P
 KC = 2 * P
 HALF = C // 2
 KB = 1024
+W2_ON_SCALAR = (44, 76)
 
 
 def tile_moe_bdx_mlp_relu_kernel(tc, dyT, a, w2, w1, gate, offs, out):
@@ -62,15 +63,15 @@ def tile_moe_bdx_mlp_relu_kernel(tc, dyT, a, w2, w1, gate, offs, out):
         def grouped_tile(name, bufs):
             return keep.tile([P, 4 * C], BF16, name=name, bufs=bufs, align_bytes=64)
 
-        def group_w2(copy, raw):
-            dst = grouped_tile("wgroup", 3)
-            copy(dst[:].rearrange("p (t m j) -> p m j t", t=4, j=4), raw[:].rearrange("p j (m t) -> p m j t", t=4))
+        def group_w2(copy, raw, dst, m0=0, m1=P):
+            copy(dst[:].rearrange("p (t m j) -> p m j t", t=4, j=4)[:, m0:m1], raw.rearrange("p j (m t) -> p m j t", t=4)[:, m0:m1])
             return dst
 
-        def mx_pair(name, width=C):
+        def mx_pair(name, width=C, scales_kb=None):
             codes = keep.tile([P, width], U32, name=name + "_codes", align_bytes=64)
-            scales = keep.tile([P, width], U8, name=name + "_scales", align_bytes=64)
-            return codes, scales
+            if scales_kb is None:
+                return codes, keep.tile([P, width], U8, name=name + "_scales", align_bytes=64)
+            return codes, at(scales_kb, [width], U8, name + "_scales")
 
         def quantize(pair, fmt, grouped, c0=0):
             cols = slice(c0, c0 + grouped.shape[1] // 4)
@@ -82,6 +83,9 @@ def tile_moe_bdx_mlp_relu_kernel(tc, dyT, a, w2, w1, gate, offs, out):
             raw = keep.tile([P] + shape, F32, name=name) if kb is None else at(kb, shape, F32, name)
             nc.sync.dma_start(out=raw[:], in_=view)
             return raw
+
+        def w1raw_at(e, c, b):
+            return 60 + 4 * (HB * (3 * e + c) + b)
 
         def by_planes(rows):
             return rows.rearrange("(p t) c -> p t c", t=4)
@@ -96,131 +100,237 @@ def tile_moe_bdx_mlp_relu_kernel(tc, dyT, a, w2, w1, gate, offs, out):
             return load("a%d%d_%d" % (e, b, s0), by_planes(a[b * PASS:(b + 1) * PASS, e * C + s0:e * C + s1]))
 
         def load_w1(e, b, c0, c1):
-            return load("w1raw%d%d_%d" % (e, b, c0), by_planes(w1[e, b * PASS:(b + 1) * PASS, c0:c1]))
+            return load("w1raw%d%d_%d" % (e, b, c0), by_planes(w1[e, b * PASS:(b + 1) * PASS, c0:c1]), w1raw_at(e, c0 // KC, b))
 
         def slots_of(e, s0=0, s1=C):
             return offs_t[:, (e * C + s0) // 16:(e * C + s1) // 16]
 
-        def relu_half(w2q, gq, a_part, daq, h):
-            cols = slice(h * HALF, (h + 1) * HALF)
-            pairs = keep.tile([P, 2, HALF, 2], BF16, name="pairs", bufs=3, align_bytes=64)
+        def relu_products(w2q, gq, a_part, pairs):
             for u in range(2):
-                bank = psum.tile([P, 2, HALF], F32, name="dh", bufs=3)
+                bank = psum.tile([P, 2, HALF], F32, name="dh", bufs=4)
                 for s in range(2):
                     t = 2 * u + s
                     nc.tensor.matmul_mx(out=bank[:, s, :], lhsT=w2q[0][:, t * P:(t + 1) * P].bitcast(E4), lhsT_scale=w2q[1][:, t * P:(t + 1) * P],
-                                        rhs=gq[0][:, cols].bitcast(E5), rhs_scale=gq[1][:, cols], start=True, stop=True)
+                                        rhs=gq[0][:].bitcast(E5), rhs_scale=gq[1][:], start=True, stop=True)
                 nc.vector.scalar_tensor_tensor(out=pairs[:, u, :, :], in0=a_part[:, 2 * u:2 * u + 2, :].rearrange("p s c -> p c s"), scalar=0.0,
                                                in1=bank[:].rearrange("p s c -> p c s"), op0=IS_GT, op1=MULT)
-            grouped = keep.tile([P, 4 * HALF], BF16, name="dagroup", bufs=3, align_bytes=64)
-            pair_words = pairs[:].rearrange("p u c s -> p u (c s)").bitcast(I32)
-            nc.vector.tensor_copy(out=grouped[:].bitcast(I32).rearrange("p (c i u) -> p c u i", i=4, u=2),
-                                  in_=pair_words.rearrange("p u (c i) -> p c u i", i=4))
-            quantize(daq, E5, grouped[:], h * HALF)
+            return pairs
 
-        def w1_chunk(name, raws, copies):
-            dst = grouped_tile("wgroup", 3)
-            for b in range(HB):
-                interleave(copies[b], words(dst[:])[:, b * KC:(b + 1) * KC, :], raws[b])
-            return quantize(mx_pair(name), E4, dst[:])
+        def join_pairs(pairs, grouped):
+            pair_words = pairs[:].rearrange("p u c s -> p u (c s)").bitcast(I32)
+            nc.vector.tensor_copy(out=grouped.bitcast(I32).rearrange("p (c i u) -> p c u i", i=4, u=2),
+                                  in_=pair_words.rearrange("p u (c i) -> p c u i", i=4))
+
+        def plain(copy):
+            return lambda dst, src: interleave(copy, dst, src)
+
+        def on_gpsimd(dst, src):
+            nc.gpsimd.tensor_scalar(out=dst, in0=src.rearrange("p t c -> p c t"), scalar1=1.0, scalar2=0.0, op0=MULT, op1=ADD)
+
+        def cast_block(kb, e, c, b, cast):
+            dst = at(kb, [4 * KC], BF16, "w1group%d%d%d" % (e, c, b))
+            cast(words(dst[:]), w1r[e, c][b][:])
+            return dst
+
+        def quantize_block(e, c, b, grouped):
+            quantize(w1q[e][c], E4, grouped[:], b * KC)
 
         def dx_bank(parts, daq, s0, s1):
             bank = psum.tile([P, C], F32, name="dx", bufs=4)
-            for b in range(HB):
-                codes, scales, c0 = parts[b]
-                nc.tensor.matmul_mx(out=bank[:, 0:s1 - s0], lhsT=codes[:, c0:c0 + P].bitcast(E4), lhsT_scale=scales[:, c0:c0 + P],
-                                    rhs=daq[b][0][:, s0:s1].bitcast(E5), rhs_scale=daq[b][1][:, s0:s1], start=(b == 0), stop=(b == HB - 1))
+            cuts = [s0, s1 - HALF, s1] if s1 - s0 == 3 * P else [s0, s1]
+            for first, last in zip(cuts, cuts[1:]):
+                for b in range(HB):
+                    codes, scales, c0 = parts[b]
+                    nc.tensor.matmul_mx(out=bank[:, first - s0:last - s0], lhsT=codes[:, c0:c0 + P].bitcast(E4), lhsT_scale=scales[:, c0:c0 + P],
+                                        rhs=daq[b][0][:, first:last].bitcast(E5), rhs_scale=daq[b][1][:, first:last], start=(b == 0), stop=(b == HB - 1))
             return bank
 
         def chunk_parts(w1q, u):
             return [(w1q[0], w1q[1], b * KC + u * P) for b in range(HB)]
 
-        def scalar_result(kt, e, parts, daq, s0=0, s1=C):
-            staged = keep.tile([P, C], F32, name="staged_scalar", bufs=2)
-            nc.scalar.copy(out=staged[:, 0:s1 - s0], in_=dx_bank(parts, daq, s0, s1)[:, 0:s1 - s0])
-            for s in range(s0, s1, HALF):
-                nc.scalar.activation(out=windows[kt][:].indirect(slots_of(e, s, s + HALF)), in_=staged[:, s - s0:s - s0 + HALF], func=COPY)
+        def result_bank(kt, e, s0=0, s1=C):
+            return kt, e, s0, dx_bank(chunk_parts(w1q[e][kt // 2], kt % 2), daq[e], s0, s1)
 
-        def vector_result(kt, e, parts, daq, staged):
-            nc.vector.tensor_copy(out=staged[:], in_=dx_bank(parts, daq, 0, C)[:])
-            nc.vector.tensor_copy(out=windows[kt][:].indirect(slots_of(e)), in_=staged[:])
+        def stage(copy, result, s0, s1, kb):
+            kt, e, first, bank = result
+            staged = keep.tile([P, C], F32, name="staged", bufs=3) if kb is None else at(kb, [s1 - s0], F32, "staged%d%d_%d" % (e, kt, s0))
+            copy(staged[:, 0:s1 - s0], bank[:, s0 - first:s1 - first])
+            return kt, e, s0, s1, staged
 
-        def store(kt):
-            nc.sync.dma_start(out=out[kt * P:(kt + 1) * P, :], in_=windows[kt][:])
+        def stage_s(kt, e, s0=0, s1=C):
+            return stage(on_scalar, result_bank(kt, e, s0, s1), s0, s1, None)
+
+        def stage_v(kb, kt, e, s0=0, s1=C):
+            return stage(on_vector, result_bank(kt, e, s0, s1), s0, s1, kb)
+
+        def scatter_s(result, s0=None, s1=None):
+            kt, e, first, last, staged = result
+            s0, s1 = (first, last) if s0 is None else (s0, s1)
+            nc.scalar.activation(out=windows[kt][:].indirect(slots_of(e, s0, s1)), in_=staged[:, s0 - first:s1 - first], func=COPY)
+
+        def scatter_v(result, s0=None, s1=None):
+            kt, e, first, last, staged = result
+            s0, s1 = (first, last) if s0 is None else (s0, s1)
+            nc.vector.tensor_copy(out=windows[kt][:].indirect(slots_of(e, s0, s1)), in_=staged[:, s0 - first:s1 - first])
+
+        def store(kt, queue=nc.sync):
+            queue.dma_start(out=out[kt * P:(kt + 1) * P, :], in_=windows[kt][:])
 
         ident = keep.tile([P, P], F32, name="ident")
         make_identity(nc, ident[:])
+        gate_row = load("gate_row", gate[0, :].rearrange("(e n m) -> n e m", e=E, m=4))
         dy = {0: load_dy(0)}
         offs_t = keep.tile([P, E * C // 16], U16, name="offs_t")
         nc.sync.dma_start(offs_t[:], offs)
-        gate0 = load("gate0", gate[0:P, 0:C])
-        gate_row = load("gate_row1", gate[1, C:2 * C].rearrange("(n m) -> n m", m=4))
         for t in range(1, 4):
             dy[t] = load_dy(t)
-        gate_bank = psum.tile([P, C], F32, name="gates")
-        for m in range(4):
-            nc.tensor.transpose(gate_bank[:, m * P:(m + 1) * P], gate_row[:, m:m + 1].to_broadcast([P, P]), ident[:])
-        w2r0 = [load_w2(0, b) for b in range(HB)]
-        a0 = [[load_a(0, b, 0, HALF) for b in range(HB)]]
-        w1r0 = [[load_w1(0, b, 0, KC) for b in range(HB)]]
-        a0.append([load_a(0, b, HALF, C) for b in range(HB)])
-        for c in (1, 2):
-            w1r0.append([load_w1(0, b, c * KC, (c + 1) * KC) for b in range(HB)])
-        w2r1 = [load_w2(1, b) for b in range(HB)]
-        a1 = [load_a(1, b, 0, C) for b in range(HB)]
-        w1r1 = [load_w1(1, b, 0, 2 * KC) for b in range(HB)]
-        w1r1_last = [load_w1(1, b, 2 * KC, K) for b in range(HB)]
+        gate_banks = {}
+        for e in range(E):
+            gate_banks[e] = psum.tile([P, C], F32, name="dx", bufs=4)
+            for m in range(4):
+                nc.tensor.transpose(gate_banks[e][:, m * P:(m + 1) * P], gate_row[:, e, m:m + 1].to_broadcast([P, P]), ident[:])
+        w2r, a_half, w1r = {}, {}, {}
 
-        g0 = at(16, [4 * C], F32, "g0")
-        g1 = at(24, [4 * C], F32, "g1")
-        for t in range(4):
-            nc.vector.tensor_tensor(g0[:, t * C:(t + 1) * C], dy[t][:].indirect(slots_of(0)), gate0[:], MULT)
-            nc.scalar.activation(out=g1[:, t * C:(t + 1) * C], in_=dy[t][:].indirect(slots_of(1)), func=COPY)
-        ggroup = grouped_tile("ggroup", 2)
-        interleave(on_vector, words(ggroup[:]), planes(g0[:]))
-        gq0 = quantize(mx_pair("gq0"), E5, ggroup[:])
-        w2q0 = [quantize(mx_pair("w2q00"), E4, group_w2(on_scalar, w2r0[0])[:])]
-        ggroup = grouped_tile("ggroup", 2)
-        dst_view, src_view = four_neighbours(words(ggroup[:]), planes(g1[:]))
-        nc.vector.tensor_tensor(dst_view, src_view, gate_bank[:].rearrange("p (m n) -> p n m", m=4).unsqueeze(2).to_broadcast([P, P, 4, 4]), MULT)
-        gq1 = quantize(mx_pair("gq1"), E5, ggroup[:])
-        w2q0.append(quantize(mx_pair("w2q01"), E4, group_w2(on_scalar, w2r0[1])[:]))
-
-        windows = [at(4 * kt, [T], F32, "window%d" % kt) for kt in range(KT)]
-
-        daq0 = [mx_pair("daq0%d" % b) for b in range(HB)]
-        for b in range(HB):
-            relu_half(w2q0[b], gq0, a0[0][b][:], daq0[b], 0)
-        w1q = w1_chunk("w1q00", [r[:] for r in w1r0[0]], [on_scalar, on_scalar])
-        for u in range(2):
-            scalar_result(u, 0, chunk_parts(w1q, u), daq0, 0, HALF)
-        for b in range(HB):
-            relu_half(w2q0[b], gq0, a0[1][b][:], daq0[b], 1)
-        for u in range(2):
-            scalar_result(u, 0, chunk_parts(w1q, u), daq0, HALF, C)
-        for c in (1, 2):
-            w1q = w1_chunk("w1q0%d" % c, [r[:] for r in w1r0[c]], [on_vector, on_vector])
-            for u in range(2):
-                scalar_result(2 * c + u, 0, chunk_parts(w1q, u), daq0)
-
-        w2q1 = [quantize(mx_pair("w2q1%d" % b), E4, group_w2(on_vector, w2r1[b])[:]) for b in range(HB)]
-        daq1 = [mx_pair("daq1%d" % b) for b in range(HB)]
-        for b in range(HB):
-            for h in range(2):
-                relu_half(w2q1[b], gq1, a1[b][:, :, h * HALF:(h + 1) * HALF], daq1[b], h)
-        w1q1 = []
-        for b in range(HB):
-            dst = grouped_tile("wgroup", 3)
-            interleave(on_vector, words(dst[:]), w1r1[b][:])
-            w1q1.append(quantize(mx_pair("w1q1%d" % b), E4, dst[:]))
-        dst = at(24, [4 * C], BF16, "w1group_last")
-        for b in range(HB):
-            interleave(on_vector, words(dst[:])[:, b * KC:(b + 1) * KC, :], w1r1_last[b][:])
-        w1q1_last = quantize(mx_pair("w1q12"), E4, dst[:])
-        parts = [[q + (kt * P,) for q in w1q1] for kt in range(4)] + [chunk_parts(w1q1_last, u) for u in range(2)]
-        for kt in range(KT):
-            if kt % 2 == 0:
-                scalar_result(kt, 1, parts[kt], daq1)
+        def load_group(kind, e, i):
+            if kind == "w2":
+                if e == 0:
+                    whole = load("w2raw0", by_planes(w2[0]))
+                    w2r[e] = [whole[:, :, b * PASS:(b + 1) * PASS] for b in range(HB)]
+                else:
+                    w2r[e] = [load_w2(e, b)[:] for b in range(HB)]
+            elif kind == "a":
+                a_half[e, i] = [load_a(e, b, i * HALF, (i + 1) * HALF) for b in range(HB)]
             else:
-                vector_result(kt, 1, parts[kt], daq1, at(24 + 2 * (kt // 2 % 2), [C], F32, "staged_vector%d" % kt))
+                w1r[e, i] = [load_w1(e, b, i * KC, (i + 1) * KC) for b in range(HB)]
+
+        for kind, e, i in (("w2", 0, 0), ("a", 0, 0), ("w1", 0, 0), ("a", 0, 1), ("w1", 0, 1), ("w1", 0, 2),
+                           ("w2", 1, 0), ("a", 1, 0), ("w1", 1, 0), ("a", 1, 1), ("w1", 1, 1), ("w1", 1, 2)):
+            load_group(kind, e, i)
+
+        def group_at(kb, name):
+            return at(kb, [4 * C], BF16, name)
+
+        g_planes = [at(16 + 8 * e, [4 * C], F32, "g%d" % e) for e in range(E)]
+        gates = [at(35, [C], F32, "gate0"), keep.tile([P, C], F32, name="gate1")]
+
+        def copy_gates(copy, e):
+            copy(gates[e][:].rearrange("p (n m) -> p n m", m=4), gate_banks[e][:].rearrange("p (m n) -> p n m", m=4))
+
+        copy_gates(on_vector, 0)
+        for t in range(4):
+            nc.vector.tensor_tensor(g_planes[0][:, t * C:(t + 1) * C], dy[t][:].indirect(slots_of(0)), gates[0][:], MULT)
+            nc.scalar.activation(out=g_planes[1][:, t * C:(t + 1) * C], in_=dy[t][:].indirect(slots_of(1)), func=COPY)
+        copy_gates(on_scalar, 1)
+        ggroup0 = group_at(48, "ggroup0")
+        gq = {(e, h): mx_pair("gq%d%d" % (e, h), HALF) for e, h in ((0, 0), (0, 1), (1, 0))}
+        for h in range(2):
+            interleave(on_vector, words(ggroup0[:])[:, h * HALF:(h + 1) * HALF, :], planes(g_planes[0][:])[:, :, h * HALF:(h + 1) * HALF])
+        quantize(gq[0, 0], E5, ggroup0[:, 0:2 * C])
+        g1_first = at(35, [4 * P], BF16, "ggroup1_first")
+        dst_view, src_view = four_neighbours(words(g1_first[:]), planes(g_planes[1][:])[:, :, 0:P])
+        nc.vector.tensor_tensor(dst_view, src_view,
+                                gate_banks[1][:].rearrange("p (m n) -> p n m", m=4)[:, 0:P // 4].unsqueeze(2).to_broadcast([P, P // 4, 4, 4]), MULT)
+
+        def gate_on_gpsimd(kb, s0, s1):
+            dst = at(kb, [4 * (s1 - s0)], BF16, "ggroup1_%d" % s0)
+            nc.gpsimd.tensor_tensor(words(dst[:]), planes(g_planes[1][:])[:, :, s0:s1].rearrange("p t c -> p c t"),
+                                    gates[1][:, s0:s1].unsqueeze(2).to_broadcast([P, s1 - s0, 4]), MULT)
+            return dst
+
+        w2groups = [group_at(36 + 4 * b, "w2group0%d" % b) for b in range(HB)]
+        for b in range(HB):
+            group_w2(on_scalar, w2r[0][b], w2groups[b], 0, W2_ON_SCALAR[b])
+            group_w2(on_vector, w2r[0][b], w2groups[b], W2_ON_SCALAR[b], P)
+        w2q = [[quantize(mx_pair("w2q0%d" % b), E4, w2groups[b][:]) for b in range(HB)]]
+        quantize(gq[0, 1], E5, ggroup0[:, 2 * C:4 * C])
+        quantize(gq[1, 0], E5, g1_first[:])
+        g1_rest = [gate_on_gpsimd(40, P, HALF)]
+        windows = [at(4 * kt, [T], F32, "window%d" % kt) for kt in range(KT)]
+        daq = [[mx_pair("daq%d%d" % (e, b)) for b in range(HB)] for e in range(E)]
+
+        w1q = [[mx_pair("w1q%d%d" % (e, c)) for c in range(3)] for e in range(E)]
+        lanes = [[52, 56], [54, 58]]
+
+        def w1_chunk(e, c, cast, between=None):
+            groups = [cast_block(lanes[b][0], e, c, b, cast) for b in range(HB)]
+            result = between() if between else None
+            for b in range(HB):
+                quantize_block(e, c, b, groups[b])
+            return result
+
+        def gpsimd_chunk(e):
+            dst = group_at(lanes[0][0], "w1group%d2" % e)
+            for b in range(HB):
+                on_gpsimd(words(dst[:])[:, b * KC:(b + 1) * KC, :], w1r[e, 2][b][:])
+            return dst
+
+        def da_half(e, h):
+            pairs = [relu_products(w2q[e][b], gq[e, h], a_half[e, h][b][:], at(lanes[b][0], [2, HALF, 2], BF16, "pairs%d%d%d" % (e, h, b))) for b in range(HB)]
+            groups = [at(lanes[b][1], [4 * HALF], BF16, "dagroup%d%d%d" % (e, h, b)) for b in range(HB)]
+            for b in range(HB):
+                join_pairs(pairs[b], groups[b][:])
+                lanes[b].reverse()
+            for b in range(HB):
+                quantize(daq[e][b], E5, groups[b][:], h * HALF)
+
+        def pair_s(results):
+            for s in range(results[0][2], results[0][3], HALF):
+                for r in results:
+                    scatter_s(r, s, s + HALF)
+
+        da_half(0, 0)
+        quantize_block(0, 0, 0, cast_block(44, 0, 0, 0, plain(on_scalar)))
+        last_group = at(46, [4 * KC], BF16, "w1group001")
+        for u in range(2):
+            interleave(on_scalar, words(last_group[:])[:, u * P:(u + 1) * P, :], w1r[0, 0][1][:, :, u * P:(u + 1) * P])
+            quantize(w1q[0][0], E4, last_group[:, 4 * u * P:4 * (u + 1) * P], KC + u * P)
+        quantize(gq[1, 0], E5, g1_rest[0][:], P)
+        g1_rest.append(gate_on_gpsimd(40, HALF, C))
+        pair_s([stage_s(kt, 0, 0, HALF) for kt in range(2)])
+        da_half(0, 1)
+        r0 = stage_s(0, 0, HALF, C)
+        r1 = w1_chunk(0, 1, plain(on_vector), lambda: stage_v(w1raw_at(0, 1, 0), 1, 0, HALF, C))
+        last_chunk = gpsimd_chunk(0)
+        scatter_s(r0)
+        scatter_v(r1)
+        held_at = w1raw_at(0, 1, 1) + 3.75
+        r3 = stage_s(3, 0, 0, HALF)
+        scatter_v(stage_v(held_at, 2, 0, 0, P))
+        quantize(w1q[0][2], E4, last_chunk[:])
+        r2 = stage_s(2, 0, P, C)
+        scatter_s(r3)
+        r3 = stage_s(3, 0, HALF, C)
+        scatter_s(r2)
+        r4 = stage_s(4, 0)
+        scatter_s(r3)
+        pair_s([r4, stage_s(5, 0)])
+
+        w2groups = [group_w2(on_vector, w2r[1][b], group_at(held_at - 3.75 + 4 * b, "w2group1%d" % b)) for b in range(HB)]
+        w2q.append([quantize(mx_pair("w2q1%d" % b), E4, w2groups[b][:]) for b in range(HB)])
+        gq[1, 1] = quantize(mx_pair("gq11", HALF, held_at + 4), E5, g1_rest[1][:])
+        lanes = [[held_at - 3.75, 52], [held_at - 1.75, 54]]
+        da_half(1, 0)
+        w1_chunk(1, 0, plain(on_vector))
+        pair_s([stage_s(kt, 1, 0, HALF) for kt in range(2)])
+        da_half(1, 1)
+        halves = w1_chunk(1, 1, plain(on_vector), lambda: [stage_v(w1raw_at(1, 1, 0) + kt, kt, 1, HALF, C) for kt in range(2)])
+        last_chunk = gpsimd_chunk(1)
+        r3 = stage_s(3, 1, 0, HALF)
+        r2 = stage_s(2, 1)
+        for kt in range(2):
+            scatter_v(halves[kt])
             store(kt)
+        scatter_s(r3)
+        r3 = stage_v(w1raw_at(1, 2, 1), 3, 1, HALF, C)
+        quantize(w1q[1][2], E4, last_chunk[:])
+        pair_s([r2])
+        store(2)
+        scatter_v(r3)
+        store(3)
+        r4 = stage_v(w1raw_at(1, 1, 1), 4, 1)
+        r5 = [stage_s(5, 1, h * HALF, (h + 1) * HALF) for h in range(2)]
+        scatter_v(r4)
+        store(4)
+        for r in r5:
+            scatter_s(r)
+        store(5, nc.scalar)

@@ -10,7 +10,6 @@ BYTES = 4 * (N * T + H * E * C + E * N * H + E * H * K + E * C + K * T) + 2 * 12
 
 F32 = mybir.dt.float32
 BF16 = mybir.dt.bfloat16
-I32 = mybir.dt.int32
 U32 = mybir.dt.uint32
 U16 = mybir.dt.uint16
 U8 = mybir.dt.uint8
@@ -105,21 +104,15 @@ def tile_moe_bdx_mlp_relu_kernel(tc, dyT, a, w2, w1, gate, offs, out):
         def slots_of(e, s0=0, s1=C):
             return offs_t[:, (e * C + s0) // 16:(e * C + s1) // 16]
 
-        def relu_products(w2q, gq, a_part, pairs):
-            for u in range(2):
-                bank = psum.tile([P, 2, HALF], F32, name="dh", bufs=4)
-                for s in range(2):
-                    t = 2 * u + s
-                    nc.tensor.matmul_mx(out=bank[:, s, :], lhsT=w2q[0][:, t * P:(t + 1) * P].bitcast(E4), lhsT_scale=w2q[1][:, t * P:(t + 1) * P],
-                                        rhs=gq[0][:].bitcast(E5), rhs_scale=gq[1][:], start=True, stop=True)
-                nc.vector.scalar_tensor_tensor(out=pairs[:, u, :, :], in0=a_part[:, 2 * u:2 * u + 2, :].rearrange("p s c -> p c s"), scalar=0.0,
-                                               in1=bank[:].rearrange("p s c -> p c s"), op0=IS_GT, op1=MULT)
-            return pairs
-
-        def join_pairs(pairs, grouped):
-            pair_words = pairs[:].rearrange("p u c s -> p u (c s)").bitcast(I32)
-            nc.vector.tensor_copy(out=grouped.bitcast(I32).rearrange("p (c i u) -> p c u i", i=4, u=2),
-                                  in_=pair_words.rearrange("p u (c i) -> p c u i", i=4))
+        def relu_products(w2q, gq, a_part, grouped):
+            for s0 in range(0, HALF, P):
+                bank = psum.tile([P, 4, P], F32, name="dh", bufs=4)
+                for t in range(4):
+                    nc.tensor.matmul_mx(out=bank[:, t, :], lhsT=w2q[0][:, t * P:(t + 1) * P].bitcast(E4), lhsT_scale=w2q[1][:, t * P:(t + 1) * P],
+                                        rhs=gq[0][:, s0:s0 + P].bitcast(E5), rhs_scale=gq[1][:, s0:s0 + P], start=True, stop=True)
+                nc.vector.scalar_tensor_tensor(out=words(grouped[:])[:, s0:s0 + P, :], in0=a_part[:, :, s0:s0 + P].rearrange("p t c -> p c t"), scalar=0.0,
+                                               in1=bank[:].rearrange("p t c -> p c t"), op0=IS_GT, op1=MULT)
+            return grouped
 
         def plain(copy):
             return lambda dst, src: interleave(copy, dst, src)
@@ -265,11 +258,7 @@ def tile_moe_bdx_mlp_relu_kernel(tc, dyT, a, w2, w1, gate, offs, out):
             return dst
 
         def da_half(e, h):
-            pairs = [relu_products(w2q[e][b], gq[e, h], a_half[e, h][b][:], at(lanes[b][0], [2, HALF, 2], BF16, "pairs%d%d%d" % (e, h, b))) for b in range(HB)]
-            groups = [at(lanes[b][1], [4 * HALF], BF16, "dagroup%d%d%d" % (e, h, b)) for b in range(HB)]
-            for b in range(HB):
-                join_pairs(pairs[b], groups[b][:])
-                lanes[b].reverse()
+            groups = [relu_products(w2q[e][b], gq[e, h], a_half[e, h][b][:], at(lanes[b][0], [4 * HALF], BF16, "dagroup%d%d%d" % (e, h, b))) for b in range(HB)]
             for b in range(HB):
                 quantize(daq[e][b], E5, groups[b][:], h * HALF)
 

@@ -18,6 +18,7 @@ E5 = mybir.dt.float8_e5m2_x4
 MULT = mybir.AluOpType.mult
 ADD = mybir.AluOpType.add
 IS_GT = mybir.AluOpType.is_gt
+SIGN = mybir.ActivationFunctionType.Sign
 COPY = mybir.ActivationFunctionType.Copy
 
 P = 128
@@ -27,7 +28,11 @@ KT = K // P
 KC = 2 * P
 HALF = C // 2
 KB = 1024
-W2_ON_SCALAR = (44, 76)
+W2RAW_AT = 108
+HELD_SCALES = {(1, 0): 48.5, (1, 1): 48.75}
+LAST_ON_VECTOR = 64
+FILL = 128
+W2_ON_SCALAR = (44, 72)
 
 
 def tile_moe_bdx_mlp_relu_kernel(tc, dyT, a, w2, w1, gate, offs, out):
@@ -110,7 +115,7 @@ def tile_moe_bdx_mlp_relu_kernel(tc, dyT, a, w2, w1, gate, offs, out):
                 for t in range(4):
                     nc.tensor.matmul_mx(out=bank[:, t, :], lhsT=w2q[0][:, t * P:(t + 1) * P].bitcast(E4), lhsT_scale=w2q[1][:, t * P:(t + 1) * P],
                                         rhs=gq[0][:, s0:s0 + P].bitcast(E5), rhs_scale=gq[1][:, s0:s0 + P], start=True, stop=True)
-                nc.vector.scalar_tensor_tensor(out=words(grouped[:])[:, s0:s0 + P, :], in0=a_part[:, :, s0:s0 + P].rearrange("p t c -> p c t"), scalar=0.0,
+                nc.vector.scalar_tensor_tensor(out=words(grouped[:])[:, s0:s0 + P, :], in0=a_part[:, s0:s0 + P, :], scalar=0.0,
                                                in1=bank[:].rearrange("p t c -> p c t"), op0=IS_GT, op1=MULT)
             return grouped
 
@@ -187,7 +192,7 @@ def tile_moe_bdx_mlp_relu_kernel(tc, dyT, a, w2, w1, gate, offs, out):
         def load_group(kind, e, i):
             if kind == "w2":
                 if e == 0:
-                    whole = load("w2raw0", by_planes(w2[0]))
+                    whole = load("w2raw0", by_planes(w2[0]), W2RAW_AT)
                     w2r[e] = [whole[:, :, b * PASS:(b + 1) * PASS] for b in range(HB)]
                 else:
                     w2r[e] = [load_w2(e, b)[:] for b in range(HB)]
@@ -196,15 +201,19 @@ def tile_moe_bdx_mlp_relu_kernel(tc, dyT, a, w2, w1, gate, offs, out):
             else:
                 w1r[e, i] = [load_w1(e, b, i * KC, (i + 1) * KC) for b in range(HB)]
 
-        for kind, e, i in (("w2", 0, 0), ("a", 0, 0), ("w1", 0, 0), ("a", 0, 1), ("w1", 0, 1), ("w1", 0, 2),
-                           ("w2", 1, 0), ("a", 1, 0), ("w1", 1, 0), ("a", 1, 1), ("w1", 1, 1), ("w1", 1, 2)):
+        for kind, e, i in (("w2", 0, 0), ("a", 0, 0), ("w1", 0, 0), ("a", 0, 1), ("w1", 0, 1), ("w1", 0, 2), ("w2", 1, 0), ("w1", 1, 0), ("a", 1, 0)):
             load_group(kind, e, i)
+        a_half[1, 1], w1r[1, 1] = [], []
+        for b in range(HB):
+            a_half[1, 1].append(load_a(1, b, HALF, C))
+            w1r[1, 1].append(load_w1(1, b, KC, 2 * KC))
+        load_group("w1", 1, 2)
 
         def group_at(kb, name):
             return at(kb, [4 * C], BF16, name)
 
         g_planes = [at(16 + 8 * e, [4 * C], F32, "g%d" % e) for e in range(E)]
-        gates = [at(35, [C], F32, "gate0"), keep.tile([P, C], F32, name="gate1")]
+        gates = [at(34, [C], F32, "gate0"), keep.tile([P, C], F32, name="gate1")]
 
         def copy_gates(copy, e):
             copy(gates[e][:].rearrange("p (n m) -> p n m", m=4), gate_banks[e][:].rearrange("p (m n) -> p n m", m=4))
@@ -213,108 +222,117 @@ def tile_moe_bdx_mlp_relu_kernel(tc, dyT, a, w2, w1, gate, offs, out):
         for t in range(4):
             nc.vector.tensor_tensor(g_planes[0][:, t * C:(t + 1) * C], dy[t][:].indirect(slots_of(0)), gates[0][:], MULT)
             nc.scalar.activation(out=g_planes[1][:, t * C:(t + 1) * C], in_=dy[t][:].indirect(slots_of(1)), func=COPY)
+        gq = {(e, h): mx_pair("gq%d%d" % (e, h), HALF, HELD_SCALES.get((e, h))) for e in range(E) for h in range(2)}
+
         copy_gates(on_scalar, 1)
-        ggroup0 = group_at(48, "ggroup0")
-        gq = {(e, h): mx_pair("gq%d%d" % (e, h), HALF) for e, h in ((0, 0), (0, 1), (1, 0))}
+        g0_groups = [at(48 + 2 * h, [4 * HALF], BF16, "ggroup0%d" % h) for h in range(2)]
         for h in range(2):
-            interleave(on_vector, words(ggroup0[:])[:, h * HALF:(h + 1) * HALF, :], planes(g_planes[0][:])[:, :, h * HALF:(h + 1) * HALF])
-        quantize(gq[0, 0], E5, ggroup0[:, 0:2 * C])
-        g1_first = at(35, [4 * P], BF16, "ggroup1_first")
-        dst_view, src_view = four_neighbours(words(g1_first[:]), planes(g_planes[1][:])[:, :, 0:P])
-        nc.vector.tensor_tensor(dst_view, src_view,
-                                gate_banks[1][:].rearrange("p (m n) -> p n m", m=4)[:, 0:P // 4].unsqueeze(2).to_broadcast([P, P // 4, 4, 4]), MULT)
-
-        def gate_on_gpsimd(kb, s0, s1):
-            dst = at(kb, [4 * (s1 - s0)], BF16, "ggroup1_%d" % s0)
-            nc.gpsimd.tensor_tensor(words(dst[:]), planes(g_planes[1][:])[:, :, s0:s1].rearrange("p t c -> p c t"),
-                                    gates[1][:, s0:s1].unsqueeze(2).to_broadcast([P, s1 - s0, 4]), MULT)
-            return dst
-
-        w2groups = [group_at(36 + 4 * b, "w2group0%d" % b) for b in range(HB)]
+            interleave(on_vector, words(g0_groups[h][:]), planes(g_planes[0][:])[:, :, h * HALF:(h + 1) * HALF])
+        for h in range(2):
+            quantize(gq[0, h], E5, g0_groups[h][:])
+        w2groups = [group_at(35.75 + 4.25 * b, "w2group0%d" % b) for b in range(HB)]
         for b in range(HB):
             group_w2(on_scalar, w2r[0][b], w2groups[b], 0, W2_ON_SCALAR[b])
             group_w2(on_vector, w2r[0][b], w2groups[b], W2_ON_SCALAR[b], P)
         w2q = [[quantize(mx_pair("w2q0%d" % b), E4, w2groups[b][:]) for b in range(HB)]]
-        quantize(gq[0, 1], E5, ggroup0[:, 2 * C:4 * C])
-        quantize(gq[1, 0], E5, g1_first[:])
-        g1_rest = [gate_on_gpsimd(40, P, HALF)]
+
+        def gate_on_gpsimd(h, kb):
+            dst = at(kb, [HALF, 4], BF16, "ggroup1%d" % h)
+            slots = slice(h * HALF, (h + 1) * HALF)
+            nc.gpsimd.tensor_tensor(dst[:], planes(g_planes[1][:])[:, :, slots].rearrange("p t c -> p c t"),
+                                    gates[1][:, slots].unsqueeze(2).to_broadcast([P, HALF, 4]), MULT)
+            return dst[:].rearrange("p c t -> p (c t)")
+
+        g1_groups = [gate_on_gpsimd(0, 40)]
         windows = [at(4 * kt, [T], F32, "window%d" % kt) for kt in range(KT)]
         daq = [[mx_pair("daq%d%d" % (e, b)) for b in range(HB)] for e in range(E)]
 
         w1q = [[mx_pair("w1q%d%d" % (e, c)) for c in range(3)] for e in range(E)]
-        lanes = [[52, 56], [54, 58]]
 
-        def w1_chunk(e, c, cast, between=None):
-            groups = [cast_block(lanes[b][0], e, c, b, cast) for b in range(HB)]
-            result = between() if between else None
-            for b in range(HB):
-                quantize_block(e, c, b, groups[b])
-            return result
+        def relu_half(e, h, kb):
+            return [relu_products(w2q[e][b], gq[e, h], a_words[e, h, b], at(kb + 2 * b, [4 * HALF], BF16, "dagroup%d%d%d" % (e, h, b))) for b in range(HB)]
 
-        def gpsimd_chunk(e):
-            dst = group_at(lanes[0][0], "w1group%d2" % e)
-            for b in range(HB):
-                on_gpsimd(words(dst[:])[:, b * KC:(b + 1) * KC, :], w1r[e, 2][b][:])
-            return dst
-
-        def da_half(e, h):
-            groups = [relu_products(w2q[e][b], gq[e, h], a_half[e, h][b][:], at(lanes[b][0], [4 * HALF], BF16, "dagroup%d%d%d" % (e, h, b))) for b in range(HB)]
+        def quantize_da(e, h, groups):
             for b in range(HB):
                 quantize(daq[e][b], E5, groups[b][:], h * HALF)
+
+        def gpsimd_chunk(e, c, kb, width=KC):
+            dst = group_at(kb, "w1group%d%d" % (e, c))
+            on_gpsimd(words(dst[:])[:, 0:KC, :], w1r[e, c][0][:])
+            on_gpsimd(words(dst[:])[:, KC:KC + width, :], w1r[e, c][1][:, :, 0:width])
+            return dst
 
         def pair_s(results):
             for s in range(results[0][2], results[0][3], HALF):
                 for r in results:
                     scatter_s(r, s, s + HALF)
 
-        da_half(0, 0)
+        a_words = {(e, h, b): a_half[e, h][b][:].rearrange("p t c -> p c t") for e in range(E) for h in range(2) for b in range(HB)}
+        signs = at(W2RAW_AT + 2, [HALF, 4], BF16, "signs")
+        dst_view, src_view = four_neighbours(signs[:], a_half[0, 0][1][:])
+        nc.scalar.activation(out=dst_view, in_=src_view, func=SIGN)
+        a_words[0, 0, 1] = signs[:]
+        groups = relu_half(0, 0, 52)
+        quantize_da(0, 0, groups)
         quantize_block(0, 0, 0, cast_block(44, 0, 0, 0, plain(on_scalar)))
         last_group = at(46, [4 * KC], BF16, "w1group001")
         for u in range(2):
             interleave(on_scalar, words(last_group[:])[:, u * P:(u + 1) * P, :], w1r[0, 0][1][:, :, u * P:(u + 1) * P])
             quantize(w1q[0][0], E4, last_group[:, 4 * u * P:4 * (u + 1) * P], KC + u * P)
-        quantize(gq[1, 0], E5, g1_rest[0][:], P)
-        g1_rest.append(gate_on_gpsimd(40, HALF, C))
+        g1_groups.append(gate_on_gpsimd(1, 46))
         pair_s([stage_s(kt, 0, 0, HALF) for kt in range(2)])
-        da_half(0, 1)
-        r0 = stage_s(0, 0, HALF, C)
-        r1 = w1_chunk(0, 1, plain(on_vector), lambda: stage_v(w1raw_at(0, 1, 0), 1, 0, HALF, C))
-        last_chunk = gpsimd_chunk(0)
-        scatter_s(r0)
+        quantize_da(0, 1, relu_half(0, 1, 52))
+        bank0 = result_bank(0, 0, HALF, C)
+        scatter_s(stage(on_scalar, bank0, HALF, C - P, None))
+        groups = [cast_block(52 + 2 * b, 0, 1, b, plain(on_vector)) for b in range(HB)]
+        for b in range(HB):
+            quantize_block(0, 1, b, groups[b])
+        r1 = stage_v(52, 1, 0, HALF, C)
+        r0 = stage(on_vector, bank0, C - P, C, 53)
+        w1group = gpsimd_chunk(0, 2, 54, KC - LAST_ON_VECTOR)
         scatter_v(r1)
-        held_at = w1raw_at(0, 1, 1) + 3.75
-        r3 = stage_s(3, 0, 0, HALF)
-        scatter_v(stage_v(held_at, 2, 0, 0, P))
-        quantize(w1q[0][2], E4, last_chunk[:])
-        r2 = stage_s(2, 0, P, C)
-        scatter_s(r3)
-        r3 = stage_s(3, 0, HALF, C)
-        scatter_s(r2)
-        r4 = stage_s(4, 0)
-        scatter_s(r3)
-        pair_s([r4, stage_s(5, 0)])
+        scatter_v(r0)
+        rest = at(52.5, [4 * LAST_ON_VECTOR], BF16, "w1group02_rest")
+        interleave(on_vector, words(rest[:]), w1r[0, 2][1][:, :, KC - LAST_ON_VECTOR:KC])
+        w2groups = [group_w2(on_vector, w2r[1][0], group_at(48.5, "w2group10"))]
+        quantize(w1q[0][2], E4, w1group[:, 0:4 * KC])
+        quantize(w1q[0][2], E4, w1group[:, 4 * KC:6 * KC], KC)
+        quantize(w1q[0][2], E4, w1group[:, 6 * KC:7 * KC], KC + P)
+        quantize(w1q[0][2], E4, rest[:], C - LAST_ON_VECTOR)
+        pair_s([stage_s(kt, 0) for kt in (2, 3)])
 
-        w2groups = [group_w2(on_vector, w2r[1][b], group_at(held_at - 3.75 + 4 * b, "w2group1%d" % b)) for b in range(HB)]
-        w2q.append([quantize(mx_pair("w2q1%d" % b), E4, w2groups[b][:]) for b in range(HB)])
-        gq[1, 1] = quantize(mx_pair("gq11", HALF, held_at + 4), E5, g1_rest[1][:])
-        lanes = [[held_at - 3.75, 52], [held_at - 1.75, 54]]
-        da_half(1, 0)
-        w1_chunk(1, 0, plain(on_vector))
+        w2q.append([quantize(mx_pair("w2q10"), E4, w2groups[0][:])])
+        w2groups.append(group_w2(on_vector, w2r[1][1], group_at(54, "w2group11")))
+        for h in range(2):
+            quantize(gq[1, h], E5, g1_groups[h])
+        w2q[1].append(quantize(mx_pair("w2q11"), E4, w2groups[1][:]))
+        w1group = gpsimd_chunk(1, 0, 56)
+        scatter_v(stage_v(49, 5, 0, 0, FILL))
+        r4, r5 = stage_s(4, 0), stage_s(5, 0, FILL, C)
+        scatter_s(r4, 0, HALF)
+        scatter_s(r5)
+        scatter_s(r4, HALF, C)
+        quantize_da(1, 0, relu_half(1, 0, 49))
+        quantize(w1q[1][0], E4, w1group[:])
         pair_s([stage_s(kt, 1, 0, HALF) for kt in range(2)])
-        da_half(1, 1)
-        halves = w1_chunk(1, 1, plain(on_vector), lambda: [stage_v(w1raw_at(1, 1, 0) + kt, kt, 1, HALF, C) for kt in range(2)])
-        last_chunk = gpsimd_chunk(1)
-        r3 = stage_s(3, 1, 0, HALF)
-        r2 = stage_s(2, 1)
+        first_block = cast_block(56, 1, 1, 0, on_gpsimd)
+        quantize_da(1, 1, relu_half(1, 1, 49))
+        second_block = cast_block(49, 1, 1, 1, plain(on_vector))
+        quantize_block(1, 1, 0, first_block)
+        quantize_block(1, 1, 1, second_block)
+        halves = [stage_v(51 + kt, kt, 1, HALF, C) for kt in range(2)]
+        w1group = gpsimd_chunk(1, 2, 47)
+        r2, r3, r3_last = stage_s(2, 1, 0, HALF), stage_s(3, 1, 0, HALF), stage_s(3, 1, HALF, C)
         for kt in range(2):
             scatter_v(halves[kt])
             store(kt)
+        scatter_s(r2)
         scatter_s(r3)
-        r3 = stage_v(w1raw_at(1, 2, 1), 3, 1, HALF, C)
-        quantize(w1q[1][2], E4, last_chunk[:])
-        pair_s([r2])
+        r2 = stage_v(w1raw_at(1, 2, 1), 2, 1, HALF, C)
+        quantize(w1q[1][2], E4, w1group[:])
+        scatter_v(r2)
         store(2)
-        scatter_v(r3)
+        scatter_s(r3_last)
         store(3)
         r4 = stage_v(w1raw_at(1, 1, 1), 4, 1)
         r5 = [stage_s(5, 1, h * HALF, (h + 1) * HALF) for h in range(2)]

@@ -29,9 +29,8 @@ KC = 2 * P
 HALF = C // 2
 KB = 1024
 W2RAW_AT = 108
-HELD_SCALES = {(1, 0): 48.5, (1, 1): 48.75}
-LAST_ON_VECTOR = 64
-FILL = 128
+HELD_SCALES = {(1, 0): 24, (1, 1): 24.25}
+LAST_ON_VECTOR = 128
 W2_ON_SCALAR = (44, 72)
 
 
@@ -201,8 +200,10 @@ def tile_moe_bdx_mlp_relu_kernel(tc, dyT, a, w2, w1, gate, offs, out):
             else:
                 w1r[e, i] = [load_w1(e, b, i * KC, (i + 1) * KC) for b in range(HB)]
 
-        for kind, e, i in (("w2", 0, 0), ("a", 0, 0), ("w1", 0, 0), ("a", 0, 1), ("w1", 0, 1), ("w1", 0, 2), ("w2", 1, 0), ("w1", 1, 0), ("a", 1, 0)):
+        for kind, e, i in (("w2", 0, 0), ("a", 0, 0), ("w1", 0, 0), ("a", 0, 1), ("w1", 0, 1), ("w1", 0, 2), ("w2", 1, 0)):
             load_group(kind, e, i)
+        w1r[1, 0] = [load_w1(1, b, 0, KC) for b in (1, 0)][::-1]
+        load_group("a", 1, 0)
         a_half[1, 1], w1r[1, 1] = [], []
         for b in range(HB):
             a_half[1, 1].append(load_a(1, b, HALF, C))
@@ -236,14 +237,13 @@ def tile_moe_bdx_mlp_relu_kernel(tc, dyT, a, w2, w1, gate, offs, out):
             group_w2(on_vector, w2r[0][b], w2groups[b], W2_ON_SCALAR[b], P)
         w2q = [[quantize(mx_pair("w2q0%d" % b), E4, w2groups[b][:]) for b in range(HB)]]
 
-        def gate_on_gpsimd(h, kb):
-            dst = at(kb, [HALF, 4], BF16, "ggroup1%d" % h)
-            slots = slice(h * HALF, (h + 1) * HALF)
-            nc.gpsimd.tensor_tensor(dst[:], planes(g_planes[1][:])[:, :, slots].rearrange("p t c -> p c t"),
-                                    gates[1][:, slots].unsqueeze(2).to_broadcast([P, HALF, 4]), MULT)
+        def gate_on_gpsimd(s0, kb):
+            dst = at(kb, [P, 4], BF16, "ggroup1_%d" % s0)
+            nc.gpsimd.tensor_tensor(dst[:], planes(g_planes[1][:])[:, :, s0:s0 + P].rearrange("p t c -> p c t"),
+                                    gates[1][:, s0:s0 + P].unsqueeze(2).to_broadcast([P, P, 4]), MULT)
             return dst[:].rearrange("p c t -> p (c t)")
 
-        g1_groups = [gate_on_gpsimd(0, 40)]
+        g1_quarters = [gate_on_gpsimd(0, 40)]
         windows = [at(4 * kt, [T], F32, "window%d" % kt) for kt in range(KT)]
         daq = [[mx_pair("daq%d%d" % (e, b)) for b in range(HB)] for e in range(E)]
 
@@ -279,7 +279,7 @@ def tile_moe_bdx_mlp_relu_kernel(tc, dyT, a, w2, w1, gate, offs, out):
         for u in range(2):
             interleave(on_scalar, words(last_group[:])[:, u * P:(u + 1) * P, :], w1r[0, 0][1][:, :, u * P:(u + 1) * P])
             quantize(w1q[0][0], E4, last_group[:, 4 * u * P:4 * (u + 1) * P], KC + u * P)
-        g1_groups.append(gate_on_gpsimd(1, 46))
+        g1_quarters.append(gate_on_gpsimd(P, 46))
         pair_s([stage_s(kt, 0, 0, HALF) for kt in range(2)])
         quantize_da(0, 1, relu_half(0, 1, 52))
         bank0 = result_bank(0, 0, HALF, C)
@@ -288,34 +288,36 @@ def tile_moe_bdx_mlp_relu_kernel(tc, dyT, a, w2, w1, gate, offs, out):
         for b in range(HB):
             quantize_block(0, 1, b, groups[b])
         r1 = stage_v(52, 1, 0, HALF, C)
-        r0 = stage(on_vector, bank0, C - P, C, 53)
+        r0 = stage(on_vector, bank0, C - P, C, 53.5)
         w1group = gpsimd_chunk(0, 2, 54, KC - LAST_ON_VECTOR)
         scatter_v(r1)
         scatter_v(r0)
-        rest = at(52.5, [4 * LAST_ON_VECTOR], BF16, "w1group02_rest")
-        interleave(on_vector, words(rest[:]), w1r[0, 2][1][:, :, KC - LAST_ON_VECTOR:KC])
-        w2groups = [group_w2(on_vector, w2r[1][0], group_at(48.5, "w2group10"))]
+        held = at(49.25, [4 * (HALF + LAST_ON_VECTOR)], BF16, "ggroup11_and_rest")
+        g11, rest = held[:, 0:4 * HALF], held[:, 4 * HALF:]
+        dst_view, src_view = four_neighbours(words(g11), planes(g_planes[1][:])[:, :, HALF:C])
+        nc.vector.tensor_tensor(dst_view, src_view, gates[1][:, HALF:C].rearrange("p (c i) -> p c i", i=4).unsqueeze(2).to_broadcast([P, HALF // 4, 4, 4]), MULT)
+        interleave(on_vector, words(rest), w1r[0, 2][1][:, :, KC - LAST_ON_VECTOR:KC])
+        w2groups = [group_w2(on_vector, w2r[1][0], group_at(24, "w2group10"))]
         quantize(w1q[0][2], E4, w1group[:, 0:4 * KC])
         quantize(w1q[0][2], E4, w1group[:, 4 * KC:6 * KC], KC)
-        quantize(w1q[0][2], E4, w1group[:, 6 * KC:7 * KC], KC + P)
-        quantize(w1q[0][2], E4, rest[:], C - LAST_ON_VECTOR)
+        quantize(w1q[0][2], E4, rest, C - LAST_ON_VECTOR)
         pair_s([stage_s(kt, 0) for kt in (2, 3)])
 
         w2q.append([quantize(mx_pair("w2q10"), E4, w2groups[0][:])])
+        for q in range(2):
+            quantize(gq[1, 0], E5, g1_quarters[q], q * P)
         w2groups.append(group_w2(on_vector, w2r[1][1], group_at(54, "w2group11")))
-        for h in range(2):
-            quantize(gq[1, h], E5, g1_groups[h])
+        quantize(gq[1, 1], E5, g11)
+        second_block = cast_block(26, 1, 0, 1, plain(on_vector))
         w2q[1].append(quantize(mx_pair("w2q11"), E4, w2groups[1][:]))
-        w1group = gpsimd_chunk(1, 0, 56)
-        scatter_v(stage_v(49, 5, 0, 0, FILL))
-        r4, r5 = stage_s(4, 0), stage_s(5, 0, FILL, C)
-        scatter_s(r4, 0, HALF)
-        scatter_s(r5)
-        scatter_s(r4, HALF, C)
-        quantize_da(1, 0, relu_half(1, 0, 49))
-        quantize(w1q[1][0], E4, w1group[:])
+        quantize_block(1, 0, 1, second_block)
+        first_block = cast_block(26, 1, 0, 0, on_gpsimd)
+        pair_s([stage_s(kt, 0) for kt in (4, 5)])
+        groups = relu_half(1, 0, 49)
+        quantize_block(1, 0, 0, first_block)
+        quantize_da(1, 0, groups)
         pair_s([stage_s(kt, 1, 0, HALF) for kt in range(2)])
-        first_block = cast_block(56, 1, 1, 0, on_gpsimd)
+        first_block = cast_block(26, 1, 1, 0, on_gpsimd)
         quantize_da(1, 1, relu_half(1, 1, 49))
         second_block = cast_block(49, 1, 1, 1, plain(on_vector))
         quantize_block(1, 1, 0, first_block)

@@ -29,7 +29,8 @@ KC = 2 * P
 HALF = C // 2
 KB = 1024
 W2RAW_AT = 108
-HELD_SCALES = {(1, 0): 24, (1, 1): 24.25}
+W2RAW1_AT = 124
+HELD_SCALES = {(1, 0): 80}
 LAST_ON_VECTOR = 128
 W2_ON_SCALAR = (44, 72)
 
@@ -190,11 +191,8 @@ def tile_moe_bdx_mlp_relu_kernel(tc, dyT, a, w2, w1, gate, offs, out):
 
         def load_group(kind, e, i):
             if kind == "w2":
-                if e == 0:
-                    whole = load("w2raw0", by_planes(w2[0]), W2RAW_AT)
-                    w2r[e] = [whole[:, :, b * PASS:(b + 1) * PASS] for b in range(HB)]
-                else:
-                    w2r[e] = [load_w2(e, b)[:] for b in range(HB)]
+                whole = load("w2raw%d" % e, by_planes(w2[e]), W2RAW1_AT if e else W2RAW_AT)
+                w2r[e] = [whole[:, :, b * PASS:(b + 1) * PASS] for b in range(HB)]
             elif kind == "a":
                 a_half[e, i] = [load_a(e, b, i * HALF, (i + 1) * HALF) for b in range(HB)]
             else:
@@ -297,33 +295,32 @@ def tile_moe_bdx_mlp_relu_kernel(tc, dyT, a, w2, w1, gate, offs, out):
         dst_view, src_view = four_neighbours(words(g11), planes(g_planes[1][:])[:, :, HALF:C])
         nc.vector.tensor_tensor(dst_view, src_view, gates[1][:, HALF:C].rearrange("p (c i) -> p c i", i=4).unsqueeze(2).to_broadcast([P, HALF // 4, 4, 4]), MULT)
         interleave(on_vector, words(rest), w1r[0, 2][1][:, :, KC - LAST_ON_VECTOR:KC])
-        w2groups = [group_w2(on_vector, w2r[1][0], group_at(24, "w2group10"))]
         quantize(w1q[0][2], E4, w1group[:, 0:4 * KC])
         quantize(w1q[0][2], E4, w1group[:, 4 * KC:6 * KC], KC)
         quantize(w1q[0][2], E4, rest, C - LAST_ON_VECTOR)
         pair_s([stage_s(kt, 0) for kt in (2, 3)])
 
-        w2q.append([quantize(mx_pair("w2q10"), E4, w2groups[0][:])])
         for q in range(2):
             quantize(gq[1, 0], E5, g1_quarters[q], q * P)
-        w2groups.append(group_w2(on_vector, w2r[1][1], group_at(54, "w2group11")))
         quantize(gq[1, 1], E5, g11)
-        second_block = cast_block(26, 1, 0, 1, plain(on_vector))
+        w2groups = [group_w2(on_vector, w2r[1][b], group_at((48.25, 54)[b], "w2group1%d" % b)) for b in range(HB)]
+        w2q.append([quantize(mx_pair("w2q10"), E4, w2groups[0][:])])
+        second_block = cast_block(W2RAW1_AT, 1, 0, 1, plain(on_vector))
         w2q[1].append(quantize(mx_pair("w2q11"), E4, w2groups[1][:]))
         quantize_block(1, 0, 1, second_block)
-        first_block = cast_block(26, 1, 0, 0, on_gpsimd)
+        first_block = cast_block(W2RAW1_AT, 1, 0, 0, on_gpsimd)
         pair_s([stage_s(kt, 0) for kt in (4, 5)])
-        groups = relu_half(1, 0, 49)
+        groups = relu_half(1, 0, 54)
         quantize_block(1, 0, 0, first_block)
         quantize_da(1, 0, groups)
         pair_s([stage_s(kt, 1, 0, HALF) for kt in range(2)])
-        first_block = cast_block(26, 1, 1, 0, on_gpsimd)
-        quantize_da(1, 1, relu_half(1, 1, 49))
-        second_block = cast_block(49, 1, 1, 1, plain(on_vector))
+        first_block = cast_block(W2RAW1_AT, 1, 1, 0, on_gpsimd)
+        quantize_da(1, 1, relu_half(1, 1, 54))
+        second_block = cast_block(54, 1, 1, 1, plain(on_vector))
         quantize_block(1, 1, 0, first_block)
         quantize_block(1, 1, 1, second_block)
-        halves = [stage_v(51 + kt, kt, 1, HALF, C) for kt in range(2)]
-        w1group = gpsimd_chunk(1, 2, 47)
+        halves = [stage_v(56 + kt, kt, 1, HALF, C) for kt in range(2)]
+        w1group = gpsimd_chunk(1, 2, 52)
         r2, r3, r3_last = stage_s(2, 1, 0, HALF), stage_s(3, 1, 0, HALF), stage_s(3, 1, HALF, C)
         for kt in range(2):
             scatter_v(halves[kt])

@@ -68,7 +68,8 @@ def tile_moe_bdx_mlp_relu_kernel(tc, dyT, a, w2, w1, gate, offs, out):
             return keep.tile([P, 4 * C], BF16, name=name, bufs=bufs, align_bytes=64)
 
         def group_w2(copy, raw, dst, m0=0, m1=P):
-            copy(dst[:].rearrange("p (t m j) -> p m j t", t=4, j=4)[:, m0:m1], raw.rearrange("p j (m t) -> p m j t", t=4)[:, m0:m1])
+            for t0 in (0, 2):
+                copy(dst[:].rearrange("p (t m j) -> p m j t", t=4, j=4)[:, m0:m1, :, t0:t0 + 2], raw.rearrange("p j (m t) -> p m j t", t=4)[:, m0:m1, :, t0:t0 + 2])
             return dst
 
         def mx_pair(name, width=C, scales_kb=None):

@@ -30,7 +30,7 @@ HALF = C // 2
 KB = 1024
 W2RAW_AT = 108
 W2RAW1_AT = 124
-HELD_SCALES = {(1, 0): 80}
+HELD_SCALES = {(0, 1): 36, (1, 0): 80}
 LAST_ON_VECTOR = 128
 W2_ON_SCALAR = (44, 72)
 
@@ -213,7 +213,7 @@ def tile_moe_bdx_mlp_relu_kernel(tc, dyT, a, w2, w1, gate, offs, out):
             return at(kb, [4 * C], BF16, name)
 
         g_planes = [at(16 + 8 * e, [4 * C], F32, "g%d" % e) for e in range(E)]
-        gates = [at(34, [C], F32, "gate0"), keep.tile([P, C], F32, name="gate1")]
+        gates = [at(34, [C], F32, "gate0"), at(W2RAW_AT + 4, [C], F32, "gate1")]
 
         def copy_gates(copy, e):
             copy(gates[e][:].rearrange("p (n m) -> p n m", m=4), gate_banks[e][:].rearrange("p (m n) -> p n m", m=4))
@@ -224,17 +224,18 @@ def tile_moe_bdx_mlp_relu_kernel(tc, dyT, a, w2, w1, gate, offs, out):
             nc.scalar.activation(out=g_planes[1][:, t * C:(t + 1) * C], in_=dy[t][:].indirect(slots_of(1)), func=COPY)
         gq = {(e, h): mx_pair("gq%d%d" % (e, h), HALF, HELD_SCALES.get((e, h))) for e in range(E) for h in range(2)}
 
-        copy_gates(on_scalar, 1)
         g0_groups = [at(48 + 2 * h, [4 * HALF], BF16, "ggroup0%d" % h) for h in range(2)]
-        for h in range(2):
-            interleave(on_vector, words(g0_groups[h][:]), planes(g_planes[0][:])[:, :, h * HALF:(h + 1) * HALF])
-        for h in range(2):
-            quantize(gq[0, h], E5, g0_groups[h][:])
+        for h, copy in enumerate((on_vector, on_scalar)):
+            interleave(copy, words(g0_groups[h][:]), planes(g_planes[0][:])[:, :, h * HALF:(h + 1) * HALF])
+        quantize(gq[0, 0], E5, g0_groups[0][:])
         w2groups = [group_at(35.75 + 4.25 * b, "w2group0%d" % b) for b in range(HB)]
         for b in range(HB):
             group_w2(on_scalar, w2r[0][b], w2groups[b], 0, W2_ON_SCALAR[b])
             group_w2(on_vector, w2r[0][b], w2groups[b], W2_ON_SCALAR[b], P)
-        w2q = [[quantize(mx_pair("w2q0%d" % b), E4, w2groups[b][:]) for b in range(HB)]]
+        copy_gates(on_scalar, 1)
+        w2q = [[quantize(mx_pair("w2q00"), E4, w2groups[0][:])]]
+        quantize(gq[0, 1], E5, g0_groups[1][:])
+        w2q[0].append(quantize(mx_pair("w2q01"), E4, w2groups[1][:]))
 
         def gate_on_gpsimd(s0, kb):
             dst = at(kb, [P, 4], BF16, "ggroup1_%d" % s0)

@@ -26,13 +26,22 @@ PASS = 512
 HB = H // PASS
 KT = K // P
 KC = 2 * P
+CHUNKS = K // KC
 HALF = C // 2
-KB = 1024
-W2RAW_AT = 108
-W2RAW1_AT = 124
-HELD_SCALES = {(0, 1): 36, (1, 0): 80}
-LAST_ON_VECTOR = 128
+
 W2_ON_SCALAR = (44, 72)
+LAST_ON_VECTOR = 128
+
+KB = 1024
+EDGE = 0.25
+PLANES_AT = (16, 24)
+GATE0_AT = 34
+W2GROUP_AT = (GATE0_AT + 2 - EDGE, 40)
+CHUNK0_AT = 44
+G0GROUP_AT = 48
+RING_AT = 52
+W1RAW_AT = 60
+W2RAW_AT = (108, 124)
 
 
 def tile_moe_bdx_mlp_relu_kernel(tc, dyT, a, w2, w1, gate, offs, out):
@@ -44,6 +53,15 @@ def tile_moe_bdx_mlp_relu_kernel(tc, dyT, a, w2, w1, gate, offs, out):
 
         def at(kb, shape, dtype, name):
             return placed.tile([P] + shape, dtype, name=name, offset=int(kb * KB), align_bytes=64)
+
+        def group_at(kb, name):
+            return at(kb, [4 * C], BF16, name)
+
+        def w1raw_at(e, c, b):
+            return W1RAW_AT + 4 * (HB * (CHUNKS * e + c) + b)
+
+        def by_planes(rows):
+            return rows.rearrange("(p t) c -> p t c", t=4)
 
         def planes(ap):
             return ap.rearrange("p (t c) -> p t c", t=4)
@@ -61,15 +79,22 @@ def tile_moe_bdx_mlp_relu_kernel(tc, dyT, a, w2, w1, gate, offs, out):
             nc.vector.tensor_copy(out=dst, in_=src)
 
         def interleave(copy, dst, src):
-            dst_view, src_view = four_neighbours(dst, src)
-            copy(dst_view, src_view)
+            copy(*four_neighbours(dst, src))
 
-        def grouped_tile(name, bufs):
-            return keep.tile([P, 4 * C], BF16, name=name, bufs=bufs, align_bytes=64)
+        def interleave_on_scalar(dst, src):
+            interleave(on_scalar, dst, src)
+
+        def interleave_on_vector(dst, src):
+            interleave(on_vector, dst, src)
+
+        def interleave_on_gpsimd(dst, src):
+            nc.gpsimd.tensor_scalar(out=dst, in0=src.rearrange("p t c -> p c t"), scalar1=1.0, scalar2=0.0, op0=MULT, op1=ADD)
 
         def group_w2(copy, raw, dst, m0=0, m1=P):
+            dst_view = dst[:].rearrange("p (t m j) -> p m j t", t=4, j=4)
+            raw_view = raw.rearrange("p j (m t) -> p m j t", t=4)
             for t0 in (0, 2):
-                copy(dst[:].rearrange("p (t m j) -> p m j t", t=4, j=4)[:, m0:m1, :, t0:t0 + 2], raw.rearrange("p j (m t) -> p m j t", t=4)[:, m0:m1, :, t0:t0 + 2])
+                copy(dst_view[:, m0:m1, :, t0:t0 + 2], raw_view[:, m0:m1, :, t0:t0 + 2])
             return dst
 
         def mx_pair(name, width=C, scales_kb=None):
@@ -89,153 +114,26 @@ def tile_moe_bdx_mlp_relu_kernel(tc, dyT, a, w2, w1, gate, offs, out):
             nc.sync.dma_start(out=raw[:], in_=view)
             return raw
 
-        def w1raw_at(e, c, b):
-            return 60 + 4 * (HB * (3 * e + c) + b)
-
-        def by_planes(rows):
-            return rows.rearrange("(p t) c -> p t c", t=4)
-
         def load_dy(t):
             return load("dy%d" % t, by_planes(dyT)[:, t, :], 4 * t)
 
-        def load_w2(e, b):
-            return load("w2raw%d%d" % (e, b), by_planes(w2[e, :, b * PASS:(b + 1) * PASS]))
+        def load_w2(e):
+            whole = load("w2raw%d" % e, by_planes(w2[e]), W2RAW_AT[e])
+            w2raw[e] = [whole[:, :, b * PASS:(b + 1) * PASS] for b in range(HB)]
 
-        def load_a(e, b, s0, s1):
-            return load("a%d%d_%d" % (e, b, s0), by_planes(a[b * PASS:(b + 1) * PASS, e * C + s0:e * C + s1]))
+        def load_a(e, h, b):
+            s0 = e * C + h * HALF
+            a_raw[e, h, b] = load("a%d%d_%d" % (e, b, h * HALF), by_planes(a[b * PASS:(b + 1) * PASS, s0:s0 + HALF]))
 
-        def load_w1(e, b, c0, c1):
-            return load("w1raw%d%d_%d" % (e, b, c0), by_planes(w1[e, b * PASS:(b + 1) * PASS, c0:c1]), w1raw_at(e, c0 // KC, b))
+        def load_w1(e, c, b):
+            view = by_planes(w1[e, b * PASS:(b + 1) * PASS, c * KC:(c + 1) * KC])
+            w1raw[e, c, b] = load("w1raw%d%d_%d" % (e, b, c * KC), view, w1raw_at(e, c, b))
 
         def slots_of(e, s0=0, s1=C):
             return offs_t[:, (e * C + s0) // 16:(e * C + s1) // 16]
 
-        def relu_products(w2q, gq, a_part, grouped):
-            for s0 in range(0, HALF, P):
-                bank = psum.tile([P, 4, P], F32, name="dh", bufs=4)
-                for t in range(4):
-                    nc.tensor.matmul_mx(out=bank[:, t, :], lhsT=w2q[0][:, t * P:(t + 1) * P].bitcast(E4), lhsT_scale=w2q[1][:, t * P:(t + 1) * P],
-                                        rhs=gq[0][:, s0:s0 + P].bitcast(E5), rhs_scale=gq[1][:, s0:s0 + P], start=True, stop=True)
-                nc.vector.scalar_tensor_tensor(out=words(grouped[:])[:, s0:s0 + P, :], in0=a_part[:, s0:s0 + P, :], scalar=0.0,
-                                               in1=bank[:].rearrange("p t c -> p c t"), op0=IS_GT, op1=MULT)
-            return grouped
-
-        def plain(copy):
-            return lambda dst, src: interleave(copy, dst, src)
-
-        def on_gpsimd(dst, src):
-            nc.gpsimd.tensor_scalar(out=dst, in0=src.rearrange("p t c -> p c t"), scalar1=1.0, scalar2=0.0, op0=MULT, op1=ADD)
-
-        def cast_block(kb, e, c, b, cast):
-            dst = at(kb, [4 * KC], BF16, "w1group%d%d%d" % (e, c, b))
-            cast(words(dst[:]), w1r[e, c][b][:])
-            return dst
-
-        def quantize_block(e, c, b, grouped):
-            quantize(w1q[e][c], E4, grouped[:], b * KC)
-
-        def dx_bank(parts, daq, s0, s1):
-            bank = psum.tile([P, C], F32, name="dx", bufs=4)
-            cuts = [s0, s1 - HALF, s1] if s1 - s0 == 3 * P else [s0, s1]
-            for first, last in zip(cuts, cuts[1:]):
-                for b in range(HB):
-                    codes, scales, c0 = parts[b]
-                    nc.tensor.matmul_mx(out=bank[:, first - s0:last - s0], lhsT=codes[:, c0:c0 + P].bitcast(E4), lhsT_scale=scales[:, c0:c0 + P],
-                                        rhs=daq[b][0][:, first:last].bitcast(E5), rhs_scale=daq[b][1][:, first:last], start=(b == 0), stop=(b == HB - 1))
-            return bank
-
-        def chunk_parts(w1q, u):
-            return [(w1q[0], w1q[1], b * KC + u * P) for b in range(HB)]
-
-        def result_bank(kt, e, s0=0, s1=C):
-            return kt, e, s0, dx_bank(chunk_parts(w1q[e][kt // 2], kt % 2), daq[e], s0, s1)
-
-        def stage(copy, result, s0, s1, kb):
-            kt, e, first, bank = result
-            staged = keep.tile([P, C], F32, name="staged", bufs=3) if kb is None else at(kb, [s1 - s0], F32, "staged%d%d_%d" % (e, kt, s0))
-            copy(staged[:, 0:s1 - s0], bank[:, s0 - first:s1 - first])
-            return kt, e, s0, s1, staged
-
-        def stage_s(kt, e, s0=0, s1=C):
-            return stage(on_scalar, result_bank(kt, e, s0, s1), s0, s1, None)
-
-        def stage_v(kb, kt, e, s0=0, s1=C):
-            return stage(on_vector, result_bank(kt, e, s0, s1), s0, s1, kb)
-
-        def scatter_s(result, s0=None, s1=None):
-            kt, e, first, last, staged = result
-            s0, s1 = (first, last) if s0 is None else (s0, s1)
-            nc.scalar.activation(out=windows[kt][:].indirect(slots_of(e, s0, s1)), in_=staged[:, s0 - first:s1 - first], func=COPY)
-
-        def scatter_v(result, s0=None, s1=None):
-            kt, e, first, last, staged = result
-            s0, s1 = (first, last) if s0 is None else (s0, s1)
-            nc.vector.tensor_copy(out=windows[kt][:].indirect(slots_of(e, s0, s1)), in_=staged[:, s0 - first:s1 - first])
-
-        def store(kt, queue=nc.sync):
-            queue.dma_start(out=out[kt * P:(kt + 1) * P, :], in_=windows[kt][:])
-
-        ident = keep.tile([P, P], F32, name="ident")
-        make_identity(nc, ident[:])
-        gate_row = load("gate_row", gate[0, :].rearrange("(e n m) -> n e m", e=E, m=4))
-        dy = {0: load_dy(0)}
-        offs_t = keep.tile([P, E * C // 16], U16, name="offs_t")
-        nc.sync.dma_start(offs_t[:], offs)
-        for t in range(1, 4):
-            dy[t] = load_dy(t)
-        gate_banks = {}
-        for e in range(E):
-            gate_banks[e] = psum.tile([P, C], F32, name="dx", bufs=4)
-            for m in range(4):
-                nc.tensor.transpose(gate_banks[e][:, m * P:(m + 1) * P], gate_row[:, e, m:m + 1].to_broadcast([P, P]), ident[:])
-        w2r, a_half, w1r = {}, {}, {}
-
-        def load_group(kind, e, i):
-            if kind == "w2":
-                whole = load("w2raw%d" % e, by_planes(w2[e]), W2RAW1_AT if e else W2RAW_AT)
-                w2r[e] = [whole[:, :, b * PASS:(b + 1) * PASS] for b in range(HB)]
-            elif kind == "a":
-                a_half[e, i] = [load_a(e, b, i * HALF, (i + 1) * HALF) for b in range(HB)]
-            else:
-                w1r[e, i] = [load_w1(e, b, i * KC, (i + 1) * KC) for b in range(HB)]
-
-        for kind, e, i in (("w2", 0, 0), ("a", 0, 0), ("w1", 0, 0), ("a", 0, 1), ("w1", 0, 1), ("w1", 0, 2), ("w2", 1, 0)):
-            load_group(kind, e, i)
-        w1r[1, 0] = [load_w1(1, b, 0, KC) for b in (1, 0)][::-1]
-        load_group("a", 1, 0)
-        a_half[1, 1], w1r[1, 1] = [], []
-        for b in range(HB):
-            a_half[1, 1].append(load_a(1, b, HALF, C))
-            w1r[1, 1].append(load_w1(1, b, KC, 2 * KC))
-        load_group("w1", 1, 2)
-
-        def group_at(kb, name):
-            return at(kb, [4 * C], BF16, name)
-
-        g_planes = [at(16 + 8 * e, [4 * C], F32, "g%d" % e) for e in range(E)]
-        gates = [at(34, [C], F32, "gate0"), at(W2RAW_AT + 4, [C], F32, "gate1")]
-
         def copy_gates(copy, e):
             copy(gates[e][:].rearrange("p (n m) -> p n m", m=4), gate_banks[e][:].rearrange("p (m n) -> p n m", m=4))
-
-        copy_gates(on_vector, 0)
-        for t in range(4):
-            nc.vector.tensor_tensor(g_planes[0][:, t * C:(t + 1) * C], dy[t][:].indirect(slots_of(0)), gates[0][:], MULT)
-            nc.scalar.activation(out=g_planes[1][:, t * C:(t + 1) * C], in_=dy[t][:].indirect(slots_of(1)), func=COPY)
-        gq = {(e, h): mx_pair("gq%d%d" % (e, h), HALF, HELD_SCALES.get((e, h))) for e in range(E) for h in range(2)}
-
-        g0_groups = [at(48 + 2 * h, [4 * HALF], BF16, "ggroup0%d" % h) for h in range(2)]
-        for h, copy in enumerate((on_vector, on_scalar)):
-            interleave(copy, words(g0_groups[h][:]), planes(g_planes[0][:])[:, :, h * HALF:(h + 1) * HALF])
-        quantize(gq[0, 0], E5, g0_groups[0][:])
-        w2groups = [group_at(35.75 + 4.25 * b, "w2group0%d" % b) for b in range(HB)]
-        for b in range(HB):
-            group_w2(on_scalar, w2r[0][b], w2groups[b], 0, W2_ON_SCALAR[b])
-            group_w2(on_vector, w2r[0][b], w2groups[b], W2_ON_SCALAR[b], P)
-        copy_gates(on_scalar, 1)
-        w2q = [[quantize(mx_pair("w2q00"), E4, w2groups[0][:])]]
-        quantize(gq[0, 1], E5, g0_groups[1][:])
-        w2q[0].append(quantize(mx_pair("w2q01"), E4, w2groups[1][:]))
 
         def gate_on_gpsimd(s0, kb):
             dst = at(kb, [P, 4], BF16, "ggroup1_%d" % s0)
@@ -243,102 +141,210 @@ def tile_moe_bdx_mlp_relu_kernel(tc, dyT, a, w2, w1, gate, offs, out):
                                     gates[1][:, s0:s0 + P].unsqueeze(2).to_broadcast([P, P, 4]), MULT)
             return dst[:].rearrange("p c t -> p (c t)")
 
-        g1_quarters = [gate_on_gpsimd(0, 40)]
-        windows = [at(4 * kt, [T], F32, "window%d" % kt) for kt in range(KT)]
-        daq = [[mx_pair("daq%d%d" % (e, b)) for b in range(HB)] for e in range(E)]
-
-        w1q = [[mx_pair("w1q%d%d" % (e, c)) for c in range(3)] for e in range(E)]
-
         def relu_half(e, h, kb):
-            return [relu_products(w2q[e][b], gq[e, h], a_words[e, h, b], at(kb + 2 * b, [4 * HALF], BF16, "dagroup%d%d%d" % (e, h, b))) for b in range(HB)]
+            groups = []
+            for b in range(HB):
+                groups.append(at(kb + 2 * b, [4 * HALF], BF16, "dagroup%d%d%d" % (e, h, b)))
+                w_codes, w_scales = w2q[e][b]
+                g_codes, g_scales = gq[e, h]
+                for s0 in range(0, HALF, P):
+                    bank = psum.tile([P, 4, P], F32, name="dh", bufs=4)
+                    for t in range(4):
+                        nc.tensor.matmul_mx(out=bank[:, t, :], lhsT=w_codes[:, t * P:(t + 1) * P].bitcast(E4),
+                                            lhsT_scale=w_scales[:, t * P:(t + 1) * P], rhs=g_codes[:, s0:s0 + P].bitcast(E5),
+                                            rhs_scale=g_scales[:, s0:s0 + P], start=True, stop=True)
+                    nc.vector.scalar_tensor_tensor(out=words(groups[b][:])[:, s0:s0 + P, :], in0=a_words[e, h, b][:, s0:s0 + P, :],
+                                                   scalar=0.0, in1=bank[:].rearrange("p t c -> p c t"), op0=IS_GT, op1=MULT)
+            return groups
 
         def quantize_da(e, h, groups):
             for b in range(HB):
                 quantize(daq[e][b], E5, groups[b][:], h * HALF)
 
-        def gpsimd_chunk(e, c, kb, width=KC):
-            dst = group_at(kb, "w1group%d%d" % (e, c))
-            on_gpsimd(words(dst[:])[:, 0:KC, :], w1r[e, c][0][:])
-            on_gpsimd(words(dst[:])[:, KC:KC + width, :], w1r[e, c][1][:, :, 0:width])
+        def cast_block(kb, e, c, b, cast):
+            dst = at(kb, [4 * KC], BF16, "w1group%d%d%d" % (e, c, b))
+            cast(words(dst[:]), w1raw[e, c, b][:])
             return dst
 
-        def pair_s(results):
-            for s in range(results[0][2], results[0][3], HALF):
-                for r in results:
-                    scatter_s(r, s, s + HALF)
+        def gpsimd_chunk(e, c, kb, width=KC):
+            dst = group_at(kb, "w1group%d%d" % (e, c))
+            interleave_on_gpsimd(words(dst[:])[:, 0:KC, :], w1raw[e, c, 0][:])
+            interleave_on_gpsimd(words(dst[:])[:, KC:KC + width, :], w1raw[e, c, 1][:, :, 0:width])
+            return dst
 
-        a_words = {(e, h, b): a_half[e, h][b][:].rearrange("p t c -> p c t") for e in range(E) for h in range(2) for b in range(HB)}
-        signs = at(W2RAW_AT + 2, [HALF, 4], BF16, "signs")
-        dst_view, src_view = four_neighbours(signs[:], a_half[0, 0][1][:])
+        def quantize_block(e, c, b, grouped):
+            quantize(w1q[e][c], E4, grouped[:], b * KC)
+
+        def result_bank(kt, e, s0, s1):
+            bank = psum.tile([P, C], F32, name="dx", bufs=4)
+            w_codes, w_scales = w1q[e][kt // 2]
+            for b in range(HB):
+                c0 = b * KC + kt % 2 * P
+                nc.tensor.matmul_mx(out=bank[:, 0:s1 - s0], lhsT=w_codes[:, c0:c0 + P].bitcast(E4), lhsT_scale=w_scales[:, c0:c0 + P],
+                                    rhs=daq[e][b][0][:, s0:s1].bitcast(E5), rhs_scale=daq[e][b][1][:, s0:s1],
+                                    start=(b == 0), stop=(b == HB - 1))
+            return kt, e, s0, bank
+
+        def stage(copy, result, s0, s1, kb=None):
+            kt, e, first, bank = result
+            if kb is None:
+                staged = keep.tile([P, C], F32, name="staged", bufs=3)
+            else:
+                staged = at(kb, [s1 - s0], F32, "staged%d%d_%d" % (e, kt, s0))
+            copy(staged[:, 0:s1 - s0], bank[:, s0 - first:s1 - first])
+            return kt, e, s0, s1, staged
+
+        def stage_on_scalar(kt, e, s0=0, s1=C):
+            return stage(on_scalar, result_bank(kt, e, s0, s1), s0, s1)
+
+        def stage_on_vector(kb, kt, e, s0=0, s1=C):
+            return stage(on_vector, result_bank(kt, e, s0, s1), s0, s1, kb)
+
+        def scatter_on_scalar(*results):
+            first, last = results[0][2:4]
+            for s0 in range(first, last, HALF):
+                s1 = min(s0 + HALF, last)
+                for kt, e, _, _, staged in results:
+                    nc.scalar.activation(out=windows[kt][:].indirect(slots_of(e, s0, s1)), in_=staged[:, s0 - first:s1 - first], func=COPY)
+
+        def scatter_on_vector(result):
+            kt, e, s0, s1, staged = result
+            nc.vector.tensor_copy(out=windows[kt][:].indirect(slots_of(e, s0, s1)), in_=staged[:, 0:s1 - s0])
+
+        def store(kt, queue=nc.sync):
+            queue.dma_start(out=out[kt * P:(kt + 1) * P, :], in_=windows[kt][:])
+
+        ident = keep.tile([P, P], F32, name="ident")
+        make_identity(nc, ident[:])
+        gate_row = load("gate_row", gate[0, :].rearrange("(e n m) -> n e m", e=E, m=4))
+        dy = [load_dy(0)]
+        offs_t = keep.tile([P, E * C // 16], U16, name="offs_t")
+        nc.sync.dma_start(offs_t[:], offs)
+        dy += [load_dy(t) for t in range(1, 4)]
+        gate_banks = []
+        for e in range(E):
+            gate_banks.append(psum.tile([P, C], F32, name="dx", bufs=4))
+            for m in range(4):
+                nc.tensor.transpose(gate_banks[e][:, m * P:(m + 1) * P], gate_row[:, e, m:m + 1].to_broadcast([P, P]), ident[:])
+        w2raw, a_raw, w1raw = {}, {}, {}
+        load_w2(0)
+        for load_part, i in ((load_a, 0), (load_w1, 0), (load_a, 1), (load_w1, 1), (load_w1, 2)):
+            for b in range(HB):
+                load_part(0, i, b)
+        load_w2(1)
+        for b in (1, 0):
+            load_w1(1, 0, b)
+        for b in range(HB):
+            load_a(1, 0, b)
+        for b in range(HB):
+            load_a(1, 1, b)
+            load_w1(1, 1, b)
+        for b in range(HB):
+            load_w1(1, 2, b)
+
+        g_planes = [at(PLANES_AT[e], [4 * C], F32, "g%d" % e) for e in range(E)]
+        gates = [at(GATE0_AT, [C], F32, "gate0"), at(W2RAW_AT[0] + 4, [C], F32, "gate1")]
+        copy_gates(on_vector, 0)
+        for t in range(4):
+            nc.vector.tensor_tensor(g_planes[0][:, t * C:(t + 1) * C], dy[t][:].indirect(slots_of(0)), gates[0][:], MULT)
+            nc.scalar.activation(out=g_planes[1][:, t * C:(t + 1) * C], in_=dy[t][:].indirect(slots_of(1)), func=COPY)
+        held_scales = {(0, 1): W2GROUP_AT[0] + EDGE, (1, 0): w1raw_at(0, CHUNKS - 1, 1)}
+        gq = {(e, h): mx_pair("gq%d%d" % (e, h), HALF, held_scales.get((e, h))) for e in range(E) for h in range(2)}
+        g0_groups = [at(G0GROUP_AT + 2 * h, [4 * HALF], BF16, "ggroup0%d" % h) for h in range(2)]
+        for h, copy in enumerate((on_vector, on_scalar)):
+            interleave(copy, words(g0_groups[h][:]), planes(g_planes[0][:])[:, :, h * HALF:(h + 1) * HALF])
+        quantize(gq[0, 0], E5, g0_groups[0][:])
+        w2groups = [group_at(W2GROUP_AT[b], "w2group0%d" % b) for b in range(HB)]
+        for b in range(HB):
+            group_w2(on_scalar, w2raw[0][b], w2groups[b], 0, W2_ON_SCALAR[b])
+            group_w2(on_vector, w2raw[0][b], w2groups[b], W2_ON_SCALAR[b], P)
+        copy_gates(on_scalar, 1)
+        w2q = [[quantize(mx_pair("w2q00"), E4, w2groups[0][:])]]
+        quantize(gq[0, 1], E5, g0_groups[1][:])
+        w2q[0].append(quantize(mx_pair("w2q01"), E4, w2groups[1][:]))
+        g1_quarters = [gate_on_gpsimd(0, W2GROUP_AT[1])]
+        windows = [at(4 * kt, [T], F32, "window%d" % kt) for kt in range(KT)]
+        daq = [[mx_pair("daq%d%d" % (e, b)) for b in range(HB)] for e in range(E)]
+        w1q = [[mx_pair("w1q%d%d" % (e, c)) for c in range(CHUNKS)] for e in range(E)]
+
+        a_words = {key: raw[:].rearrange("p t c -> p c t") for key, raw in a_raw.items()}
+        signs = at(W2RAW_AT[0] + 2, [HALF, 4], BF16, "signs")
+        dst_view, src_view = four_neighbours(signs[:], a_raw[0, 0, 1][:])
         nc.scalar.activation(out=dst_view, in_=src_view, func=SIGN)
         a_words[0, 0, 1] = signs[:]
-        groups = relu_half(0, 0, 52)
-        quantize_da(0, 0, groups)
-        quantize_block(0, 0, 0, cast_block(44, 0, 0, 0, plain(on_scalar)))
-        last_group = at(46, [4 * KC], BF16, "w1group001")
+        quantize_da(0, 0, relu_half(0, 0, RING_AT))
+        quantize_block(0, 0, 0, cast_block(CHUNK0_AT, 0, 0, 0, interleave_on_scalar))
+        by_tiles = at(CHUNK0_AT + 2, [4 * KC], BF16, "w1group001")
         for u in range(2):
-            interleave(on_scalar, words(last_group[:])[:, u * P:(u + 1) * P, :], w1r[0, 0][1][:, :, u * P:(u + 1) * P])
-            quantize(w1q[0][0], E4, last_group[:, 4 * u * P:4 * (u + 1) * P], KC + u * P)
-        g1_quarters.append(gate_on_gpsimd(P, 46))
-        pair_s([stage_s(kt, 0, 0, HALF) for kt in range(2)])
-        quantize_da(0, 1, relu_half(0, 1, 52))
+            interleave_on_scalar(words(by_tiles[:])[:, u * P:(u + 1) * P, :], w1raw[0, 0, 1][:, :, u * P:(u + 1) * P])
+            quantize(w1q[0][0], E4, by_tiles[:, 4 * u * P:4 * (u + 1) * P], KC + u * P)
+        g1_quarters.append(gate_on_gpsimd(P, CHUNK0_AT + 2))
+        scatter_on_scalar(*[stage_on_scalar(kt, 0, 0, HALF) for kt in range(2)])
+
+        quantize_da(0, 1, relu_half(0, 1, RING_AT))
         bank0 = result_bank(0, 0, HALF, C)
-        scatter_s(stage(on_scalar, bank0, HALF, C - P, None))
-        groups = [cast_block(52 + 2 * b, 0, 1, b, plain(on_vector)) for b in range(HB)]
+        scatter_on_scalar(stage(on_scalar, bank0, HALF, C - P))
+        blocks = [cast_block(RING_AT + 2 * b, 0, 1, b, interleave_on_vector) for b in range(HB)]
         for b in range(HB):
-            quantize_block(0, 1, b, groups[b])
-        r1 = stage_v(52, 1, 0, HALF, C)
-        r0 = stage(on_vector, bank0, C - P, C, 53.5)
-        w1group = gpsimd_chunk(0, 2, 54, KC - LAST_ON_VECTOR)
-        scatter_v(r1)
-        scatter_v(r0)
-        held = at(49.25, [4 * (HALF + LAST_ON_VECTOR)], BF16, "ggroup11_and_rest")
+            quantize_block(0, 1, b, blocks[b])
+        result1 = stage_on_vector(RING_AT, 1, 0, HALF, C)
+        result0 = stage(on_vector, bank0, C - P, C, RING_AT + 1.5)
+        chunk = gpsimd_chunk(0, 2, RING_AT + 2, KC - LAST_ON_VECTOR)
+        scatter_on_vector(result1)
+        scatter_on_vector(result0)
+        held = at(RING_AT + EDGE - 3, [4 * (HALF + LAST_ON_VECTOR)], BF16, "ggroup11_and_rest")
         g11, rest = held[:, 0:4 * HALF], held[:, 4 * HALF:]
         dst_view, src_view = four_neighbours(words(g11), planes(g_planes[1][:])[:, :, HALF:C])
-        nc.vector.tensor_tensor(dst_view, src_view, gates[1][:, HALF:C].rearrange("p (c i) -> p c i", i=4).unsqueeze(2).to_broadcast([P, HALF // 4, 4, 4]), MULT)
-        interleave(on_vector, words(rest), w1r[0, 2][1][:, :, KC - LAST_ON_VECTOR:KC])
-        quantize(w1q[0][2], E4, w1group[:, 0:4 * KC])
-        quantize(w1q[0][2], E4, w1group[:, 4 * KC:6 * KC], KC)
-        quantize(w1q[0][2], E4, rest, C - LAST_ON_VECTOR)
-        pair_s([stage_s(kt, 0) for kt in (2, 3)])
+        gate_view = gates[1][:, HALF:C].rearrange("p (c i) -> p c i", i=4).unsqueeze(2).to_broadcast([P, HALF // 4, 4, 4])
+        nc.vector.tensor_tensor(dst_view, src_view, gate_view, MULT)
+        interleave_on_vector(words(rest), w1raw[0, 2, 1][:, :, KC - LAST_ON_VECTOR:KC])
+        quantize_block(0, 2, 0, chunk[:, 0:4 * KC])
+        quantize_block(0, 2, 1, chunk[:, 4 * KC:4 * (2 * KC - LAST_ON_VECTOR)])
+        quantize(w1q[0][2], E4, rest, 2 * KC - LAST_ON_VECTOR)
+        scatter_on_scalar(*[stage_on_scalar(kt, 0) for kt in (2, 3)])
 
         for q in range(2):
             quantize(gq[1, 0], E5, g1_quarters[q], q * P)
         quantize(gq[1, 1], E5, g11)
-        w2groups = [group_w2(on_vector, w2r[1][b], group_at((48.25, 54)[b], "w2group1%d" % b)) for b in range(HB)]
+        w2groups = [group_w2(on_vector, w2raw[1][b], group_at(kb, "w2group1%d" % b))
+                    for b, kb in enumerate((RING_AT + EDGE - 4, RING_AT + 2))]
         w2q.append([quantize(mx_pair("w2q10"), E4, w2groups[0][:])])
-        second_block = cast_block(W2RAW1_AT, 1, 0, 1, plain(on_vector))
+        block1 = cast_block(W2RAW_AT[1], 1, 0, 1, interleave_on_vector)
         w2q[1].append(quantize(mx_pair("w2q11"), E4, w2groups[1][:]))
-        quantize_block(1, 0, 1, second_block)
-        first_block = cast_block(W2RAW1_AT, 1, 0, 0, on_gpsimd)
-        pair_s([stage_s(kt, 0) for kt in (4, 5)])
-        groups = relu_half(1, 0, 54)
-        quantize_block(1, 0, 0, first_block)
+        quantize_block(1, 0, 1, block1)
+        block0 = cast_block(W2RAW_AT[1], 1, 0, 0, interleave_on_gpsimd)
+        scatter_on_scalar(*[stage_on_scalar(kt, 0) for kt in (4, 5)])
+        groups = relu_half(1, 0, RING_AT + 2)
+        quantize_block(1, 0, 0, block0)
         quantize_da(1, 0, groups)
-        pair_s([stage_s(kt, 1, 0, HALF) for kt in range(2)])
-        first_block = cast_block(W2RAW1_AT, 1, 1, 0, on_gpsimd)
-        quantize_da(1, 1, relu_half(1, 1, 54))
-        second_block = cast_block(54, 1, 1, 1, plain(on_vector))
-        quantize_block(1, 1, 0, first_block)
-        quantize_block(1, 1, 1, second_block)
-        halves = [stage_v(56 + kt, kt, 1, HALF, C) for kt in range(2)]
-        w1group = gpsimd_chunk(1, 2, 52)
-        r2, r3, r3_last = stage_s(2, 1, 0, HALF), stage_s(3, 1, 0, HALF), stage_s(3, 1, HALF, C)
+        scatter_on_scalar(*[stage_on_scalar(kt, 1, 0, HALF) for kt in range(2)])
+
+        block0 = cast_block(W2RAW_AT[1], 1, 1, 0, interleave_on_gpsimd)
+        quantize_da(1, 1, relu_half(1, 1, RING_AT + 2))
+        block1 = cast_block(RING_AT + 2, 1, 1, 1, interleave_on_vector)
+        quantize_block(1, 1, 0, block0)
+        quantize_block(1, 1, 1, block1)
+        halves = [stage_on_vector(RING_AT + 4 + kt, kt, 1, HALF, C) for kt in range(2)]
+        chunk = gpsimd_chunk(1, 2, RING_AT)
+        result2, result3 = [stage_on_scalar(kt, 1, 0, HALF) for kt in (2, 3)]
+        bank3 = result_bank(3, 1, HALF, C)
+        result3_third = stage(on_scalar, bank3, HALF, C - P)
         for kt in range(2):
-            scatter_v(halves[kt])
+            scatter_on_vector(halves[kt])
             store(kt)
-        scatter_s(r2)
-        scatter_s(r3)
-        r2 = stage_v(w1raw_at(1, 2, 1), 2, 1, HALF, C)
-        quantize(w1q[1][2], E4, w1group[:])
-        scatter_v(r2)
+        scatter_on_scalar(result2, result3)
+        result2_last = stage_on_vector(w1raw_at(1, 2, 1), 2, 1, HALF, C)
+        quantize(w1q[1][2], E4, chunk[:])
+        result3_last = stage(on_vector, bank3, C - P, C, w1raw_at(1, 2, 1) + 1)
+        scatter_on_vector(result2_last)
         store(2)
-        scatter_s(r3_last)
+        scatter_on_scalar(result3_third)
+        scatter_on_vector(result3_last)
         store(3)
-        r4 = stage_v(w1raw_at(1, 1, 1), 4, 1)
-        r5 = [stage_s(5, 1, h * HALF, (h + 1) * HALF) for h in range(2)]
-        scatter_v(r4)
-        store(4)
-        for r in r5:
-            scatter_s(r)
+        halves = [stage_on_scalar(5, 1, h * HALF, (h + 1) * HALF) for h in range(2)]
+        result4 = stage_on_vector(w1raw_at(1, 1, 1), 4, 1)
+        for half in halves:
+            scatter_on_scalar(half)
         store(5, nc.scalar)
+        scatter_on_vector(result4)
+        store(4)

@@ -52,7 +52,7 @@ def tile_moe_bdx_mlp_relu_kernel(tc, dyT, a, w2, w1, gate, offs, out):
         psum = ctx.enter_context(tc.psum_pool(name="psum", bufs=1))
 
         def at(kb, shape, dtype, name):
-            return placed.tile([P] + shape, dtype, name=name, offset=int(kb * KB), align_bytes=64)
+            return placed.tile([P] + shape, dtype, name=name, offset=int(kb * KB), align_bytes=256)
 
         def group_at(kb, name):
             return at(kb, [4 * C], BF16, name)
@@ -110,7 +110,7 @@ def tile_moe_bdx_mlp_relu_kernel(tc, dyT, a, w2, w1, gate, offs, out):
 
         def load(name, view, kb=None):
             shape = list(view.shape[1:])
-            raw = keep.tile([P] + shape, F32, name=name) if kb is None else at(kb, shape, F32, name)
+            raw = keep.tile([P] + shape, F32, name=name, align_bytes=256) if kb is None else at(kb, shape, F32, name)
             nc.sync.dma_start(out=raw[:], in_=view)
             return raw
 

@@ -31,6 +31,7 @@ HALF = C // 2
 
 W2_ON_SCALAR = (44, 72)
 LAST_ON_VECTOR = 128
+SHARE3 = 160
 
 KB = 1024
 EDGE = 0.25
@@ -42,6 +43,8 @@ G0GROUP_AT = 48
 RING_AT = 52
 W1RAW_AT = 60
 W2RAW_AT = (108, 124)
+G10_AT = GATE0_AT + EDGE - 2
+CHUNK1_AT = 140
 
 
 def tile_moe_bdx_mlp_relu_kernel(tc, dyT, a, w2, w1, gate, offs, out):
@@ -188,7 +191,7 @@ def tile_moe_bdx_mlp_relu_kernel(tc, dyT, a, w2, w1, gate, offs, out):
         def stage(copy, result, s0, s1, kb=None):
             kt, e, first, bank = result
             if kb is None:
-                staged = keep.tile([P, C], F32, name="staged", bufs=3)
+                staged = keep.tile([P, C], F32, name="staged", bufs=4)
             else:
                 staged = at(kb, [s1 - s0], F32, "staged%d%d_%d" % (e, kt, s0))
             copy(staged[:, 0:s1 - s0], bank[:, s0 - first:s1 - first])
@@ -206,6 +209,10 @@ def tile_moe_bdx_mlp_relu_kernel(tc, dyT, a, w2, w1, gate, offs, out):
                 s1 = min(s0 + HALF, last)
                 for kt, e, _, _, staged in results:
                     nc.scalar.activation(out=windows[kt][:].indirect(slots_of(e, s0, s1)), in_=staged[:, s0 - first:s1 - first], func=COPY)
+
+        def scatter_part(result, s0, s1):
+            kt, e, first, last, staged = result
+            nc.scalar.activation(out=windows[kt][:].indirect(slots_of(e, s0, s1)), in_=staged[:, s0 - first:s1 - first], func=COPY)
 
         def scatter_on_vector(result):
             kt, e, s0, s1, staged = result
@@ -247,12 +254,17 @@ def tile_moe_bdx_mlp_relu_kernel(tc, dyT, a, w2, w1, gate, offs, out):
         copy_gates(on_vector, 0)
         for t in range(4):
             nc.vector.tensor_tensor(g_planes[0][:, t * C:(t + 1) * C], dy[t][:].indirect(slots_of(0)), gates[0][:], MULT)
-            nc.scalar.activation(out=g_planes[1][:, t * C:(t + 1) * C], in_=dy[t][:].indirect(slots_of(1)), func=COPY)
-        held_scales = {(0, 1): W2GROUP_AT[0] + EDGE, (1, 0): w1raw_at(0, CHUNKS - 1, 1)}
+            for s0, s1 in ((0, C),) if t < 3 else ((0, HALF), (HALF, C)):
+                nc.scalar.activation(out=g_planes[1][:, t * C + s0:t * C + s1], in_=dy[t][:].indirect(slots_of(1, s0, s1)), func=COPY)
+        held_scales = {(0, 1): W2GROUP_AT[0] + EDGE, (1, 0): CHUNK1_AT + 4 - EDGE, (1, 1): w1raw_at(0, CHUNKS - 1, 1) + 1}
         gq = {(e, h): mx_pair("gq%d%d" % (e, h), HALF, held_scales.get((e, h))) for e in range(E) for h in range(2)}
         g0_groups = [at(G0GROUP_AT + 2 * h, [4 * HALF], BF16, "ggroup0%d" % h) for h in range(2)]
         for h, copy in enumerate((on_vector, on_scalar)):
             interleave(copy, words(g0_groups[h][:]), planes(g_planes[0][:])[:, :, h * HALF:(h + 1) * HALF])
+        g10 = at(G10_AT, [4 * HALF], BF16, "ggroup10")
+        dst_view, src_view = four_neighbours(words(g10[:]), planes(g_planes[1][:])[:, :, 0:HALF])
+        gate_view = gate_banks[1][:].rearrange("p (i c) -> p c i", i=4)[:, 0:HALF // 4, :].unsqueeze(2).to_broadcast([P, HALF // 4, 4, 4])
+        nc.vector.tensor_tensor(dst_view, src_view, gate_view, MULT)
         quantize(gq[0, 0], E5, g0_groups[0][:])
         w2groups = [group_at(W2GROUP_AT[b], "w2group0%d" % b) for b in range(HB)]
         for b in range(HB):
@@ -262,52 +274,51 @@ def tile_moe_bdx_mlp_relu_kernel(tc, dyT, a, w2, w1, gate, offs, out):
         w2q = [[quantize(mx_pair("w2q00"), E4, w2groups[0][:])]]
         quantize(gq[0, 1], E5, g0_groups[1][:])
         w2q[0].append(quantize(mx_pair("w2q01"), E4, w2groups[1][:]))
-        g1_quarters = [gate_on_gpsimd(0, W2GROUP_AT[1])]
+        g1_quarters = [gate_on_gpsimd(HALF, W2GROUP_AT[1])]
         windows = [at(4 * kt, [T], F32, "window%d" % kt) for kt in range(KT)]
         daq = [[mx_pair("daq%d%d" % (e, b)) for b in range(HB)] for e in range(E)]
-        w1q = [[mx_pair("w1q%d%d" % (e, c)) for c in range(CHUNKS)] for e in range(E)]
+        w1q = [[mx_pair("w1q%d%d" % (e, c), C, CHUNK1_AT + 1 + EDGE if (e, c) == (0, 2) else None) for c in range(CHUNKS)] for e in range(E)]
 
         a_words = {key: raw[:].rearrange("p t c -> p c t") for key, raw in a_raw.items()}
         signs = at(W2RAW_AT[0] + 2, [HALF, 4], BF16, "signs")
         dst_view, src_view = four_neighbours(signs[:], a_raw[0, 0, 1][:])
         nc.scalar.activation(out=dst_view, in_=src_view, func=SIGN)
         a_words[0, 0, 1] = signs[:]
-        quantize_da(0, 0, relu_half(0, 0, RING_AT))
+        quantize_da(0, 0, relu_half(0, 0, CHUNK1_AT))
         quantize_block(0, 0, 0, cast_block(CHUNK0_AT, 0, 0, 0, interleave_on_scalar))
         by_tiles = at(CHUNK0_AT + 2, [4 * KC], BF16, "w1group001")
         for u in range(2):
             interleave_on_scalar(words(by_tiles[:])[:, u * P:(u + 1) * P, :], w1raw[0, 0, 1][:, :, u * P:(u + 1) * P])
             quantize(w1q[0][0], E4, by_tiles[:, 4 * u * P:4 * (u + 1) * P], KC + u * P)
-        g1_quarters.append(gate_on_gpsimd(P, CHUNK0_AT + 2))
+        g1_quarters.append(gate_on_gpsimd(HALF + P, CHUNK0_AT + 2))
         scatter_on_scalar(*[stage_on_scalar(kt, 0, 0, HALF) for kt in range(2)])
 
-        quantize_da(0, 1, relu_half(0, 1, RING_AT))
-        bank0 = result_bank(0, 0, HALF, C)
-        scatter_on_scalar(stage(on_scalar, bank0, HALF, C - P))
-        blocks = [cast_block(RING_AT + 2 * b, 0, 1, b, interleave_on_vector) for b in range(HB)]
+        quantize_da(0, 1, relu_half(0, 1, CHUNK1_AT))
+        scatter_on_scalar(stage_on_scalar(0, 0, HALF, C))
+        blocks = [cast_block(CHUNK1_AT + 2 * b, 0, 1, b, interleave_on_vector) for b in range(HB)]
         for b in range(HB):
             quantize_block(0, 1, b, blocks[b])
-        result1 = stage_on_vector(RING_AT, 1, 0, HALF, C)
-        result0 = stage(on_vector, bank0, C - P, C, RING_AT + 1.5)
-        chunk = gpsimd_chunk(0, 2, RING_AT + 2, KC - LAST_ON_VECTOR)
+        result1 = stage_on_vector(CHUNK1_AT, 1, 0, HALF, C)
+        quantize(gq[1, 0], E5, g10[:])
+        chunk = gpsimd_chunk(0, 2, G10_AT - 2, KC - LAST_ON_VECTOR)
         scatter_on_vector(result1)
-        scatter_on_vector(result0)
-        held = at(RING_AT + EDGE - 3, [4 * (HALF + LAST_ON_VECTOR)], BF16, "ggroup11_and_rest")
-        g11, rest = held[:, 0:4 * HALF], held[:, 4 * HALF:]
-        dst_view, src_view = four_neighbours(words(g11), planes(g_planes[1][:])[:, :, HALF:C])
-        gate_view = gates[1][:, HALF:C].rearrange("p (c i) -> p c i", i=4).unsqueeze(2).to_broadcast([P, HALF // 4, 4, 4])
-        nc.vector.tensor_tensor(dst_view, src_view, gate_view, MULT)
+        bank2, bank3 = [result_bank(kt, 0, 0, C) for kt in (2, 3)]
+        result2 = stage(on_scalar, bank2, 0, C)
+        scatter_on_vector(stage(on_vector, bank3, 0, SHARE3, CHUNK1_AT + 1))
+        result3 = stage(on_scalar, bank3, SHARE3, C)
+        rest = at(CHUNK1_AT + EDGE, [4 * LAST_ON_VECTOR], BF16, "w1group_rest")[:]
         interleave_on_vector(words(rest), w1raw[0, 2, 1][:, :, KC - LAST_ON_VECTOR:KC])
         quantize_block(0, 2, 0, chunk[:, 0:4 * KC])
         quantize_block(0, 2, 1, chunk[:, 4 * KC:4 * (2 * KC - LAST_ON_VECTOR)])
         quantize(w1q[0][2], E4, rest, 2 * KC - LAST_ON_VECTOR)
-        scatter_on_scalar(*[stage_on_scalar(kt, 0) for kt in (2, 3)])
+        scatter_part(result2, 0, HALF)
+        scatter_part(result3, SHARE3, C)
+        scatter_part(result2, HALF, C)
 
         for q in range(2):
-            quantize(gq[1, 0], E5, g1_quarters[q], q * P)
-        quantize(gq[1, 1], E5, g11)
+            quantize(gq[1, 1], E5, g1_quarters[q], q * P)
         w2groups = [group_w2(on_vector, w2raw[1][b], group_at(kb, "w2group1%d" % b))
-                    for b, kb in enumerate((RING_AT + EDGE - 4, RING_AT + 2))]
+                    for b, kb in enumerate((28, 32))]
         w2q.append([quantize(mx_pair("w2q10"), E4, w2groups[0][:])])
         block1 = cast_block(W2RAW_AT[1], 1, 0, 1, interleave_on_vector)
         w2q[1].append(quantize(mx_pair("w2q11"), E4, w2groups[1][:]))
@@ -332,7 +343,7 @@ def tile_moe_bdx_mlp_relu_kernel(tc, dyT, a, w2, w1, gate, offs, out):
         for kt in range(2):
             scatter_on_vector(halves[kt])
             store(kt)
-        scatter_on_scalar(result2, result3)
+        scatter_on_scalar(result3, result2)
         result2_last = stage_on_vector(w1raw_at(1, 2, 1), 2, 1, HALF, C)
         quantize(w1q[1][2], E4, chunk[:])
         result3_last = stage(on_vector, bank3, C - P, C, w1raw_at(1, 2, 1) + 1)

@@ -29,9 +29,8 @@ KC = 2 * P
 CHUNKS = K // KC
 HALF = C // 2
 
-W2_ON_SCALAR = (44, 72)
+W2_ON_SCALAR = (44, 64)
 LAST_ON_VECTOR = 128
-SHARE3 = 160
 
 KB = 1024
 EDGE = 0.25
@@ -93,10 +92,10 @@ def tile_moe_bdx_mlp_relu_kernel(tc, dyT, a, w2, w1, gate, offs, out):
         def interleave_on_gpsimd(dst, src):
             nc.gpsimd.tensor_scalar(out=dst, in0=src.rearrange("p t c -> p c t"), scalar1=1.0, scalar2=0.0, op0=MULT, op1=ADD)
 
-        def group_w2(copy, raw, dst, m0=0, m1=P):
+        def group_w2(copy, raw, dst, m0=0, m1=P, pairs=(0, 2)):
             dst_view = dst[:].rearrange("p (t m j) -> p m j t", t=4, j=4)
             raw_view = raw.rearrange("p j (m t) -> p m j t", t=4)
-            for t0 in (0, 2):
+            for t0 in pairs:
                 copy(dst_view[:, m0:m1, :, t0:t0 + 2], raw_view[:, m0:m1, :, t0:t0 + 2])
             return dst
 
@@ -135,8 +134,9 @@ def tile_moe_bdx_mlp_relu_kernel(tc, dyT, a, w2, w1, gate, offs, out):
         def slots_of(e, s0=0, s1=C):
             return offs_t[:, (e * C + s0) // 16:(e * C + s1) // 16]
 
-        def copy_gates(copy, e):
-            copy(gates[e][:].rearrange("p (n m) -> p n m", m=4), gate_banks[e][:].rearrange("p (m n) -> p n m", m=4))
+        def copy_gates(copy, e, s0=0):
+            copy(gates[e][:].rearrange("p (n m) -> p n m", m=4)[:, s0 // 4:, :],
+                 gate_banks[e][:].rearrange("p (m n) -> p n m", m=4)[:, s0 // 4:, :])
 
         def gate_on_gpsimd(s0, kb):
             dst = at(kb, [P, 4], BF16, "ggroup1_%d" % s0)
@@ -181,11 +181,13 @@ def tile_moe_bdx_mlp_relu_kernel(tc, dyT, a, w2, w1, gate, offs, out):
         def result_bank(kt, e, s0, s1):
             bank = psum.tile([P, C], F32, name="dx", bufs=4)
             w_codes, w_scales = w1q[e][kt // 2]
+            runs = [(s0, HALF), (HALF, s1)] if s1 - s0 == 3 * P else [(s0, s1)]
             for b in range(HB):
                 c0 = b * KC + kt % 2 * P
-                nc.tensor.matmul_mx(out=bank[:, 0:s1 - s0], lhsT=w_codes[:, c0:c0 + P].bitcast(E4), lhsT_scale=w_scales[:, c0:c0 + P],
-                                    rhs=daq[e][b][0][:, s0:s1].bitcast(E5), rhs_scale=daq[e][b][1][:, s0:s1],
-                                    start=(b == 0), stop=(b == HB - 1))
+                for r0, r1 in runs:
+                    nc.tensor.matmul_mx(out=bank[:, r0 - s0:r1 - s0], lhsT=w_codes[:, c0:c0 + P].bitcast(E4),
+                                        lhsT_scale=w_scales[:, c0:c0 + P], rhs=daq[e][b][0][:, r0:r1].bitcast(E5),
+                                        rhs_scale=daq[e][b][1][:, r0:r1], start=(b == 0 and r0 == s0), stop=(b == HB - 1 and r1 == s1))
             return kt, e, s0, bank
 
         def stage(copy, result, s0, s1, kb=None):
@@ -269,15 +271,17 @@ def tile_moe_bdx_mlp_relu_kernel(tc, dyT, a, w2, w1, gate, offs, out):
         w2groups = [group_at(W2GROUP_AT[b], "w2group0%d" % b) for b in range(HB)]
         for b in range(HB):
             group_w2(on_scalar, w2raw[0][b], w2groups[b], 0, W2_ON_SCALAR[b])
-            group_w2(on_vector, w2raw[0][b], w2groups[b], W2_ON_SCALAR[b], P)
-        copy_gates(on_scalar, 1)
+        group_w2(on_vector, w2raw[0][0], w2groups[0], W2_ON_SCALAR[0], P)
+        group_w2(on_vector, w2raw[0][1], w2groups[1], W2_ON_SCALAR[1], P, (0,))
         w2q = [[quantize(mx_pair("w2q00"), E4, w2groups[0][:])]]
+        group_w2(on_vector, w2raw[0][1], w2groups[1], W2_ON_SCALAR[1], P, (2,))
+        copy_gates(on_scalar, 1, HALF)
         quantize(gq[0, 1], E5, g0_groups[1][:])
         w2q[0].append(quantize(mx_pair("w2q01"), E4, w2groups[1][:]))
         g1_quarters = [gate_on_gpsimd(HALF, W2GROUP_AT[1])]
         windows = [at(4 * kt, [T], F32, "window%d" % kt) for kt in range(KT)]
         daq = [[mx_pair("daq%d%d" % (e, b)) for b in range(HB)] for e in range(E)]
-        w1q = [[mx_pair("w1q%d%d" % (e, c), C, CHUNK1_AT + 1 + EDGE if (e, c) == (0, 2) else None) for c in range(CHUNKS)] for e in range(E)]
+        w1q = [[mx_pair("w1q%d%d" % (e, c), C, {(0, 2): CHUNK1_AT + 1 + EDGE, (1, 1): RING_AT + 5}.get((e, c))) for c in range(CHUNKS)] for e in range(E)]
 
         a_words = {key: raw[:].rearrange("p t c -> p c t") for key, raw in a_raw.items()}
         signs = at(W2RAW_AT[0] + 2, [HALF, 4], BF16, "signs")
@@ -302,17 +306,16 @@ def tile_moe_bdx_mlp_relu_kernel(tc, dyT, a, w2, w1, gate, offs, out):
         quantize(gq[1, 0], E5, g10[:])
         chunk = gpsimd_chunk(0, 2, G10_AT - 2, KC - LAST_ON_VECTOR)
         scatter_on_vector(result1)
-        bank2, bank3 = [result_bank(kt, 0, 0, C) for kt in (2, 3)]
-        result2 = stage(on_scalar, bank2, 0, C)
-        scatter_on_vector(stage(on_vector, bank3, 0, SHARE3, CHUNK1_AT + 1))
-        result3 = stage(on_scalar, bank3, SHARE3, C)
+        scatter_on_vector(stage_on_vector(CHUNK1_AT + 1, 3, 0, 0, P))
+        result2 = stage_on_scalar(2, 0)
+        result3 = stage_on_scalar(3, 0, P, C)
         rest = at(CHUNK1_AT + EDGE, [4 * LAST_ON_VECTOR], BF16, "w1group_rest")[:]
         interleave_on_vector(words(rest), w1raw[0, 2, 1][:, :, KC - LAST_ON_VECTOR:KC])
         quantize_block(0, 2, 0, chunk[:, 0:4 * KC])
         quantize_block(0, 2, 1, chunk[:, 4 * KC:4 * (2 * KC - LAST_ON_VECTOR)])
         quantize(w1q[0][2], E4, rest, 2 * KC - LAST_ON_VECTOR)
         scatter_part(result2, 0, HALF)
-        scatter_part(result3, SHARE3, C)
+        scatter_part(result3, P, C)
         scatter_part(result2, HALF, C)
 
         for q in range(2):
@@ -335,8 +338,8 @@ def tile_moe_bdx_mlp_relu_kernel(tc, dyT, a, w2, w1, gate, offs, out):
         block1 = cast_block(RING_AT + 2, 1, 1, 1, interleave_on_vector)
         quantize_block(1, 1, 0, block0)
         quantize_block(1, 1, 1, block1)
-        halves = [stage_on_vector(RING_AT + 4 + kt, kt, 1, HALF, C) for kt in range(2)]
-        chunk = gpsimd_chunk(1, 2, RING_AT)
+        halves = [stage_on_vector(RING_AT + 2 + EDGE + kt, kt, 1, HALF, C) for kt in range(2)]
+        chunk = gpsimd_chunk(1, 2, RING_AT + EDGE - 2)
         result2, result3 = [stage_on_scalar(kt, 1, 0, HALF) for kt in (2, 3)]
         bank3 = result_bank(3, 1, HALF, C)
         result3_third = stage(on_scalar, bank3, HALF, C - P)
@@ -344,8 +347,9 @@ def tile_moe_bdx_mlp_relu_kernel(tc, dyT, a, w2, w1, gate, offs, out):
             scatter_on_vector(halves[kt])
             store(kt)
         scatter_on_scalar(result3, result2)
+        quantize(w1q[1][2], E4, chunk[:, 0:4 * KC])
         result2_last = stage_on_vector(w1raw_at(1, 2, 1), 2, 1, HALF, C)
-        quantize(w1q[1][2], E4, chunk[:])
+        quantize(w1q[1][2], E4, chunk[:, 4 * KC:], KC)
         result3_last = stage(on_vector, bank3, C - P, C, w1raw_at(1, 2, 1) + 1)
         scatter_on_vector(result2_last)
         store(2)

@@ -44,6 +44,8 @@ W1RAW_AT = 60
 W2RAW_AT = (108, 124)
 G10_AT = GATE0_AT + EDGE - 2
 CHUNK1_AT = 140
+LAST_DA_AT = 144
+SHIFT = 32
 
 
 def tile_moe_bdx_mlp_relu_kernel(tc, dyT, a, w2, w1, gate, offs, out):
@@ -178,8 +180,9 @@ def tile_moe_bdx_mlp_relu_kernel(tc, dyT, a, w2, w1, gate, offs, out):
         def quantize_block(e, c, b, grouped):
             quantize(w1q[e][c], E4, grouped[:], b * KC)
 
-        def result_bank(kt, e, s0, s1):
-            bank = psum.tile([P, C], F32, name="dx", bufs=4)
+        def result_bank(kt, e, s0, s1, bank=None):
+            if bank is None:
+                bank = psum.tile([P, C], F32, name="dx", bufs=4)
             w_codes, w_scales = w1q[e][kt // 2]
             runs = [(s0, HALF), (HALF, s1)] if s1 - s0 == 3 * P else [(s0, s1)]
             for b in range(HB):
@@ -280,7 +283,7 @@ def tile_moe_bdx_mlp_relu_kernel(tc, dyT, a, w2, w1, gate, offs, out):
         w2q[0].append(quantize(mx_pair("w2q01"), E4, w2groups[1][:]))
         g1_quarters = [gate_on_gpsimd(HALF, W2GROUP_AT[1])]
         windows = [at(4 * kt, [T], F32, "window%d" % kt) for kt in range(KT)]
-        daq = [[mx_pair("daq%d%d" % (e, b)) for b in range(HB)] for e in range(E)]
+        daq = [[mx_pair("daq%d%d" % (e, b), C, LAST_DA_AT if (e, b) == (1, 1) else None) for b in range(HB)] for e in range(E)]
         w1q = [[mx_pair("w1q%d%d" % (e, c), C, {(0, 2): CHUNK1_AT + 1 + EDGE, (1, 1): RING_AT + 5}.get((e, c))) for c in range(CHUNKS)] for e in range(E)]
 
         a_words = {key: raw[:].rearrange("p t c -> p c t") for key, raw in a_raw.items()}
@@ -338,26 +341,33 @@ def tile_moe_bdx_mlp_relu_kernel(tc, dyT, a, w2, w1, gate, offs, out):
         block1 = cast_block(RING_AT + 2, 1, 1, 1, interleave_on_vector)
         quantize_block(1, 1, 0, block0)
         quantize_block(1, 1, 1, block1)
-        halves = [stage_on_vector(RING_AT + 2 + EDGE + kt, kt, 1, HALF, C) for kt in range(2)]
+        halves = [stage_on_vector(W2RAW_AT[1] + kt, kt, 1, HALF, C) for kt in range(2)]
         chunk = gpsimd_chunk(1, 2, RING_AT + EDGE - 2)
-        result2, result3 = [stage_on_scalar(kt, 1, 0, HALF) for kt in (2, 3)]
+        bank2 = result_bank(2, 1, 0, HALF)
+        result2 = stage(on_scalar, bank2, 0, HALF - SHIFT)
+        result3 = stage_on_scalar(3, 1, 0, HALF)
         bank3 = result_bank(3, 1, HALF, C)
         result3_third = stage(on_scalar, bank3, HALF, C - P)
         for kt in range(2):
             scatter_on_vector(halves[kt])
             store(kt)
-        scatter_on_scalar(result3, result2)
+        scatter_on_scalar(result2)
+        scatter_on_scalar(result3)
         quantize(w1q[1][2], E4, chunk[:, 0:4 * KC])
-        result2_last = stage_on_vector(w1raw_at(1, 2, 1), 2, 1, HALF, C)
+        staged = at(w1raw_at(1, 2, 1), [HALF + SHIFT], F32, "staged12_last")
+        on_vector(staged[:, 0:SHIFT], bank2[3][:, HALF - SHIFT:HALF])
+        on_vector(staged[:, SHIFT:], result_bank(2, 1, HALF, C)[3][:, 0:HALF])
+        result2_last = (2, 1, HALF - SHIFT, C, staged)
         quantize(w1q[1][2], E4, chunk[:, 4 * KC:], KC)
-        result3_last = stage(on_vector, bank3, C - P, C, w1raw_at(1, 2, 1) + 1)
         scatter_on_vector(result2_last)
         store(2)
         scatter_on_scalar(result3_third)
+        halves = [stage_on_scalar(5, 1, h * HALF, (h + 1) * HALF) for h in range(2)]
+        bank4 = result_bank(4, 1, 0, C, psum.tile([P, 4, P], F32, name="dh", bufs=4)[:].rearrange("p t c -> p (t c)"))
+        result3_last = stage(on_vector, bank3, C - P, C, LAST_DA_AT)
+        result4 = stage(on_vector, bank4, 0, C, w1raw_at(1, 1, 1))
         scatter_on_vector(result3_last)
         store(3)
-        halves = [stage_on_scalar(5, 1, h * HALF, (h + 1) * HALF) for h in range(2)]
-        result4 = stage_on_vector(w1raw_at(1, 1, 1), 4, 1)
         for half in halves:
             scatter_on_scalar(half)
         store(5, nc.scalar)

from contextlib import ExitStack

import concourse.mybir as mybir
from concourse.masks import make_identity

E, C, T = 2, 512, 1024
K, H, N = 768, 1024, 512
FLOPS = 2 * E * C * (N * H + H * K)
BYTES = 4 * (N * T + H * E * C + E * N * H + E * H * K + E * C + K * T) + 2 * 128 * (E * C // 16)

F32 = mybir.dt.float32
BF16 = mybir.dt.bfloat16
U32 = mybir.dt.uint32
U16 = mybir.dt.uint16
U8 = mybir.dt.uint8
E4 = mybir.dt.float8_e4m3fn_x4
E5 = mybir.dt.float8_e5m2_x4
MULT = mybir.AluOpType.mult
ADD = mybir.AluOpType.add
IS_GT = mybir.AluOpType.is_gt
SIGN = mybir.ActivationFunctionType.Sign
COPY = mybir.ActivationFunctionType.Copy

P = 128
PASS = 512
HB = H // PASS
KT = K // P
KC = 2 * P
CHUNKS = K // KC
HALF = C // 2

W2_ON_SCALAR = (44, 64)
LAST_ON_VECTOR = 128

KB = 1024
EDGE = 0.25
PLANES_AT = (16, 24)
GATE0_AT = 34
W2GROUP_AT = (GATE0_AT + 2 - EDGE, 40)
CHUNK0_AT = 44
G0GROUP_AT = 48
RING_AT = 52
W1RAW_AT = 60
W2RAW_AT = (108, 124)
G10_AT = GATE0_AT + EDGE - 2
CHUNK1_AT = 140
LAST_DA_AT = 144
SHIFT = 32


def tile_moe_bdx_mlp_relu_kernel(tc, dyT, a, w2, w1, gate, offs, out):
    nc = tc.nc
    with ExitStack() as ctx:
        keep = ctx.enter_context(tc.tile_pool(name="keep", bufs=1))
        placed = ctx.enter_context(tc.tile_pool(name="placed", bufs=1))
        psum = ctx.enter_context(tc.psum_pool(name="psum", bufs=1))

        def at(kb, shape, dtype, name):
            return placed.tile([P] + shape, dtype, name=name, offset=int(kb * KB), align_bytes=256)

        def group_at(kb, name):
            return at(kb, [4 * C], BF16, name)

        def w1raw_at(e, c, b):
            return W1RAW_AT + 4 * (HB * (CHUNKS * e + c) + b)

        def by_planes(rows):
            return rows.rearrange("(p t) c -> p t c", t=4)

        def planes(ap):
            return ap.rearrange("p (t c) -> p t c", t=4)

        def words(ap):
            return ap.rearrange("p (c t) -> p c t", t=4)

        def four_neighbours(dst, src):
            return dst.rearrange("p (c i) t -> p c t i", i=4), src.rearrange("p t (c i) -> p c t i", i=4)

        def on_scalar(dst, src):
            nc.scalar.copy(out=dst, in_=src)

        def on_vector(dst, src):
            nc.vector.tensor_copy(out=dst, in_=src)

        def interleave(copy, dst, src):
            copy(*four_neighbours(dst, src))

        def interleave_on_scalar(dst, src):
            interleave(on_scalar, dst, src)

        def interleave_on_vector(dst, src):
            interleave(on_vector, dst, src)

        def interleave_on_gpsimd(dst, src):
            nc.gpsimd.tensor_scalar(out=dst, in0=src.rearrange("p t c -> p c t"), scalar1=1.0, scalar2=0.0, op0=MULT, op1=ADD)

        def group_w2(copy, raw, dst, m0=0, m1=P, pairs=(0, 2)):
            dst_view = dst[:].rearrange("p (t m j) -> p m j t", t=4, j=4)
            raw_view = raw.rearrange("p j (m t) -> p m j t", t=4)
            for t0 in pairs:
                copy(dst_view[:, m0:m1, :, t0:t0 + 2], raw_view[:, m0:m1, :, t0:t0 + 2])
            return dst

        def mx_pair(name, width=C, scales_kb=None):
            codes = keep.tile([P, width], U32, name=name + "_codes", align_bytes=64)
            if scales_kb is None:
                return codes, keep.tile([P, width], U8, name=name + "_scales", align_bytes=64)
            return codes, at(scales_kb, [width], U8, name + "_scales")

        def quantize(pair, fmt, grouped, c0=0):
            cols = slice(c0, c0 + grouped.shape[1] // 4)
            nc.vector.quantize_mx(out=pair[0][:, cols].bitcast(fmt), scales=pair[1][:, cols], in_=grouped)
            return pair

        def load(name, view, kb=None):
            shape = list(view.shape[1:])
            raw = keep.tile([P] + shape, F32, name=name, align_bytes=256) if kb is None else at(kb, shape, F32, name)
            nc.sync.dma_start(out=raw[:], in_=view)
            return raw

        def load_dy(t):
            return load("dy%d" % t, by_planes(dyT)[:, t, :], 4 * t)

        def load_w2(e):
            whole = load("w2raw%d" % e, by_planes(w2[e]), W2RAW_AT[e])
            w2raw[e] = [whole[:, :, b * PASS:(b + 1) * PASS] for b in range(HB)]

        def load_a(e, h, b):
            s0 = e * C + h * HALF
            a_raw[e, h, b] = load("a%d%d_%d" % (e, b, h * HALF), by_planes(a[b * PASS:(b + 1) * PASS, s0:s0 + HALF]))

        def load_w1(e, c, b):
            view = by_planes(w1[e, b * PASS:(b + 1) * PASS, c * KC:(c + 1) * KC])
            w1raw[e, c, b] = load("w1raw%d%d_%d" % (e, b, c * KC), view, w1raw_at(e, c, b))

        def slots_of(e, s0=0, s1=C):
            return offs_t[:, (e * C + s0) // 16:(e * C + s1) // 16]

        def copy_gates(copy, e, s0=0):
            copy(gates[e][:].rearrange("p (n m) -> p n m", m=4)[:, s0 // 4:, :],
                 gate_banks[e][:].rearrange("p (m n) -> p n m", m=4)[:, s0 // 4:, :])

        def gate_on_gpsimd(s0, kb):
            dst = at(kb, [P, 4], BF16, "ggroup1_%d" % s0)
            nc.gpsimd.tensor_tensor(dst[:], planes(g_planes[1][:])[:, :, s0:s0 + P].rearrange("p t c -> p c t"),
                                    gates[1][:, s0:s0 + P].unsqueeze(2).to_broadcast([P, P, 4]), MULT)
            return dst[:].rearrange("p c t -> p (c t)")

        def relu_half(e, h, kb):
            groups = []
            for b in range(HB):
                groups.append(at(kb + 2 * b, [4 * HALF], BF16, "dagroup%d%d%d" % (e, h, b)))
                w_codes, w_scales = w2q[e][b]
                g_codes, g_scales = gq[e, h]
                for s0 in range(0, HALF, P):
                    bank = psum.tile([P, 4, P], F32, name="dh", bufs=4)
                    for t in range(4):
                        nc.tensor.matmul_mx(out=bank[:, t, :], lhsT=w_codes[:, t * P:(t + 1) * P].bitcast(E4),
                                            lhsT_scale=w_scales[:, t * P:(t + 1) * P], rhs=g_codes[:, s0:s0 + P].bitcast(E5),
                                            rhs_scale=g_scales[:, s0:s0 + P], start=True, stop=True)
                    nc.vector.scalar_tensor_tensor(out=words(groups[b][:])[:, s0:s0 + P, :], in0=a_words[e, h, b][:, s0:s0 + P, :],
                                                   scalar=0.0, in1=bank[:].rearrange("p t c -> p c t"), op0=IS_GT, op1=MULT)
            return groups

        def quantize_da(e, h, groups):
            for b in range(HB):
                quantize(daq[e][b], E5, groups[b][:], h * HALF)

        def cast_block(kb, e, c, b, cast):
            dst = at(kb, [4 * KC], BF16, "w1group%d%d%d" % (e, c, b))
            cast(words(dst[:]), w1raw[e, c, b][:])
            return dst

        def gpsimd_chunk(e, c, kb, width=KC):
            dst = group_at(kb, "w1group%d%d" % (e, c))
            interleave_on_gpsimd(words(dst[:])[:, 0:KC, :], w1raw[e, c, 0][:])
            interleave_on_gpsimd(words(dst[:])[:, KC:KC + width, :], w1raw[e, c, 1][:, :, 0:width])
            return dst

        def quantize_block(e, c, b, grouped):
            quantize(w1q[e][c], E4, grouped[:], b * KC)

        def result_bank(kt, e, s0, s1, bank=None):
            if bank is None:
                bank = psum.tile([P, C], F32, name="dx", bufs=4)
            w_codes, w_scales = w1q[e][kt // 2]
            runs = [(s0, HALF), (HALF, s1)] if s1 - s0 == 3 * P else [(s0, s1)]
            for b in range(HB):
                c0 = b * KC + kt % 2 * P
                for r0, r1 in runs:
                    nc.tensor.matmul_mx(out=bank[:, r0 - s0:r1 - s0], lhsT=w_codes[:, c0:c0 + P].bitcast(E4),
                                        lhsT_scale=w_scales[:, c0:c0 + P], rhs=daq[e][b][0][:, r0:r1].bitcast(E5),
                                        rhs_scale=daq[e][b][1][:, r0:r1], start=(b == 0 and r0 == s0), stop=(b == HB - 1 and r1 == s1))
            return kt, e, s0, bank

        def stage(copy, result, s0, s1, kb=None):
            kt, e, first, bank = result
            if kb is None:
                staged = keep.tile([P, C], F32, name="staged", bufs=4)
            else:
                staged = at(kb, [s1 - s0], F32, "staged%d%d_%d" % (e, kt, s0))
            copy(staged[:, 0:s1 - s0], bank[:, s0 - first:s1 - first])
            return kt, e, s0, s1, staged

        def stage_on_scalar(kt, e, s0=0, s1=C):
            return stage(on_scalar, result_bank(kt, e, s0, s1), s0, s1)

        def stage_on_vector(kb, kt, e, s0=0, s1=C):
            return stage(on_vector, result_bank(kt, e, s0, s1), s0, s1, kb)

        def scatter_on_scalar(*results):
            first, last = results[0][2:4]
            for s0 in range(first, last, HALF):
                s1 = min(s0 + HALF, last)
                for kt, e, _, _, staged in results:
                    nc.scalar.activation(out=windows[kt][:].indirect(slots_of(e, s0, s1)), in_=staged[:, s0 - first:s1 - first], func=COPY)

        def scatter_part(result, s0, s1):
            kt, e, first, last, staged = result
            nc.scalar.activation(out=windows[kt][:].indirect(slots_of(e, s0, s1)), in_=staged[:, s0 - first:s1 - first], func=COPY)

        def scatter_on_vector(result):
            kt, e, s0, s1, staged = result
            nc.vector.tensor_copy(out=windows[kt][:].indirect(slots_of(e, s0, s1)), in_=staged[:, 0:s1 - s0])

        def store(kt, queue=nc.sync):
            queue.dma_start(out=out[kt * P:(kt + 1) * P, :], in_=windows[kt][:])

        ident = keep.tile([P, P], F32, name="ident")
        make_identity(nc, ident[:])
        gate_row = load("gate_row", gate[0, :].rearrange("(e n m) -> n e m", e=E, m=4))
        dy = [load_dy(0)]
        offs_t = keep.tile([P, E * C // 16], U16, name="offs_t")
        nc.sync.dma_start(offs_t[:], offs)
        dy += [load_dy(t) for t in range(1, 4)]
        gate_banks = []
        for e in range(E):
            gate_banks.append(psum.tile([P, C], F32, name="dx", bufs=4))
            for m in range(4):
                nc.tensor.transpose(gate_banks[e][:, m * P:(m + 1) * P], gate_row[:, e, m:m + 1].to_broadcast([P, P]), ident[:])
        w2raw, a_raw, w1raw = {}, {}, {}
        load_w2(0)
        for load_part, i in ((load_a, 0), (load_w1, 0), (load_a, 1), (load_w1, 1), (load_w1, 2)):
            for b in range(HB):
                load_part(0, i, b)
        load_w2(1)
        for b in (1, 0):
            load_w1(1, 0, b)
        for b in range(HB):
            load_a(1, 0, b)
        for b in range(HB):
            load_a(1, 1, b)
            load_w1(1, 1, b)
        for b in range(HB):
            load_w1(1, 2, b)

        g_planes = [at(PLANES_AT[e], [4 * C], F32, "g%d" % e) for e in range(E)]
        gates = [at(GATE0_AT, [C], F32, "gate0"), at(W2RAW_AT[0] + 4, [C], F32, "gate1")]
        copy_gates(on_vector, 0)
        for t in range(4):
            nc.vector.tensor_tensor(g_planes[0][:, t * C:(t + 1) * C], dy[t][:].indirect(slots_of(0)), gates[0][:], MULT)
            for s0, s1 in ((0, C),) if t < 3 else ((0, HALF), (HALF, C)):
                nc.scalar.activation(out=g_planes[1][:, t * C + s0:t * C + s1], in_=dy[t][:].indirect(slots_of(1, s0, s1)), func=COPY)
        held_scales = {(0, 1): W2GROUP_AT[0] + EDGE, (1, 0): CHUNK1_AT + 4 - EDGE, (1, 1): w1raw_at(0, CHUNKS - 1, 1) + 1}
        gq = {(e, h): mx_pair("gq%d%d" % (e, h), HALF, held_scales.get((e, h))) for e in range(E) for h in range(2)}
        g0_groups = [at(G0GROUP_AT + 2 * h, [4 * HALF], BF16, "ggroup0%d" % h) for h in range(2)]
        for h, copy in enumerate((on_vector, on_scalar)):
            interleave(copy, words(g0_groups[h][:]), planes(g_planes[0][:])[:, :, h * HALF:(h + 1) * HALF])
        g10 = at(G10_AT, [4 * HALF], BF16, "ggroup10")
        dst_view, src_view = four_neighbours(words(g10[:]), planes(g_planes[1][:])[:, :, 0:HALF])
        gate_view = gate_banks[1][:].rearrange("p (i c) -> p c i", i=4)[:, 0:HALF // 4, :].unsqueeze(2).to_broadcast([P, HALF // 4, 4, 4])
        nc.vector.tensor_tensor(dst_view, src_view, gate_view, MULT)
        quantize(gq[0, 0], E5, g0_groups[0][:])
        w2groups = [group_at(W2GROUP_AT[b], "w2group0%d" % b) for b in range(HB)]
        for b in range(HB):
            group_w2(on_scalar, w2raw[0][b], w2groups[b], 0, W2_ON_SCALAR[b])
        group_w2(on_vector, w2raw[0][0], w2groups[0], W2_ON_SCALAR[0], P)
        group_w2(on_vector, w2raw[0][1], w2groups[1], W2_ON_SCALAR[1], P, (0,))
        w2q = [[quantize(mx_pair("w2q00"), E4, w2groups[0][:])]]
        group_w2(on_vector, w2raw[0][1], w2groups[1], W2_ON_SCALAR[1], P, (2,))
        copy_gates(on_scalar, 1, HALF)
        quantize(gq[0, 1], E5, g0_groups[1][:])
        w2q[0].append(quantize(mx_pair("w2q01"), E4, w2groups[1][:]))
        g1_quarters = [gate_on_gpsimd(HALF, W2GROUP_AT[1])]
        windows = [at(4 * kt, [T], F32, "window%d" % kt) for kt in range(KT)]
        daq = [[mx_pair("daq%d%d" % (e, b), C, LAST_DA_AT if (e, b) == (1, 1) else None) for b in range(HB)] for e in range(E)]
        w1q = [[mx_pair("w1q%d%d" % (e, c), C, {(0, 2): CHUNK1_AT + 1 + EDGE, (1, 1): RING_AT + 5}.get((e, c))) for c in range(CHUNKS)] for e in range(E)]

        a_words = {key: raw[:].rearrange("p t c -> p c t") for key, raw in a_raw.items()}
        signs = at(W2RAW_AT[0] + 2, [HALF, 4], BF16, "signs")
        dst_view, src_view = four_neighbours(signs[:], a_raw[0, 0, 1][:])
        nc.scalar.activation(out=dst_view, in_=src_view, func=SIGN)
        a_words[0, 0, 1] = signs[:]
        quantize_da(0, 0, relu_half(0, 0, CHUNK1_AT))
        quantize_block(0, 0, 0, cast_block(CHUNK0_AT, 0, 0, 0, interleave_on_scalar))
        by_tiles = at(CHUNK0_AT + 2, [4 * KC], BF16, "w1group001")
        for u in range(2):
            interleave_on_scalar(words(by_tiles[:])[:, u * P:(u + 1) * P, :], w1raw[0, 0, 1][:, :, u * P:(u + 1) * P])
            quantize(w1q[0][0], E4, by_tiles[:, 4 * u * P:4 * (u + 1) * P], KC + u * P)
        g1_quarters.append(gate_on_gpsimd(HALF + P, CHUNK0_AT + 2))
        scatter_on_scalar(*[stage_on_scalar(kt, 0, 0, HALF) for kt in range(2)])

        quantize_da(0, 1, relu_half(0, 1, CHUNK1_AT))
        scatter_on_scalar(stage_on_scalar(0, 0, HALF, C))
        blocks = [cast_block(CHUNK1_AT + 2 * b, 0, 1, b, interleave_on_vector) for b in range(HB)]
        for b in range(HB):
            quantize_block(0, 1, b, blocks[b])
        result1 = stage_on_vector(CHUNK1_AT, 1, 0, HALF, C)
        quantize(gq[1, 0], E5, g10[:])
        chunk = gpsimd_chunk(0, 2, G10_AT - 2, KC - LAST_ON_VECTOR)
        scatter_on_vector(result1)
        scatter_on_vector(stage_on_vector(CHUNK1_AT + 1, 3, 0, 0, P))
        result2 = stage_on_scalar(2, 0)
        result3 = stage_on_scalar(3, 0, P, C)
        rest = at(CHUNK1_AT + EDGE, [4 * LAST_ON_VECTOR], BF16, "w1group_rest")[:]
        interleave_on_vector(words(rest), w1raw[0, 2, 1][:, :, KC - LAST_ON_VECTOR:KC])
        quantize_block(0, 2, 0, chunk[:, 0:4 * KC])
        quantize_block(0, 2, 1, chunk[:, 4 * KC:4 * (2 * KC - LAST_ON_VECTOR)])
        quantize(w1q[0][2], E4, rest, 2 * KC - LAST_ON_VECTOR)
        scatter_part(result2, 0, HALF)
        scatter_part(result3, P, C)
        scatter_part(result2, HALF, C)

        for q in range(2):
            quantize(gq[1, 1], E5, g1_quarters[q], q * P)
        w2groups = [group_w2(on_vector, w2raw[1][b], group_at(kb, "w2group1%d" % b))
                    for b, kb in enumerate((28, 32))]
        w2q.append([quantize(mx_pair("w2q10"), E4, w2groups[0][:])])
        block1 = cast_block(W2RAW_AT[1], 1, 0, 1, interleave_on_vector)
        w2q[1].append(quantize(mx_pair("w2q11"), E4, w2groups[1][:]))
        quantize_block(1, 0, 1, block1)
        block0 = cast_block(W2RAW_AT[1], 1, 0, 0, interleave_on_gpsimd)
        scatter_on_scalar(*[stage_on_scalar(kt, 0) for kt in (4, 5)])
        groups = relu_half(1, 0, RING_AT + 2)
        quantize_block(1, 0, 0, block0)
        quantize_da(1, 0, groups)
        scatter_on_scalar(*[stage_on_scalar(kt, 1, 0, HALF) for kt in range(2)])

        block0 = cast_block(W2RAW_AT[1], 1, 1, 0, interleave_on_gpsimd)
        quantize_da(1, 1, relu_half(1, 1, RING_AT + 2))
        block1 = cast_block(RING_AT + 2, 1, 1, 1, interleave_on_vector)
        quantize_block(1, 1, 0, block0)
        quantize_block(1, 1, 1, block1)
        halves = [stage_on_vector(W2RAW_AT[1] + kt, kt, 1, HALF, C) for kt in range(2)]
        chunk = gpsimd_chunk(1, 2, RING_AT + EDGE - 2)
        bank2 = result_bank(2, 1, 0, HALF)
        result2 = stage(on_scalar, bank2, 0, HALF - SHIFT)
        result3 = stage_on_scalar(3, 1, 0, HALF)
        bank3 = result_bank(3, 1, HALF, C)
        result3_third = stage(on_scalar, bank3, HALF, C - P)
        for kt in range(2):
            scatter_on_vector(halves[kt])
            store(kt)
        scatter_on_scalar(result2)
        scatter_on_scalar(result3)
        quantize(w1q[1][2], E4, chunk[:, 0:4 * KC])
        staged = at(w1raw_at(1, 2, 1), [HALF + SHIFT], F32, "staged12_last")
        on_vector(staged[:, 0:SHIFT], bank2[3][:, HALF - SHIFT:HALF])
        on_vector(staged[:, SHIFT:], result_bank(2, 1, HALF, C)[3][:, 0:HALF])
        result2_last = (2, 1, HALF - SHIFT, C, staged)
        quantize(w1q[1][2], E4, chunk[:, 4 * KC:], KC)
        scatter_on_vector(result2_last)
        store(2)
        scatter_on_scalar(result3_third)
        halves = [stage_on_scalar(5, 1, h * HALF, (h + 1) * HALF) for h in range(2)]
        bank4 = result_bank(4, 1, 0, C, psum.tile([P, 4, P], F32, name="dh", bufs=4)[:].rearrange("p t c -> p (t c)"))
        result3_last = stage(on_vector, bank3, C - P, C, LAST_DA_AT)
        result4 = stage(on_vector, bank4, 0, C, w1raw_at(1, 1, 1))
        scatter_on_vector(result3_last)
        store(3)
        for half in halves:
            scatter_on_scalar(half)
        store(5, nc.scalar)
        scatter_on_vector(result4)
        store(4)
